import numpy as np, ml_dtypes
CORES = [3,7,11,15,131,135,139,143]
N = 8
BF = ml_dtypes.bfloat16
W, L, RO, SH = 2048, 256, 8, (3,)
KK = np.arange(16, dtype=np.int32).reshape(1, 1, 16, 1)
REC = np.array([0.3, 0.0, 1.0, 0.5, 1.0, 0.3, 1.0, 1.0]).reshape(1, 8, 1, 1)
def spans(rng, kind):
    p = np.argsort(rng.random((N, 8, 16, L)), axis=2).astype(np.float64); x = rng.random((N, 8, 16, L)); t = rng.random((N, 8, 16, L))
    s = np.exp2(-rng.integers(0, 6, (N, 8, 1, L)).astype(np.float64))
    c = np.where((kind == 1) | (kind == 3), p, x)
    dur = np.where(kind == 1, 0.5, np.where(kind == 2, 1.0 + t, np.where(kind == 3, 31.0 - 2.0 * p, t * s)))
    pos = np.argsort(np.argsort(np.concatenate([c, c + dur], axis=2), axis=2, kind="stable"), axis=2)
    return pos[:, :, :16], pos[:, :, 16:]
def kinds(rng):
    return rng.choice(np.array([0, 0, 0, 0, 1, 2, 3]), (N, 8, 1, L))
def parts(rng):
    xt = np.floor(rng.random((N, 8, 16, W)) * rng.choice(np.array([12, 24, 40, 64]), (N, 8, 1, W))).astype(np.int64)
    vt = rng.integers(0, 64, (N, 8, 16, W))
    z0 = np.floor(rng.random((N, 8, 16, L)) * rng.choice(np.array([16, 32, 64]), (N, 8, 1, L))).astype(np.int64)
    nm = rng.integers(0, 4096, (N, 8, 16, L)); wt = rng.integers(0, 4096, (N, 8, 16))
    th = rng.integers(150, 330, (N, 8, 1)) + rng.integers(-60, 61, (N, 8, 16))
    th[np.arange(N), rng.integers(0, 8, N)] = rng.integers(0, 30, (N, 16))
    return xt, vt, z0, nm, wt, th
def aim(c):
    return (c - 37 * KK) & 4095
def few(a):
    return np.ascontiguousarray(np.reshape(a, (N, 128, -1))).astype(np.float32).astype(BF)
def big(a):
    return np.ascontiguousarray(np.reshape(a, (N, 128, -1))).astype(np.int32)
def pack(xt, vt, z0, nm, ca, rt, wt, th):
    return {"xt": few(xt), "vt": few(vt), "z0": few(z0), "nm": big(nm), "ca": few(ca), "rt": few(rt), "wt": big(wt), "th": big(th)}
def setup_inputs(rng):
    xt, vt, z0, nm, wt, th = parts(rng); ca, rt = spans(rng, kinds(rng))
    return pack(xt, vt, z0, nm, ca, rt, wt, th)
def uneven(rng, bits, *shape):
    return np.minimum(np.floor(np.exp2(bits * rng.random(shape))), 2 ** bits).astype(np.int64) - 1
def sized(rng, n):
    a = np.minimum(np.floor(np.exp2(6.0 * rng.random((N, 8, 1, n))) * rng.random((N, 8, 16, n))), 63).astype(np.int64)
    return np.where(rng.random((N, 8, 1, n)) < 0.5, a, 63 - a)
def setup_inputs_spread(rng):
    ca, rt = spans(rng, kinds(rng))
    return pack(sized(rng, W), sized(rng, W), sized(rng, L), uneven(rng, 12, N, 8, 16, L), ca, rt, uneven(rng, 12, N, 8, 16), np.minimum(uneven(rng, 10, N, 8, 16), 1007))
def tips(rng, n):
    return np.where(rng.random((N, 8, 1, n)) < REC, 63 * rng.integers(0, 2, (N, 8, 1, n)), 63 * rng.integers(0, 2, (N, 8, 16, n)))
def setup_inputs_ends(rng):
    xt, vt, z0 = tips(rng, W), tips(rng, W), tips(rng, L)
    nm = 4095 * rng.integers(0, 2, (N, 8, 16, L)); wt = 4095 * rng.integers(0, 2, (N, 8, 16)); th = 1007 * rng.integers(0, 2, (N, 8, 16))
    th[:, :, 0] = 0; th[:, :, 15] = 1007
    us = np.arange(W); hit = np.flatnonzero((((us * us) >> 5) + 37 * us + 613) & (W - 1) == W - 1)
    one = 65 if len(hit) == 0 else (-65 * int(hit[rng.integers(0, len(hit))])) & 4095
    wt[:, 0] = 4095; wt[:, 6:] = 0; wt[:, 7, 15] = 65; wt[:, 6, 15] = one
    last = np.array([0, 1, 6, L - 2, L - 1])
    z0[:, 0][..., last] = 63; z0[:, 7][..., last] = 63; nm[:, 7][..., last] = 4095
    ca, rt = spans(rng, rng.choice(np.array([1, 2, 3]), (N, 8, 1, L)))
    return pack(xt, vt, z0, nm, ca, rt, wt, th)
def setup_inputs_corners(rng):
    xt, vt, z0, nm, wt, th = parts(rng); H = W // 2
    hi = rng.integers(0, 64, (N, 4, 16, H)) * (rng.random((N, 4, 1, H)) < 0.5); hi[:, :, :8] = 63; hi[:, :, 8] = 0
    lo = np.where(rng.random((N, 4, 1, H)) < 0.5, 63, rng.integers(0, 64, (N, 4, 16, H))); lo[:, :, :9] = 0
    xt[:, :4, :, :H] = hi; xt[:, :4, :, H:] = lo; z0[:, :4] = rng.integers(1, 63, (N, 4, 16, L)); wt[:, :4] = 0; th[:, :4] = 0
    kind = kinds(rng); kind[:, :4] = rng.choice(np.array([1, 2, 2, 3]), (N, 4, 1, L)); kind[:, 4] = 1; kind[:, 5] = 2; kind[:, 6] = 3
    ca, rt = spans(rng, kind)
    many = rng.choice(np.array([0, 1, RO // 2, RO - 2, RO - 1, 16]), (N, 8, 1, L)); many[:, 1] = rng.integers(0, 2, (N, 1, L)); many[:, 2] = RO // 2; many[:, 3] = 16
    many[:, 0, :, L - 1] = RO - 2
    order = np.argsort(np.argsort(ca, axis=2), axis=2)
    c = np.where(order < many, rng.integers(0, H - 32, (N, 8, 16, L)), rng.integers(H, W - 32, (N, 8, 16, L)))
    nm[:, :4] = aim(c)[:, :4]
    wt[:, 4] = 4095 * rng.integers(0, 2, (N, 16)); th[:, 4] = 0; th[:, 7] = np.where(rng.random((N, 16)) < 0.25, 1007, 0)
    return pack(xt, vt, z0, nm, ca, rt, wt, th)
def setup_inputs_crowd(rng):
    xt, vt, z0, nm, wt, th = parts(rng); Q = W // 4
    xt[..., :Q] = rng.integers(40, 64, (N, 8, 16, Q)); xt[..., Q:2 * Q] = rng.integers(24, 33, (N, 8, 16, Q)); xt[..., 2 * Q:] = 0
    z0 = rng.integers(1, 8, (N, 8, 16, L)); wt[:, 0::2] = 0; wt[:, 1::2] = W // 2
    xt[:, 1::2] = (xt[:, 1::2] >> 1) << 1; z0[:, 1::2] = np.maximum((z0[:, 1::2] >> 1) << 1, 2)
    vt[..., 613] = 0; th = rng.integers(0, 300, (N, 8, 16))
    ca, rt = spans(rng, kinds(rng)); first = ca == np.min(ca, axis=2, keepdims=True)
    low = rng.integers(2 * Q, W - 32, (N, 8, 16, L)); mid = rng.integers(Q, 2 * Q - 32, (N, 8, 16, L))
    c = np.where(first, rng.integers(0, Q - 32, (N, 8, 16, L)), np.where(rng.random((N, 8, 1, L)) < 0.5, mid, low))
    out = np.zeros((N, 8, 1, L), bool); out[1, 7, 0, L - 1] = True
    for q in range(2, N - 1):
        for g in range(1, 8, 2): out[q, g, 0, rng.integers(0, L)] = True
    nm = aim(np.where(out, low, c))
    e = N - 1; cols = np.arange(W)
    xt[e] = rng.integers(0, 64, (8, 16, W)); xt[e, :, 8:] = xt[e, :, 8:] >> 2; vt[e, :, 8:] = vt[e, :, 8:] >> 2
    z0[e, :, :8] = 0; z0[e, :, 8:] = rng.integers(50, 64, (8, 8, L)); th[e] = rng.integers(0, 100, (8, 16))
    wt[e, 0::2] = rng.integers(0, 4096, (4, 16)); nm[e, 0::2] = rng.integers(0, 4096, (4, 16, L))
    wt[e, 1::2] = 0; wt[e, 1::2, 0] = 1; wt[e, 1::2, 1] = 64
    xt[e, 1::2, 0] = cols & 63; xt[e, 1::2, 1] = cols >> 6; xt[e, 1::2, 2] = np.where(cols < 600, 0, rng.integers(1, 64, (4, W)))
    us = np.arange(600, W); us = us[np.unique(((us * us >> 5) + 37 * us) & (W - 1), return_index=True)[1]]
    for g in range(1, 8, 2): nm[e, g] = np.where(first[e, g], aim(np.resize(rng.permutation(us), L))[0, 0], 0)
    return pack(xt, vt, z0, nm, ca, rt, wt, th)
def setup_inputs_twins(rng):
    xt, vt, z0, nm, wt, th = parts(rng); B = W // 128
    b = np.floor(rng.random((1, 8, 16, B)) * rng.choice(np.array([12, 24, 40, 64]), (1, 8, 1, B))).astype(np.int64)
    xt = np.repeat(np.repeat(b, 128, axis=3), N, axis=0)
    a = rng.integers(0, 40, (1, 8, 16, L // 2)); z0 = np.repeat(np.concatenate([a, a], axis=3), N, axis=0)
    a = rng.integers(0, 4096, (1, 8, 16, L // 2)); nm = np.repeat(np.concatenate([a, a], axis=3), N, axis=0)
    wt = np.repeat(wt[:1], N, axis=0); th = rng.integers(0, 4, (N, 8, 16)); ca, rt = spans(rng, kinds(rng))
    return pack(xt, vt, z0, nm, ca, rt, wt, th)
def check_inputs(d):
    bad = []
    for k, lo, hi in (("xt", 0, 63), ("vt", 0, 63), ("z0", 0, 63), ("nm", 0, 4095), ("ca", 0, 30), ("rt", 1, 31), ("wt", 0, 4095), ("th", 0, 1007)):
        a = np.asarray(d[k]).astype(np.float64)
        if not np.all((a >= lo) & (a <= hi)): bad.append("range of " + k)
        elif not np.all(a == np.floor(a)): bad.append("whole numbers in " + k)
    c = np.asarray(d["ca"]).astype(np.float64).reshape(N, 8, 16, L); r = np.asarray(d["rt"]).astype(np.float64).reshape(N, 8, 16, L)
    if not np.all(c < r): bad.append("ca under rt")
    e = np.sort(np.concatenate([c, r], axis=2), axis=2)
    if not np.all(e[:, :, 1:] > e[:, :, :-1]): bad.append("positions of a lane distinct")
    return bad
def ints(a):
    return np.asarray(a).astype(np.float32).astype(np.int32)
def pick(t, ix):
    return np.stack([np.stack([np.take(t[q, g], ix[q, g], axis=1) for g in range(8)]) for q in range(N)])
def mark(x, w):
    return np.sum(x * w, axis=2, dtype=np.int32) & (W - 1)
def place(u, d):
    return ((u * u >> 5) + 37 * u + 613 * d) & (W - 1)
def reference(xt, vt, z0, nm, ca, rt, wt, th):
    X = ints(xt).reshape(N, 8, 16, W); V = ints(vt).reshape(N, 8, 16, W); z = ints(z0).reshape(N, 8, 16, L)
    n = nm.astype(np.int32).reshape(N, 8, 16, L); c = ints(ca).reshape(N, 8, 16, L); r = ints(rt).reshape(N, 8, 16, L)
    w = wt.astype(np.int32).reshape(N, 8, 16, 1); t = th.astype(np.int32).reshape(N, 8, 16, 1)
    lev = np.zeros((N, 8, 16, L), np.int32); dep = np.zeros((N, 8, L), np.int32); ptr = np.full((N, 8, L), -1, np.int32)
    stk = np.zeros((N, 8, 16, RO, L), np.int32); A = np.zeros((N, 1, 1, 1), np.int32); height = np.arange(RO).reshape(1, 1, 1, RO, 1)
    for step in range(RO):
        kap = np.min(np.where(lev > 0, 32, r), axis=2, keepdims=True)
        can = (lev == 0) & (c > ptr[:, :, None]) & (c < kap)
        uz = mark(z, w); zz = z[:, :, :, None]
        y = pick(X, ((n * uz[:, :, None] >> 5) + n + 37 * KK + A) & (W - 1))
        zk = np.abs(zz - y); rows = np.sum(y >= zz, axis=2, dtype=np.int32)
        v = pick(V, place(mark(zk, w[..., None]), dep[:, :, None] + 1))
        far = np.sum(np.abs(v - zk), axis=2, dtype=np.int32)
        key = np.where(can & (rows >= 8) & (far > t), c, 32)
        k = np.argmin(key, axis=2); push = np.min(key, axis=2) < 32; pop = ~push & (dep > 0)
        at = place(uz, dep); wins = {}
        for q in range(N):
            for g in range(8):
                i = np.flatnonzero(pop[q, g]); p, f = np.unique(at[q, g, i], return_index=True)
                wins[q, g] = (p, z[q, g][:, i[f]])
        for d in (0,) + SH:
            for q in range(N):
                for g in range(8):
                    V[(q + d) % N, g][:, wins[q, g][0]] = wins[q, g][1]
        old = np.take_along_axis(stk, np.maximum(dep - 1, 0)[:, :, None, None, :], axis=3)[:, :, :, 0]
        new = np.take_along_axis(zk, k[:, :, None, None, :], axis=3)[:, :, :, 0]
        stk = np.where(push[:, :, None, None, :] & (dep[:, :, None, None, :] == height), zz, stk)
        P, O, D = push[:, :, None], pop[:, :, None], dep[:, :, None]
        top = O & (lev == D)
        ptr = np.where(pop, np.sum(np.where(top, c, 0), axis=2, dtype=np.int32), -1)
        lev = np.where(P & (KK == k[:, :, None]), D + 1, np.where(top, 0, lev))
        z = np.where(P, new, np.where(O, old, 63 - z))
        dep = dep + push.astype(np.int32) - pop.astype(np.int32)
        A = (np.sum(pop, axis=(1, 2)) & 31).reshape(N, 1, 1, 1)
    return {"yv": V.reshape(N, 128, W).astype(np.float32).astype(BF), "yz": z.reshape(N, 128, L).astype(np.float32).astype(BF),
            "yl": lev.reshape(N, 128, L).astype(np.float32).astype(BF), "yp": ptr.astype(np.float32)}

@@ -1,0 +1,638 @@
+import math
+from concourse.mybir import AluOpType as ALU, AxisListType, ActivationFunctionType as AF
+
+W, L, RO, SH = 2048, 256, 8, 3
+CFG = {
+    "h1": ["S2V2 S2V2 V4 V4", "S4 S4 V4 V4", "S4 S4 V4 V4"],
+    "h2": ["S2V2 S2V2 V4 V2V1V1", "S2V2 S2V2 S2V2 V2V1V1", "S2V2 S2V2 S2V2 V2V1V1"],
+    "pg": [2, 3], "lead": True,
+    "oc": [4, 12], "seed": 0, "amp": 0.0, "xl": 2500, "it": 3,
+}
+MOVES = [(36, -2500), (2103, 2500), (2170, -2500), (2054, 2500), (2116, 5000), (2040, 150), (2006, -1000), (2052, -1000), (2024, 400), (3044, 5000), (2043, 400), (2154, -1000), (2109, 5000), (30, 5000), (2008, 5000), (2140, 400), (2037, -150), (2048, -2500), (2107, 5000), (2099, 150), (1026, 2500), (2127, -150), (2095, -400), (3037, -5000), (2026, -1000), (2028, 150), (2111, 1000), (2046, 1000), (2065, -2500), (2060, -5000), (1050, -5000), (2144, -2500), (1106, 1000), (2098, 400), (2072, -1000), (2070, -1000), (2075, 1000), (2143, -5000), (2148, -400), (2010, -2500), (2066, -5000), (56, 5000), (1143, -5000), (2037, -150), (2155, 150), (95, -2500), (2078, -1000), (59, -1000), (2111, 2500), (34, 2500), (12, 1000), (2061, -5000), (2006, -150), (2154, 150), (1131, -2500), (2055, -1000), (2134, 1000), (2141, -400), (3042, -400), (3086, 2500), (2152, 1000), (3003, 1000), (3119, 2500), (2145, -5000), (2012, -150), (43, 5000), (3008, 400), (2156, 150), (2038, 150), (2143, 2500), (2142, 1000), (2155, 150), (2011, -150), (2145, 1000), (3059, -2500), (2136, 1000), (3104, 1000), (51, -2500), (2026, -150), (13, 2500), (3052, 400), (2139, 2500), (2194, -150), (52, 1000), (2164, -400), (2110, 1000), (2048, 2500), (3022, 150), (2059, -2500), (2098, 400), (2195, -150), (2155, 1000), (2137, 400), (1095, -150), (2046, 1000), (2021, -150)]
+W16 = True
+EQ16 = True
+NEZ, NEO = 8, 8
+BIG = float(2 ** 24)
+MAG = 1.5 * 2 ** 23
+POP = float(32 << 17)
+SL0 = 17
+F, B, I, U = "float32", "bfloat16", "int32", "uint16"
+
+
+def _sb(n, d):
+    return ("sbuf", [128, n], d)
+
+
+SCRATCH = {
+    "xw": _sb(W + 32, B), "vw": _sb(W + L, B), "zs": _sb(26 * L, B), "yb": _sb(4096, B), "sg": _sb(4096, B), "eb": _sb(4096, B),
+    "lz": _sb(7 * L, B), "lo": _sb(7 * 16, U), "so": _sb(7 * 16, U),
+    "nmi": _sb(L, I), "cr": _sb(2 * L, B), "wti": _sb(1, I), "thi": _sb(1, I),
+    "nf": _sb(L, F), "nw": _sb(2 * L, F), "crw": _sb(4 * L, B), "nb": _sb(L, F),
+    "cab": _sb(L, B), "ca32": _sb(L, B), "eca": _sb(L, B), "ert": _sb(L, B),
+    "pi": _sb(1, I), "ci": _sb(16, I), "cf": _sb(32, F), "cb": _sb(2, B),
+    "iq": _sb(144, F), "ig": _sb(128, F), "ik": _sb(L, F), "im": _sb(L, F), "iti": _sb(16, I), "t16": _sb(64, F), "t16i": _sb(16, I),
+    "idn": _sb(128, B), "nid": _sb(128, B), "bid": _sb(128, B), "swb": _sb(128, B), "swf": _sb(128, F),
+    "zhi": _sb(144, "float16" if W16 else B), "zpb": _sb(144, B), "zon": _sb(144, B), "znb": _sb(144, B),
+    "wb": _sb(128, B), "wd": _sb(128, B), "bb": _sb(128, B), "hal": _sb(128, F), "g8": _sb(8, B),
+    "msk": _sb(L, F), "thm": _sb(L, "float16"), "thr": _sb(L, B), "cneg": _sb(64, B),
+    "bct": _sb(16, U), "bcc": _sb(16, U), "pma": _sb(16, U), "pmb": _sb(16, U), "lc": _sb(16, F), "dum": _sb(16, F),
+    "p1": _sb(L, I), "p2": _sb(L, I), "p3": _sb(L, I), "o1": _sb(L, U),
+    "r1": _sb(L, F), "r2": _sb(L, F), "xx": _sb(L, F), "qq": _sb(L, F), "h1": _sb(L, I), "h2": _sb(L, I), "o2": _sb(L, U),
+    "pk": _sb(L, F), "key": _sb(L, F), "acc": _sb(L, F),
+    "c1": _sb(L, B), "c2": _sb(L, B), "c3": _sb(L, B), "ee": _sb(L, B), "gg": _sb(L, B), "lv": _sb(4 * L, B), "eru": _sb(L, B), "s1": _sb(16, F),
+    "kf": _sb(16, F), "ki": _sb(16, I), "u32": _sb(32, I), "a1": _sb(16, I), "a2": _sb(16, I), "a3": _sb(16, U),
+    "cc": _sb(16, I), "cx": _sb(16, I), "cl": _sb(16, F), "cs": _sb(32, F), "tri": _sb(32, F), "dl": _sb(16, F), "dtm": _sb(32, F),
+    "n1": _sb(16, F), "n2": _sb(16, F), "n3": _sb(16, F), "stk": _sb(2 * 128, F), "sd": _sb(96, F), "se": _sb(96, F), "np1": _sb(16, F),
+    "uf": _sb(16, F), "uq": _sb(16, F), "ph": _sb(16, I), "pl": _sb(32, I), "dt0": _sb(16, F),
+    "sgn": _sb(16, B), "cnt": _sb(1, F), "ar": _sb(1, I), "av": _sb(1, F), "kd": _sb(16, F), "npb": _sb(16, B), "pm": _sb(16, F),
+    "xd": _sb(L, "float16"), "pb": _sb(L, U if EQ16 else F), "eq": _sb(2176, B), "los": _sb(L, B), "w1": _sb(16, F), "w2": _sb(16, F),
+    "ylt": _sb(L, B), "ylo": _sb(L, B), "xp": _sb(L, B), "ypo": _sb(L, F),
+}
+ALIAS = {"xp": "c1", "ylt": "c2", "ylo": "c3", "ypo": "r1", "nf": "r2"}
+for _n in ALIAS:
+    SCRATCH.pop(_n, None)
+SCRATCH["idf"] = _sb(128, F)
+SCRATCH["pkc"] = _sb(L, F)
+PS = ["d0", "d1", "ur0", "ur1", "f0", "f1", "cst", "mi"]
+for _n in PS:
+    SCRATCH[_n] = ("psum", [128, 512], F)
+DMAS = ["nm", "ca", "rt", "z0", "wt", "th", "xt", "xe", "vt", "yv", "yv2", "yz", "yl", "yp"]
+SEMAPHORES = ["eV", "eS", "eP", "eG", "sent"] + ["m_" + n for n in DMAS] + ["az%d" % s for s in range(RO)] + ["ao%d" % s for s in range(RO)]
+CACHE = {}
+LAT = 70
+GC, SC, TT = 1.56, 3.8, 2.0
+
+
+def build(g, core, T, topo, rank):
+    ops, role = [], [0]
+    two = {n: SCRATCH[n][2] in (B, U, "float16") for n in SCRATCH}
+
+    def a(n, c0=0, c1=None, st=1, p=128):
+        n = ALIAS.get(n, n)
+        return (n, c0, SCRATCH[n][1][1] if c1 is None else c1, st, p)
+
+    def ind(w, o):
+        return ("*", w, o)
+
+    def ap(x):
+        if not isinstance(x, tuple):
+            return x
+        if x[0] == "*":
+            return ap(x[1]).indirect(ap(x[2]))
+        if x[3] == 1:
+            return T[x[0]][0:x[4], x[1]:x[2]]
+        return T[x[0]][0:x[4], x[1]:x[2]:x[3]]
+
+    def regs(xs):
+        r = []
+        for x in xs:
+            if isinstance(x, tuple):
+                r += [x[1], x[2]] if x[0] == "*" else [x]
+        return r
+
+    def num(x):
+        return 16 * num(x[2]) if x[0] == "*" else len(range(x[1], x[2], x[3]))
+
+    def add(e, cost, rd, wr, fn, sem=None, lat=0, after=None):
+        r, w = regs(rd), []
+        for x in wr:
+            if x[0] == "*":
+                w.append(x[1]); r.append(x[2])
+            else:
+                w.append(x)
+        ops.append({"e": e, "c": cost, "r": r, "w": w, "f": fn, "sem": sem, "lat": lat, "after": after, "role": role[0]})
+        role[0] += 1
+        return len(ops) - 1
+
+    def vcost(o, i, rate=None):
+        n = num(o)
+        if o[0] == "*":
+            return 60 + SC * n
+        if i[0] == "*":
+            return 60 + GC * n
+        if rate is None:
+            rate = 0.5 if two[o[0]] and two[i[0]] else 1.0
+        return 20 + max(64, rate * n)
+
+    def cp(o, i):
+        add("V", vcost(o, i), [i], [o], lambda: g.vector.tensor_copy(ap(o), ap(i)))
+
+    def ms(o, v):
+        add("V", 20 + max(64, num(o) * (0.5 if two[o[0]] else 1)), [], [o], lambda: g.vector.memset(ap(o), v))
+
+    def tt(o, x, y, op):
+        rate = 1.0 if (x[0] in PS or y[0] in PS) else TT
+        add("V", vcost(o, x, rate), [x, y], [o], lambda: g.vector.tensor_tensor(ap(o), ap(x), ap(y), op))
+
+    def ts(o, x, s1, op0, s2=None, op1=None):
+        if op1 is None:
+            fn = lambda: g.vector.tensor_scalar(ap(o), ap(x), ap(s1), None, op0)
+        else:
+            fn = lambda: g.vector.tensor_scalar(ap(o), ap(x), ap(s1), ap(s2), op0, op1)
+        add("V", vcost(o, x), [x, s1, s2], [o], fn)
+
+    def tr(o, i):
+        add("V", vcost(o, i), [i], [o], lambda: g.vector.transpose(ap(o), ap(i)))
+
+    def act(o, i, f, bias=0.0, scale=1.0, acc=None):
+        c = (80 + GC * num(o)) if i[0] == "*" else 40 + max(64, num(o))
+        if acc is None:
+            fn = lambda: g.scalar.activation(ap(o), ap(i), f, bias=ap(bias), scale=ap(scale))
+        else:
+            fn = lambda: g.scalar.activation(ap(o), ap(i), f, bias=ap(bias), scale=ap(scale), accum_out=ap(acc))
+        add("S", c, [i, bias, scale], [o] + ([acc] if acc else []), fn)
+
+    def mm(items, start=True, stop=True):
+        def fn():
+            r = None
+            for j, (o, l, x) in enumerate(items):
+                r = g.tensor.matmul(ap(o), ap(l), ap(x), start and j == 0, stop and j == len(items) - 1)
+            return r
+        c = sum(max(64, num(x)) * (0.5 if two[x[0]] else 2.0) for o, l, x in items) + 40
+        add("P", c, [z for o, l, x in items for z in (l, x)], [o for o, l, x in items], fn)
+
+    def red(o, z, src, c0, c1):
+        return [(o, a(z, 15 - m, 143 - m), a(src, c0 + m, c1, 16)) for m in range(16)]
+
+    def ured(o, src, c0, c1):
+        return red(o, "zhi", src, c0, c1) + ([] if W16 else red(o, "zlo", src, c0, c1))
+
+    def iota(o, pat, base=0, cm=0):
+        if SCRATCH[o[0]][2] == I:
+            fn = lambda: g.iota(ap(o), pat, base, cm)
+        else:
+            fn = lambda: g.iota(ap(o), pat, base, cm, allow_small_or_imprecise_dtypes=True)
+        add("G", 160 + 2 * num(o), [], [o], fn)
+
+    def dma(q, name, o, i, lat):
+        eng = g.sync if q == "Y" else g.scalar
+        add(q, 70, [i], [o] if isinstance(o, tuple) else [], lambda: eng.dma_start(ap(o), ap(i)), sem=("m_" + name, 16), lat=lat)
+
+    dst = T.cores[(rank + SH) % len(T.cores)]
+    src = T.cores[(rank - SH) % len(T.cores)]
+    rid, pid = topo.addr(dst, core)
+    sent = [0]
+
+    def send(o, i, sem, ne, lat):
+        en = topo.engines(core, dst)[:ne]
+        m = sum(1 << e for e in en)
+        sent[0] += len(en)
+        j = add("G", 600, [i], [], lambda: g.remote_dma(ap(o), ap(i), T.sem[sem], T.sem.sent, pid, rid, m), sem=("", 0))
+        add("X", 0, [], [o], None, sem=(sem, len(topo.engines(src, core)[:ne])), lat=lat, after=j)
+
+    def zsl(s):
+        return a("zs", s * L, (s + 1) * L)
+
+    def col(n, j):
+        return a(n, j, j + 1)
+
+    dma("Y", "nm", a("nmi"), T.nm[:], 2400)
+    dma("S", "z0", zsl(SL0), T.z0[:], 2400)
+    dma("Y", "wt", a("wti"), T.wt[:], 2400)
+    dma("S", "xe", a("xw", W, W + 32), T.xt[:, 0:32], 2400)
+    dma("Y", "xt", a("xw", 0, W), T.xt[:], 4500)
+    dma("S", "ca", a("cr", 0, L), T.ca[:], 2600)
+    dma("S", "rt", a("cr", L, 2 * L), T.rt[:], 2600)
+    dma("S", "th", a("thi"), T.th[:], 2600)
+    dma("Y", "vt", a("vw", 0, W), T.vt[:], 6000)
+    iota(a("pi"), [[0, 1]], 0, 1)
+    iota(a("iq"), [[1, 144]])
+    iota(a("iti"), [[1, 16]])
+    iota(a("ik"), [[1, 16], [0, 16]])
+    iota(a("ig"), [[16, 8], [0, 16]])
+    iota(a("im"), [[0, 16], [1, 16]])
+    AND, SHR = ALU.bitwise_and, ALU.arith_shift_right
+    P_, M_, G_, Z_, X_, SW, TH, WH, WL, CN, PA, Y_, TB, TC = range(14)
+    cp(col("cf", P_), a("pi"))
+    ts(col("ci", 0), a("pi"), 15, AND); cp(col("cf", M_), col("ci", 0))
+    tt(col("cf", G_), col("cf", P_), col("cf", M_), ALU.subtract)
+    ts(col("cf", Z_), col("cf", G_), 15.0, ALU.add)
+    ts(col("ci", 1), a("pi"), 4, SHR, 1, AND); cp(col("cf", X_), col("ci", 1))
+    ts(col("cf", TB), col("cf", X_), -32.0, ALU.mult, col("cf", P_), ALU.add)
+    ts(col("cf", SW), col("cf", TB), 16.0, ALU.add)
+    ts(a("swf"), a("iq", 0, 128), col("cf", SW), ALU.is_equal)
+    ts(col("ci", 2), a("pi"), 1, AND); ts(col("ci", 3), a("pi"), 14, AND)
+    ts(col("cf", Y_), col("ci", 2), col("cf", X_), ALU.not_equal, 256.0, ALU.mult)
+    ts(col("cf", TC), col("ci", 3), col("cf", X_), ALU.add, 16.0, ALU.mult)
+    ts(a("pma"), a("iti"), col("cf", Y_), ALU.add, col("cf", TC), ALU.add)
+    ts(a("bct"), a("iti"), 0.0, ALU.mult, col("cf", M_), ALU.add)
+    cp(a("nf"), a("nmi")); tr(a("nw", 0, L), a("nf"))
+    mm([(a("mi", 0, L), a("swf"), a("nw", 0, L))])
+    act(a("nw", L, 2 * L), a("mi", 0, L), AF.Identity)
+    cp(a("nb"), ind(a("nw"), a("pma")))
+    if W16:
+        ts(col("ci", 4), a("wti"), 2047, AND); cp(col("cf", WH), col("ci", 4))
+    else:
+        ts(col("ci", 4), a("wti"), 2040, AND); cp(col("cf", WH), col("ci", 4))
+        ts(col("ci", 5), a("wti"), 7, AND); cp(col("cf", WL), col("ci", 5))
+        ts(a("zlo"), a("iq"), col("cf", Z_), ALU.is_equal, col("cf", WL), ALU.mult)
+    ts(a("zhi"), a("iq"), col("cf", Z_), ALU.is_equal, col("cf", WH), ALU.mult)
+    act(zsl(16), zsl(SL0), AF.Identity, bias=63.0, scale=-1.0)
+    mm(ured(a("ur0", 0, 32), "zs", 16 * L, 18 * L))
+    cp(a("h1", 0, 32), a("ur0", 0, 32)); ts(a("h2", 0, 32), a("h1", 0, 32), 2047, AND)
+    ts(a("u32", 0, 16), a("h2", 16, 32), 32.0, ALU.add)
+    ts(a("stk", 16, 32), a("h2", 0, 16), float((31 << 17) + 16 * 4096 + 32), ALU.add)
+    ts(a("cst", L, 2 * L), a("ik"), 1184.0, ALU.mult)
+    ts(a("idn"), a("iq", 0, 128), col("cf", P_), ALU.is_equal)
+    ts(a("nid"), a("idn"), -1.0, ALU.mult); ts(a("bid"), a("idn"), 2048.0 * BIG, ALU.mult)
+    ts(a("zon"), a("iq"), col("cf", Z_), ALU.is_equal); ts(a("znb"), a("zon"), -BIG, ALU.mult); ts(a("zpb"), a("zon"), BIG, ALU.mult)
+    ts(a("wb"), a("ig"), col("cf", G_), ALU.is_equal, 65536.0, ALU.mult)
+    ts(a("bb"), a("wb"), 256.0, ALU.mult)
+    ts(col("cf", CN), col("cf", M_), 0.0, ALU.is_equal, -2.0 ** -6, ALU.mult)
+    ts(col("cf", PA), col("cf", M_), 1.0, ALU.is_equal, 2.0 ** -17, ALU.mult)
+    ts(a("t16"), a("iq", 0, 64), 0.0, ALU.mult, col("cf", CN), ALU.add)
+    ts(a("cneg"), a("t16"), col("cf", PA), ALU.add)
+    ts(col("cf", TH), a("thi"), 0.5, ALU.add)
+    ts(a("thm"), a("ik"), col("cf", M_), ALU.is_equal, col("cf", TH), ALU.mult)
+    cp(a("swb"), a("swf"))
+    LN2 = math.log(2.0)
+    for h in range(2):
+        tr(a("crw", 2 * h * L, (2 * h + 1) * L), a("cr", h * L, (h + 1) * L))
+        mm([(a("mi", 0, L), a("swb"), a("crw", 2 * h * L, (2 * h + 1) * L))])
+        act(a("crw", (2 * h + 1) * L, (2 * h + 2) * L), a("mi", 0, L), AF.Identity)
+    act(a("cab"), ind(a("crw", 0, 2 * L), a("pma")), AF.Identity)
+    act(a("eca"), a("cab"), AF.Exp, bias=31 * LN2, scale=-LN2)
+    act(a("ert"), ind(a("crw", 2 * L, 4 * L), a("pma")), AF.Exp, bias=31 * LN2, scale=-LN2)
+    act(col("cb", 0), col("cf", M_), AF.Exp, bias=-1 * LN2, scale=-LN2)
+    act(a("thr"), a("im"), AF.Exp, bias=16 * LN2, scale=-LN2)
+    ts(a("ca32"), a("cab"), 32.0, ALU.add)
+    ts(a("acc"), a("ik"), 4096.0, ALU.mult, 1055.5, ALU.add)
+    act(a("key"), a("cab"), AF.Identity, scale=float(1 << 17))
+    tt(a("pkc"), a("key"), a("acc"), ALU.add)
+    ts(a("idf"), a("iq", 0, 128), col("cf", P_), ALU.is_equal)
+    ts(a("wd"), a("wb"), col("cb", 0), ALU.mult)
+    ts(a("msk"), a("im"), col("cf", M_), ALU.is_equal)
+    cp(a("bcc"), a("iti"))
+    ts(a("lc"), a("iti"), 16.0, ALU.mult, col("cf", M_), ALU.add); ts(a("dum"), a("lc"), float(W), ALU.add)
+    ms(a("hal"), 0.5); ms(a("vw", W, W + L), 0.0); ms(a("cs", 0, 16), 0.0); ms(a("tri", 0, 16), 0.25)
+    ms(a("dtm", 0, 16), 19616.0 - 592.0 ** 2)
+    ms(a("stk", 32, 128), 0.0); ms(a("stk", 144, 256), 0.0)
+    ts(a("t16i"), a("iti"), 1, AND)
+    ts(a("w1"), a("t16i"), col("cf", X_), ALU.not_equal, 256.0, ALU.mult)
+    ts(a("a1"), a("iti"), 14, AND); tt(a("w2"), a("w1"), a("a1"), ALU.add)
+    ts(col("cf", TC + 1), col("cf", M_), 16.0, ALU.mult, col("cf", X_), ALU.add)
+    ts(a("pmb"), a("w2"), col("cf", TC + 1), ALU.add)
+    ts(a("g8"), a("ig", 0, 128, 16), col("cf", G_), ALU.is_equal)
+
+    blk = [0]
+
+    def chunks(text):
+        r, k = [], 0
+        for x in text.split():
+            r.append([])
+            for i in range(0, len(x), 2):
+                r[-1].append((x[i], k, k + int(x[i + 1]))); k += int(x[i + 1])
+        return r
+
+    def columns(s):
+        c0, first = 0, None
+        for nk in CFG["oc"]:
+            c1 = c0 + 16 * nk
+            tt(a("p1", c0, c1), ind(a("u32", 16 * (s % 2), 16 * (s % 2) + 16), a("bct", 0, nk)), a("nb", c0, c1), ALU.mult)
+            tt(a("p2", c0, c1), a("p1", c0, c1), a("cst", L + c0, L + c1), ALU.add)
+            ts(a("p3", c0, c1), a("p2", c0, c1), 5, SHR, 2047, AND)
+            if s >= 2:
+                ts(a("o1", c0, c1), a("p3", c0, c1), a("av"), ALU.add)
+            else:
+                cp(a("o1", c0, c1), a("p3", c0, c1))
+            c0 = c1
+            first = len(ops) - 1 if first is None else first
+        return first
+
+    for s in range(RO):
+        pa, pb_ = s % 2, (s + 1) % 2
+        z = zsl(SL0 + s)
+        u32, dtm, lv = a("u32", 16 * pa, 16 * pa + 16), a("dtm", 16 * pa, 16 * pa + 16), a("lv", 2 * pa * L, (2 * pa + 1) * L)
+        last = s == RO - 1
+        kind = 0 if s == 0 else 2 if last else 1
+        role[0] = 1000 * (kind + 1)
+        h1, h2 = chunks(CFG["h1"][kind]), chunks(CFG["h2"][kind])
+        if s == 0:
+            columns(0)
+        else:
+            send(a("lz", (s - 1) * L, s * L), z, "az%d" % s, NEZ, 3000)
+        if s == 0:
+            mm([(a("f1", L, L + 16), a("idn"), a("ert", 16 * k, 16 * k + 16)) for k in range(16)])
+        else:
+            mm([(a("f1", 0, L), a("bid"), lv), (a("f1", 0, L), a("nid"), a("ert"))])
+            act(a("eru"), a("f1", 0, L), AF.Relu, scale=-1.0)
+            mm([(a("f1", L, L + 16), a("idn"), a("eru", 16 * k, 16 * k + 16)) for k in range(16)])
+        act(a("s1"), a("f1", L, L + 16), AF.Identity)
+        tt(a("c1"), ind(a("s1"), a("bct")), a("eca"), ALU.is_ge)
+        if s >= 1:
+            tt(a("c2"), ind(a("cc"), a("bct")), a("ca32"), ALU.is_ge)
+            pl = a("pl", 16 * pa, 16 * pa + 16)
+            cp(a("uf"), u32); act(a("uq"), a("uf"), AF.Square, bias=560.0)
+            act(a("dt0"), dtm, AF.Identity, bias=-19616.0)
+            tt(a("ph"), a("uq"), a("dt0"), ALU.add); ts(pl, a("ph"), 5, SHR, 2047, AND)
+        def pens(c0, c1):
+            return [a("c1", c0, c1), a("c3", c0, c1)] + ([a("c2", c0, c1), a("lv", lv[1] + c0, lv[1] + c1)] if s else [])
+
+        pk0 = 0
+        for c, pieces in enumerate(h1):
+            for md, k0, k1 in pieces:
+                if md == "S":
+                    act(a("yb", k0 * L, k1 * L), ind(a("xw"), a("o1", 16 * k0, 16 * k1)), AF.Identity)
+                    for k in range(k0, k1, 2):
+                        d = "d%d" % (blk[0] % 2); blk[0] += 1
+                        n = min(2, k1 - k)
+                        mm([(a(d, 0, n * L), a("idn"), a("yb", k * L, (k + n) * L))] + [(a(d, i * L, (i + 1) * L), a("nid"), z) for i in range(n)])
+                        act(a("zs", k * L, (k + n) * L), a(d, 0, n * L), AF.Abs)
+                        act(a("sg", k * L, (k + n) * L), a(d, 0, n * L), AF.Sign, bias=0.5)
+                else:
+                    for k in range(k0, k1):
+                        tt(a("yb", k * L, (k + 1) * L), ind(a("xw"), a("o1", 16 * k, 16 * k + 16)), z, ALU.subtract)
+                    act(a("zs", k0 * L, k1 * L), a("yb", k0 * L, k1 * L), AF.Abs)
+                    if md == "V":
+                        ts(a("sg", k0 * L, k1 * L), a("yb", k0 * L, k1 * L), 0.0, ALU.is_ge, -0.5, ALU.add)
+                    else:
+                        act(a("sg", k0 * L, k1 * L), a("yb", k0 * L, k1 * L), AF.Sign, bias=0.5)
+            k0, k1 = pieces[0][1], pieces[-1][2]
+            c0, c1, w = 16 * k0, 16 * k1, 16 * (k1 - k0)
+            ur = "ur%d" % (c % 2)
+            mm([(a(ur, 0, w), a("wb"), a("cneg", 0, w))] + ured(a(ur, 0, w), "zs", k0 * L, k1 * L))
+            act(a("r1", c0, c1), a(ur, 0, w), AF.Identity, bias=MAG, scale=2.0 ** -11)
+            act(a("r2", c0, c1), a("r1", c0, c1), AF.Identity, bias=2048.0 * MAG, scale=-2048.0)
+            tt(a("xx", c0, c1), a(ur, 0, w), a("r2", c0, c1), ALU.add)
+            act(a("qq", c0, c1), a("xx", c0, c1), AF.Square, bias=1615.5)
+            mm(red(a("f0", c0, c1), "zon", "sg", k0 * L, k1 * L))
+            if c in CFG["pg"]:
+                act(a("c3", pk0, c1), a("f0", pk0, c1), AF.Relu, scale=-1.0)
+                mm([(a("cst", pk0, c1), a("idf"), a("pkc", pk0, c1))] + [(a("cst", pk0, c1), a("bid"), x) for x in pens(pk0, c1)])
+                tt(a("pk", pk0, c1), a("xx", pk0, c1), a("cst", pk0, c1), ALU.add)
+                pk0 = c1
+            tt(a("h1", c0, c1), ind(dtm, a("bct", 0, w // 16)), a("qq", c0, c1), ALU.add)
+            ts(a("h2", c0, c1), a("h1", c0, c1), 5, SHR, 2047, AND)
+            cp(a("o2", c0, c1), a("h2", c0, c1))
+        if s >= 1:
+            tt(a("xd"), ind(pl, a("bcc")), a("msk"), ALU.mult)
+            mm([(a("mi", 0, L), a("wb"), a("xd"))])
+            ts(a("pb"), a("mi", 0, L), 2.0 ** -16, ALU.mult)
+        top = a("stk", 128 * pa + 16, 128 * pa + 32)
+        cur, off = None, 0
+        for c, pieces in enumerate(h2):
+            for md, k0, k1 in pieces:
+                e = a("eb", k0 * L, k1 * L)
+                v = ind(a("vw", 0, W), a("o2", 16 * k0, 16 * k1))
+                if md == "S":
+                    act(e, v, AF.Identity)
+                    for k in range(k0, k1, 2):
+                        d = "d%d" % (blk[0] % 2); blk[0] += 1
+                        n = min(2, k1 - k) * L
+                        mm([(a(d, 0, n), a("idn"), a("eb", k * L, k * L + n)), (a(d, 0, n), a("nid"), a("zs", k * L, k * L + n))])
+                        act(a("eb", k * L, k * L + n), a(d, 0, n), AF.Abs)
+                else:
+                    tt(e, v, a("zs", k0 * L, k1 * L), ALU.subtract)
+                    if md == "V":
+                        act(e, e, AF.Abs)
+                    else:
+                        ts(a("yb", k0 * L, k1 * L), e, 0.0, ALU.max, 2.0, ALU.mult)
+            k0, k1 = pieces[0][1], pieces[-1][2]
+            c0, c1, w = 16 * k0, 16 * k1, 16 * (k1 - k0)
+            f = a("f%d" % ((c + 1) % 2), 0, w)
+            if md == "R":
+                mm([(f, a("bb"), a("thm", c0, c1))] + red(f, "zpb", "eb", k0 * L, k1 * L), stop=False)
+                mm(red(f, "znb", "yb", k0 * L, k1 * L), start=False)
+            else:
+                mm([(f, a("bb"), a("thm", c0, c1))] + red(f, "znb", "eb", k0 * L, k1 * L))
+            key = a("key", c0, c1)
+            tt(key, f, a("pk", c0, c1), ALU.max)
+            if cur is None:
+                tt(a("key", 0, 16), a("key", 0, 16), top, ALU.min)
+                cur = key
+            else:
+                nx = a("kf") if w == 16 and c + 1 == len(h2) else a("acc", off, off + w)
+                off += w
+                tt(nx, cur, key, ALU.min)
+                cur = nx
+            wn = 16 * (h2[c + 1][-1][2] - h2[c + 1][0][1]) if c + 1 < len(h2) else 16
+            while num(cur) > wn:
+                h = num(cur) // 2
+                nx = a("kf") if h == 16 and c + 1 == len(h2) else a("acc", off, off + h)
+                off += h
+                tt(nx, a(cur[0], cur[1], cur[1] + h), a(cur[0], cur[1] + h, cur[2]), ALU.min)
+                cur = nx
+        cp(a("ki"), a("kf"))
+        if s >= 1:
+            if not last:
+                act(a("sgn"), a("kf"), AF.Sign, bias=-POP, acc=a("cnt"))
+                mm([(a("mi", 300, 301), a("hal"), a("cnt"))])
+            act(a("kd"), a("kf"), AF.Identity, bias=-POP)
+            act(a("npb"), a("kf"), AF.Relu, bias=POP, scale=-1.0)
+        if not last:
+            ts(a("u32", 16 * pb_, 16 * pb_ + 16), a("ki"), 4095, AND)
+            if s >= 1:
+                ts(a("ar"), a("mi", 300, 301), 1.0 / 32, ALU.mult, -31.0 / 64, ALU.add)
+                ts(a("av"), a("ar"), -32.0, ALU.mult, a("mi", 300, 301), ALU.add)
+            lead = columns(s + 1)
+        ts(a("a1"), a("ki"), 4, SHR, 31 << 8, AND); tt(a("a2"), a("a1"), a("lc"), ALU.add); cp(a("a3"), a("a2"))
+        cp(zsl(SL0 + s + 1), ind(a("zs", 0, (SL0 + s + 1) * L), a("a3")))
+        ts(a("cc"), a("ki"), 17, SHR); ts(a("cx"), a("ki"), 17, SHR, 31, AND)
+        ts(a("cl"), a("cc"), 30.0, ALU.max, 32.0, ALU.min)
+        cs, tri = a("cs", 16 * pb_, 16 * pb_ + 16), a("tri", 16 * pb_, 16 * pb_ + 16)
+        tt(cs, a("cs", 16 * pa, 16 * pa + 16), a("cl"), ALU.add)
+        act(tri, cs, AF.Square, bias=31.0 * (s + 1) + 0.5, scale=-1.0)
+        tt(a("dl"), tri, a("tri", 16 * pa, 16 * pa + 16), ALU.subtract)
+        tt(a("ee"), ind(a("cx"), a("bct")), a("cab"), ALU.is_equal)
+        tt(a("gg"), ind(a("dl"), a("bct")), a("ee"), ALU.mult)
+        if s == 0:
+            cp(a("lv", 2 * pb_ * L, (2 * pb_ + 1) * L), a("gg"))
+        else:
+            mm([(a("f1", 0, L), a("idn"), lv), (a("f1", 0, L), a("idn"), a("gg"))])
+            act(a("lv", 2 * pb_ * L, (2 * pb_ + 1) * L), a("f1", 0, L), AF.Identity)
+        if not last:
+            act(a("dtm", 16 * pb_, 16 * pb_ + 16), cs, AF.Identity, bias=19616.0 * (31 * (s + 1) + 1) - 592.0 ** 2, scale=-19616.0)
+            nl = 16 * min(s + 2, RO - 1 - s)
+            b0, b1 = 128 * pa, 128 * pb_
+            act(a("n1"), a("cl"), AF.Identity, bias=float(31 * 2 ** 22 + (SL0 + s) * 4096), scale=-float(2 ** 22))
+            act(a("np1"), a("cl"), AF.Sign, bias=32.0, scale=-1.0)
+            ts(a("n3"), a("cc"), float(1 << 17), ALU.mult)
+            tt(a("n2"), a("n3"), u32, ALU.add); tt(a("stk", b0, b0 + 16), a("n2"), a("n1"), ALU.add)
+            tt(a("sd", 0, nl), a("stk", b0, b0 + nl), a("stk", b0 + 32, b0 + 32 + nl), ALU.subtract)
+            tt(a("se", 0, nl), ind(a("np1"), a("bct", 0, nl // 16)), a("sd", 0, nl), ALU.mult)
+            tt(a("stk", b1 + 16, b1 + 16 + nl), a("se", 0, nl), a("stk", b0 + 32, b0 + 32 + nl), ALU.add)
+        if s >= 1:
+            tt(a("pm"), pl, a("kd"), ALU.min)
+            if not last and CFG["lead"]:
+                ops[-1]["after"] = lead
+            mm([(a("mi", 0, L), a("nid"), a("thr"))], stop=False)
+            o = 0
+            for t in range(16):
+                n = L - 16 * t
+                ts(a("eq", o, o + n), a("pb", 16 * t, L), col("pm", t), ALU.is_equal)
+                it = [(a("mi", 16 * t, 16 * t + 16), a("wd"), a("eq", o, o + 16))]
+                if t < 15:
+                    it.append((a("mi", 16 * t + 16, L), a("wb"), a("eq", o + 16, o + n)))
+                mm(it, start=False, stop=t == 15)
+                o += n
+            act(a("los"), a("mi", 0, L), AF.Relu, bias=256.0, scale=256.0)
+            mm([(a("mi", L, L + 16), a("idn"), a("npb"))] + red(a("mi", L, L + 16), "zon", "los", 0, L))
+            tt(a("w1"), a("mi", L, L + 16), pl, ALU.max); tt(a("w2"), a("w1"), a("dum"), ALU.min)
+            so = a("so", 16 * (s - 1), 16 * s)
+            cp(so, a("w2"))
+            send(a("lo", 16 * (s - 1), 16 * s), so, "ao%d" % s, NEO, CFG["xl"])
+            cp(ind(a("vw"), so), z)
+            cp(ind(a("vw"), a("lo", 16 * (s - 1), 16 * s)), a("lz", (s - 1) * L, s * L))
+    dma("Y", "yz", T.yz[:], zsl(SL0 + RO), 2400)
+    mm([(a("ur0", 0, L), a("swb"), a("lv", 0, L))])
+    act(a("lv", L, 2 * L), a("ur0", 0, L), AF.Identity)
+    act(a("ylt"), ind(a("lv", 0, 2 * L), a("pmb")), AF.Identity, scale=0.5)
+    tr(a("ylo"), a("ylt"))
+    dma("Y", "yl", T.yl[:], a("ylo"), 2400)
+    tt(a("xp"), ind(a("cc"), a("bcc")), a("msk"), ALU.mult)
+    mm([(a("ur1", 0, L, 1, 8), a("g8"), a("xp"))])
+    ts(a("ypo", 0, L, 1, 8), a("ur1", 0, L, 1, 8), -32.0, ALU.add, -1.0, ALU.max)
+    dma("Y", "yp", T.yp[:], a("ypo", 0, L, 1, 8), 2400)
+    dma("Y", "yv", T.yv[:, 0:W // 2], a("vw", 0, W // 2), 3500)
+    dma("S", "yv2", T.yv[:, W // 2:W], a("vw", W // 2, W), 3500)
+    return ops, sent[0]
+
+
+def plan(ops, hook=None):
+    n = len(ops)
+    dep = [dict() for _ in range(n)]
+    hist, turn = {}, {}
+    for j, o in enumerate(ops):
+        if o["after"] is not None:
+            dep[j][o["after"]] = False
+        for x, wr in [(x, False) for x in o["r"]] + [(x, True) for x in o["w"]]:
+            h = hist.setdefault(x[0], [])
+            ps = x[0] in PS
+            for (i, c0, c1, w) in h:
+                if i == j:
+                    continue
+                hit = c0 < x[2] and x[1] < c1 and (w or wr)
+                same = ops[i]["e"] == o["e"]
+                if ps and not same:
+                    dep[j][i] = True
+                elif ps and o["e"] == "P":
+                    dep[j].setdefault(i, False)
+                elif hit:
+                    dep[j][i] = True
+            if ps:
+                if h and ops[h[-1][0]]["e"] != o["e"]:
+                    h[:] = [e for e in h if ops[e[0]]["e"] == ops[h[-1][0]]["e"] and e[0] > turn.get(x[0], -1)]
+                    turn[x[0]] = j - 1
+            elif wr:
+                h[:] = [e for e in h if not (x[1] <= e[1] and e[2] <= x[2])]
+            h.append((j, x[1], x[2], wr))
+    pri = [0.0] * n
+    succ = [[] for _ in range(n)]
+    for j in range(n):
+        for i in dep[j]:
+            succ[i].append(j)
+    cost = [max(o["c"], 1.0) for o in ops]
+    back = [[(i, ops[i]["lat"] + LAT if dep[j][i] else 0.0) for i in dep[j]] for j in range(n)]
+    fwd = [[(k, ops[j]["lat"] + LAT if dep[k][j] else 0.0) for k in succ[j]] for j in range(n)]
+    x = CFG["seed"] * 7919 + 1
+    for j in range(n - 1, -1, -1):
+        x = (x * 1103515245 + 12345) % 2147483648
+        pri[j] = cost[j] * (1.0 + CFG["amp"] * x / 2147483648.0) + max([pri[k] + d for k, d in fwd[j]] + [ops[j]["lat"]])
+
+    def place(turns, pre, head):
+        st, line = [0.0] * n, {}
+        for j in turns:
+            t = max([st[i] + cost[i] + d for i, d in pre[j]] + [head[j]])
+            s0, s1 = line.setdefault(ops[j]["e"], ([], []))
+            lo, hi = 0, len(s1)
+            while lo < hi:
+                mid = (lo + hi) // 2
+                if s1[mid] <= t:
+                    lo = mid + 1
+                else:
+                    hi = mid
+            while lo < len(s0) and s0[lo] < t + cost[j]:
+                t = max(t, s1[lo]); lo += 1
+            s0.insert(lo, t); s1.insert(lo, t + cost[j]); st[j] = t
+        return st
+
+    zero, tail = [0.0] * n, [o["lat"] for o in ops]
+    st = place(sorted(range(n), key=lambda j: -pri[j]), back, zero)
+    best = None
+    for _ in range(CFG["it"]):
+        end = max(st[j] + cost[j] + tail[j] for j in range(n))
+        if best is None or end < best[0]:
+            best = (end, st)
+        rv = place(sorted(range(n), key=lambda j: -(st[j] + cost[j])), fwd, tail)
+        st = place(sorted(range(n), key=lambda j: -(rv[j] + cost[j])), back, zero)
+    end, st = best
+
+    def move(st, role, by):
+        key = [st[j] + (by if ops[j]["role"] == role else 0.0) for j in range(n)]
+        for j in range(n):
+            for i in dep[j]:
+                if key[j] <= key[i]:
+                    key[j] = key[i] + 0.01
+        return place(sorted(range(n), key=lambda j: key[j]), back, zero)
+
+    for role, by in MOVES:
+        st = move(st, role, by)
+    if hook is not None:
+        st = hook(st, move, back)
+    end = max(st[j] + cost[j] + tail[j] for j in range(n))
+    order = sorted((st[j], j) for j in range(n))
+    seq = [j for t, j in order]
+    pos, cnt = {}, {}
+    for j in seq:
+        e = ops[j]["e"]
+        if ops[j]["sem"] is None:
+            cnt[e] = cnt.get(e, 0) + 1
+            pos[j] = (e, cnt[e])
+        else:
+            pos[j] = (j, 1)
+    known, clock, waits, need = {}, {}, {}, set()
+    for j in seq:
+        e = ops[j]["e"]
+        if e == "X":
+            clock[j] = {j: 1}
+            continue
+        kn = known.setdefault(e, {})
+        ws = []
+        for i in sorted((i for i in dep[j] if dep[j][i]), key=lambda i: -pos[i][1]):
+            key, p = pos[i]
+            if kn.get(key, 0) < p:
+                ws.append(i); need.add(i)
+                for k2, p2 in clock[i].items():
+                    if kn.get(k2, 0) < p2:
+                        kn[k2] = p2
+        waits[j] = ws
+        clock[j] = dict(kn); clock[j][pos[j][0]] = pos[j][1]
+    return {"seq": seq, "waits": waits, "need": need, "end": end, "order": order}
+
+
+def rank_program(g, core, T, topo):
+    rank = T.rank_of(core)
+    if rank is None:
+        return
+    ops, sent = build(g, core, T, topo, rank)
+    if "p" not in CACHE:
+        CACHE["p"] = plan(ops)
+    p = CACHE["p"]
+    q = {"V": g.vector, "S": g.scalar, "P": g.tensor, "G": g, "Y": g.sync}
+    val, cnt = {}, {"V": 0, "S": 0, "P": 0, "G": 0}
+    for j in p["seq"]:
+        o = ops[j]
+        if o["sem"] is not None:
+            val[j] = o["sem"]
+        elif j in p["need"]:
+            cnt[o["e"]] += 1
+            val[j] = ("e" + o["e"], cnt[o["e"]])
+    for j in p["seq"]:
+        o = ops[j]
+        if o["e"] == "X":
+            continue
+        for i in p["waits"][j]:
+            q[o["e"]].wait_ge(T.sem[val[i][0]], val[i][1])
+        r = o["f"]()
+        if o["sem"] is not None:
+            if o["sem"][0]:
+                r.then_inc(T.sem[o["sem"][0]], 16)
+        elif j in p["need"]:
+            r.then_inc(T.sem["e" + o["e"]], 1)
+    for e in cnt:
+        if cnt[e]:
+            g.wait_ge(T.sem["e" + e], cnt[e])
+    g.wait_ge(T.sem.sent, sent)
+    for o in ops:
+        if o["sem"] is not None and o["sem"][0]:
+            g.wait_ge(T.sem[o["sem"][0]], o["sem"][1])

@@ -3,20 +3,22 @@ from concourse.mybir import AluOpType as ALU, AxisListType, ActivationFunctionTy
 
 W, L, RO, SH = 2048, 256, 8, 3
 CFG = {
-    "h1": ["S2V2 S2V2 V4 V4", "S4 S4 V4 V4", "S4 S4 V4 V4"],
-    "h2": ["S2V2 S2V2 V4 V2V1V1", "S2V2 S2V2 S2V2 V2V1V1", "S2V2 S2V2 S2V2 V2V1V1"],
-    "pg": [2, 3], "lead": True,
-    "oc": [4, 12], "seed": 0, "amp": 0.0, "xl": 2500, "it": 3,
+    "h1": ["S4 B4 B4 B4"] * 3,
+    "h2": ["S2V2 S2V2 S2V2 V4"] * 3,
+    "oc": [8, 8], "seed": 0, "amp": 0.0, "xl": 4000, "it": 3, "po": 10, "zv": "S", "tries": 9000,
+    "lat": 250, "pm": 0, "px": 0.05, "ov": 5, "soft": False, "fb": 1000, "views": [], "f": 1.3, "gm": 0.85, "k0": 0.75, "k1": 1.1, "heat": 300, "cv": True, "a3": "P",
+    "uv": "VVVV", "kv": "DDDC", "kb": ["m2", "k0", "k1", "m2"], "ord": ["XXXXERRRRVVVV"] * 3,
+    "hint": True, "tx": [1900, 2600, 5000, 7400], "tv": [12000, 12000, 13500, 13000, 15000, 14000, 15000], "tr": [7000, 9000, 11000, 13000],
+    "rb": ["m1"] * 4, "tb": [1500, 3500, 5000, 3000, 8000, 5000], "td": [0, 7000, 4000, 10500, 9000, 10000], "eb": ["d0", "d1"], "fk": ["ff", "m1", "ff", "m1"],
 }
-MOVES = [(36, -2500), (2103, 2500), (2170, -2500), (2054, 2500), (2116, 5000), (2040, 150), (2006, -1000), (2052, -1000), (2024, 400), (3044, 5000), (2043, 400), (2154, -1000), (2109, 5000), (30, 5000), (2008, 5000), (2140, 400), (2037, -150), (2048, -2500), (2107, 5000), (2099, 150), (1026, 2500), (2127, -150), (2095, -400), (3037, -5000), (2026, -1000), (2028, 150), (2111, 1000), (2046, 1000), (2065, -2500), (2060, -5000), (1050, -5000), (2144, -2500), (1106, 1000), (2098, 400), (2072, -1000), (2070, -1000), (2075, 1000), (2143, -5000), (2148, -400), (2010, -2500), (2066, -5000), (56, 5000), (1143, -5000), (2037, -150), (2155, 150), (95, -2500), (2078, -1000), (59, -1000), (2111, 2500), (34, 2500), (12, 1000), (2061, -5000), (2006, -150), (2154, 150), (1131, -2500), (2055, -1000), (2134, 1000), (2141, -400), (3042, -400), (3086, 2500), (2152, 1000), (3003, 1000), (3119, 2500), (2145, -5000), (2012, -150), (43, 5000), (3008, 400), (2156, 150), (2038, 150), (2143, 2500), (2142, 1000), (2155, 150), (2011, -150), (2145, 1000), (3059, -2500), (2136, 1000), (3104, 1000), (51, -2500), (2026, -150), (13, 2500), (3052, 400), (2139, 2500), (2194, -150), (52, 1000), (2164, -400), (2110, 1000), (2048, 2500), (3022, 150), (2059, -2500), (2098, 400), (2195, -150), (2155, 1000), (2137, 400), (1095, -150), (2046, 1000), (2021, -150)]
-W16 = True
-EQ16 = True
+MAG, UO = 1.5 * 2 ** 23, 1023.5
 NEZ, NEO = 8, 8
-BIG = float(2 ** 24)
-MAG = 1.5 * 2 ** 23
 POP = float(32 << 17)
+CB = 129
 SL0 = 17
-F, B, I, U = "float32", "bfloat16", "int32", "uint16"
+XW = W + 64
+PAIRS = [(i, i) for i in range(4)] + [(i, j) for j in range(4) for i in range(j)]
+F, B, I, U, H = "float32", "bfloat16", "int32", "uint16", "float16"
 
 
 def _sb(n, d):
@@ -24,39 +26,30 @@ def _sb(n, d):
 
 
 SCRATCH = {
-    "xw": _sb(W + 32, B), "vw": _sb(W + L, B), "zs": _sb(26 * L, B), "yb": _sb(4096, B), "sg": _sb(4096, B), "eb": _sb(4096, B),
+    "xw": _sb(XW, B), "vw": _sb(W + L, B), "zs": _sb(26 * L, B), "yb": _sb(4096, B), "sg": _sb(4096, B), "eb": _sb(4096, B), "rb": _sb(4096, B),
     "lz": _sb(7 * L, B), "lo": _sb(7 * 16, U), "so": _sb(7 * 16, U),
     "nmi": _sb(L, I), "cr": _sb(2 * L, B), "wti": _sb(1, I), "thi": _sb(1, I),
-    "nf": _sb(L, F), "nw": _sb(2 * L, F), "crw": _sb(4 * L, B), "nb": _sb(L, F),
-    "cab": _sb(L, B), "ca32": _sb(L, B), "eca": _sb(L, B), "ert": _sb(L, B),
-    "pi": _sb(1, I), "ci": _sb(16, I), "cf": _sb(32, F), "cb": _sb(2, B),
-    "iq": _sb(144, F), "ig": _sb(128, F), "ik": _sb(L, F), "im": _sb(L, F), "iti": _sb(16, I), "t16": _sb(64, F), "t16i": _sb(16, I),
-    "idn": _sb(128, B), "nid": _sb(128, B), "bid": _sb(128, B), "swb": _sb(128, B), "swf": _sb(128, F),
-    "zhi": _sb(144, "float16" if W16 else B), "zpb": _sb(144, B), "zon": _sb(144, B), "znb": _sb(144, B),
-    "wb": _sb(128, B), "wd": _sb(128, B), "bb": _sb(128, B), "hal": _sb(128, F), "g8": _sb(8, B),
-    "msk": _sb(L, F), "thm": _sb(L, "float16"), "thr": _sb(L, B), "cneg": _sb(64, B),
-    "bct": _sb(16, U), "bcc": _sb(16, U), "pma": _sb(16, U), "pmb": _sb(16, U), "lc": _sb(16, F), "dum": _sb(16, F),
-    "p1": _sb(L, I), "p2": _sb(L, I), "p3": _sb(L, I), "o1": _sb(L, U),
-    "r1": _sb(L, F), "r2": _sb(L, F), "xx": _sb(L, F), "qq": _sb(L, F), "h1": _sb(L, I), "h2": _sb(L, I), "o2": _sb(L, U),
-    "pk": _sb(L, F), "key": _sb(L, F), "acc": _sb(L, F),
-    "c1": _sb(L, B), "c2": _sb(L, B), "c3": _sb(L, B), "ee": _sb(L, B), "gg": _sb(L, B), "lv": _sb(4 * L, B), "eru": _sb(L, B), "s1": _sb(16, F),
-    "kf": _sb(16, F), "ki": _sb(16, I), "u32": _sb(32, I), "a1": _sb(16, I), "a2": _sb(16, I), "a3": _sb(16, U),
-    "cc": _sb(16, I), "cx": _sb(16, I), "cl": _sb(16, F), "cs": _sb(32, F), "tri": _sb(32, F), "dl": _sb(16, F), "dtm": _sb(32, F),
-    "n1": _sb(16, F), "n2": _sb(16, F), "n3": _sb(16, F), "stk": _sb(2 * 128, F), "sd": _sb(96, F), "se": _sb(96, F), "np1": _sb(16, F),
-    "uf": _sb(16, F), "uq": _sb(16, F), "ph": _sb(16, I), "pl": _sb(32, I), "dt0": _sb(16, F),
-    "sgn": _sb(16, B), "cnt": _sb(1, F), "ar": _sb(1, I), "av": _sb(1, F), "kd": _sb(16, F), "npb": _sb(16, B), "pm": _sb(16, F),
-    "xd": _sb(L, "float16"), "pb": _sb(L, U if EQ16 else F), "eq": _sb(2176, B), "los": _sb(L, B), "w1": _sb(16, F), "w2": _sb(16, F),
-    "ylt": _sb(L, B), "ylo": _sb(L, B), "xp": _sb(L, B), "ypo": _sb(L, F),
+    "nw": _sb(2 * L, F), "crw": _sb(4 * L, B), "nb": _sb(L, F), "cab": _sb(L, B), "c144": _sb(L, B), "eca": _sb(L, B), "ert": _sb(L, B),
+    "pi": _sb(1, I), "ci": _sb(16, I), "cf": _sb(32, F), "co": _sb(8, F),
+    "iq": _sb(144, F), "ig": _sb(128, F), "ik": _sb(L, F), "im": _sb(L, F), "iti": _sb(16, I), "t16i": _sb(16, I),
+    "idn": _sb(128, B), "nid": _sb(128, B), "hug": _sb(128, B), "n2k": _sb(128, B), "n64": _sb(128, B), "uo": _sb(128, H), "wbb": _sb(128, B), "zpo": _sb(144, B), "sO": _sb(16, H), "zer": _sb(128, B),
+    "idf": _sb(128, F), "nif": _sb(128, F), "swb": _sb(128, B), "swf": _sb(128, F),
+    "zhi": _sb(144, H), "zhn": _sb(144, H), "zon": _sb(144, B), "zne": _sb(144, B), "wb": _sb(128, B), "hal": _sb(128, F), "g8": _sb(8, B),
+    "msk": _sb(L, B), "thm": _sb(L, H), "sk": _sb(L, H), "c16": _sb(L, H), "c129": _sb(L, B), "slc": _sb(16 * RO, B), "l16": _sb(16, B),
+    "sM": _sb(L, B), "sW": _sb(L, B), "sD": _sb(L, H), "sA": _sb(64, B), "sC": _sb(64, B), "sel": _sb(2048, B), "tg": _sb(640, B),
+    "bct": _sb(16, U), "bcc": _sb(16, U), "pma": _sb(16, U), "pmb": _sb(16, U), "rpl": _sb(8, U), "dum": _sb(16, F),
+    "p1": _sb(L, F), "rr": _sb(L, B), "o1": _sb(L, U), "r1": _sb(L, F), "xx": _sb(L, F), "qq": _sb(L, F), "rq": _sb(L, B), "h1": _sb(L, I), "h2": _sb(L, I), "o2": _sb(L, U),
+    "acc": _sb(L, F), "c1": _sb(L, B), "c2": _sb(L, B), "c3": _sb(L, B), "c4": _sb(L, B), "ee": _sb(L, B), "gg": _sb(L, B), "lv": _sb(2 * L, B),
+    "eru": _sb(L, B), "kt": _sb(128, B), "lb": _sb(80, B), "lt": _sb(128, B),
+    "kf": _sb(16, F), "ki": _sb(16, I), "u32": _sb(16, I), "uf": _sb(32, F), "a3": _sb(16, U), "stk": _sb(2 * 192, F), "sc": _sb(64, F),
+    "uq": _sb(16, F), "pl": _sb(16, I), "rep": _sb(112, H), "rpa": _sb(128, B), "g8r": _sb(128, B), "z8": _sb(144, B), "bc8": _sb(8, U),
+    "cnt": _sb(1, F), "ar": _sb(1, B), "av": _sb(1, F), "eq": _sb(640, B), "los": _sb(L, B), "w1": _sb(16, F), "w2": _sb(16, F),
 }
-ALIAS = {"xp": "c1", "ylt": "c2", "ylo": "c3", "ypo": "r1", "nf": "r2"}
-for _n in ALIAS:
-    SCRATCH.pop(_n, None)
-SCRATCH["idf"] = _sb(128, F)
-SCRATCH["pkc"] = _sb(L, F)
-PS = ["d0", "d1", "ur0", "ur1", "f0", "f1", "cst", "mi"]
+ALIAS = {"xp": "c1", "ylt": "c2", "ylo": "c3", "ypo": "qq", "nf": "acc"}
+PS = ["d0", "d1", "k0", "k1", "ff", "qb", "m1", "m2"]
 for _n in PS:
     SCRATCH[_n] = ("psum", [128, 512], F)
-DMAS = ["nm", "ca", "rt", "z0", "wt", "th", "xt", "xe", "vt", "yv", "yv2", "yz", "yl", "yp"]
+DMAS = ["nm", "ca", "rt", "z0", "wt", "th", "xt", "x2", "xe", "vt", "yv", "yv2", "yz", "yl", "yp"]
 SEMAPHORES = ["eV", "eS", "eP", "eG", "sent"] + ["m_" + n for n in DMAS] + ["az%d" % s for s in range(RO)] + ["ao%d" % s for s in range(RO)]
 CACHE = {}
 LAT = 70
@@ -64,8 +57,13 @@ GC, SC, TT = 1.56, 3.8, 2.0
 
 
 def build(g, core, T, topo, rank):
-    ops, role = [], [0]
-    two = {n: SCRATCH[n][2] in (B, U, "float16") for n in SCRATCH}
+    ops, step, group, since = [], [-1, 0, 0], {}, {}
+
+    def at(s, t):
+        step[2] = 40000 * (s + 1) + t * CFG["k1"] * (1.0 if s else CFG["k0"])
+        since.clear()
+
+    two = {n: SCRATCH[n][2] in (B, U, H) for n in SCRATCH}
 
     def a(n, c0=0, c1=None, st=1, p=128):
         n = ALIAS.get(n, n)
@@ -100,8 +98,10 @@ def build(g, core, T, topo, rank):
                 w.append(x[1]); r.append(x[2])
             else:
                 w.append(x)
-        ops.append({"e": e, "c": cost, "r": r, "w": w, "f": fn, "sem": sem, "lat": lat, "after": after, "role": role[0]})
-        role[0] += 1
+        ops.append({"e": e, "c": cost, "r": r, "w": w, "f": fn, "sem": sem, "lat": lat, "after": after, "step": step[0], "role": step[1], "h": step[2] + since.get(e, 0),
+                    "g": any(isinstance(x, tuple) and x[0] == "*" for x in rd + wr)})
+        step[1] += 1
+        since[e] = since.get(e, 0) + cost
         return len(ops) - 1
 
     def vcost(o, i, rate=None):
@@ -134,7 +134,7 @@ def build(g, core, T, topo, rank):
     def tr(o, i):
         add("V", vcost(o, i), [i], [o], lambda: g.vector.transpose(ap(o), ap(i)))
 
-    def act(o, i, f, bias=0.0, scale=1.0, acc=None):
+    def act(o, i, f=AF.Identity, bias=0.0, scale=1.0, acc=None):
         c = (80 + GC * num(o)) if i[0] == "*" else 40 + max(64, num(o))
         if acc is None:
             fn = lambda: g.scalar.activation(ap(o), ap(i), f, bias=ap(bias), scale=ap(scale))
@@ -142,20 +142,25 @@ def build(g, core, T, topo, rank):
             fn = lambda: g.scalar.activation(ap(o), ap(i), f, bias=ap(bias), scale=ap(scale), accum_out=ap(acc))
         add("S", c, [i, bias, scale], [o] + ([acc] if acc else []), fn)
 
-    def mm(items, start=True, stop=True):
+    def mm(items, start=True, each=0):
+        stop = [True]
+        if not start:
+            group[items[0][0][0]][0] = False
+        group[items[0][0][0]] = stop
+
         def fn():
             r = None
             for j, (o, l, x) in enumerate(items):
-                r = g.tensor.matmul(ap(o), ap(l), ap(x), start and j == 0, stop and j == len(items) - 1)
+                if each:
+                    r = g.tensor.matmul(ap(o), ap(l), ap(x), j % each == 0, j % each == each - 1)
+                else:
+                    r = g.tensor.matmul(ap(o), ap(l), ap(x), start and j == 0, stop[0] and j == len(items) - 1)
             return r
-        c = sum(max(64, num(x)) * (0.5 if two[x[0]] else 2.0) for o, l, x in items) + 40
-        add("P", c, [z for o, l, x in items for z in (l, x)], [o for o, l, x in items], fn)
+        c = sum(max(min(64, num(l)), num(x)) * (0.5 if two[x[0]] else 2.0) for o, l, x in items) + CFG["po"]
+        add("P", c, [z for o, l, x in items for z in (l, x)], [o for o, l, x in items], fn, lat=40 - CFG["po"])
 
     def red(o, z, src, c0, c1):
         return [(o, a(z, 15 - m, 143 - m), a(src, c0 + m, c1, 16)) for m in range(16)]
-
-    def ured(o, src, c0, c1):
-        return red(o, "zhi", src, c0, c1) + ([] if W16 else red(o, "zlo", src, c0, c1))
 
     def iota(o, pat, base=0, cm=0):
         if SCRATCH[o[0]][2] == I:
@@ -164,6 +169,9 @@ def build(g, core, T, topo, rank):
             fn = lambda: g.iota(ap(o), pat, base, cm, allow_small_or_imprecise_dtypes=True)
         add("G", 160 + 2 * num(o), [], [o], fn)
 
+    def pick(o, pat, op, fill, base, cm):
+        add("G", 205 + 2 * num(o), [o], [o], lambda: g.affine_select(ap(o), ap(o), pat, op, fill, base, cm))
+
     def dma(q, name, o, i, lat):
         eng = g.sync if q == "Y" else g.scalar
         add(q, 70, [i], [o] if isinstance(o, tuple) else [], lambda: eng.dma_start(ap(o), ap(i)), sem=("m_" + name, 16), lat=lat)
@@ -171,13 +179,14 @@ def build(g, core, T, topo, rank):
     dst = T.cores[(rank + SH) % len(T.cores)]
     src = T.cores[(rank - SH) % len(T.cores)]
     rid, pid = topo.addr(dst, core)
-    sent = [0]
+    sent = [0, None]
 
     def send(o, i, sem, ne, lat):
         en = topo.engines(core, dst)[:ne]
         m = sum(1 << e for e in en)
         sent[0] += len(en)
-        j = add("G", 600, [i], [], lambda: g.remote_dma(ap(o), ap(i), T.sem[sem], T.sem.sent, pid, rid, m), sem=("", 0))
+        j = add("G", 600, [i], [], lambda: g.remote_dma(ap(o), ap(i), T.sem[sem], T.sem.sent, pid, rid, m), sem=("", 0), after=sent[1])
+        sent[1] = j
         add("X", 0, [], [o], None, sem=(sem, len(topo.engines(src, core)[:ne])), lat=lat, after=j)
 
     def zsl(s):
@@ -189,20 +198,21 @@ def build(g, core, T, topo, rank):
     dma("Y", "nm", a("nmi"), T.nm[:], 2400)
     dma("S", "z0", zsl(SL0), T.z0[:], 2400)
     dma("Y", "wt", a("wti"), T.wt[:], 2400)
-    dma("S", "xe", a("xw", W, W + 32), T.xt[:, 0:32], 2400)
+    dma("S", "xe", a("xw", XW - 64, XW), T.xt[:, 0:64], 2400)
     dma("Y", "xt", a("xw", 0, W), T.xt[:], 4500)
     dma("S", "ca", a("cr", 0, L), T.ca[:], 2600)
     dma("S", "rt", a("cr", L, 2 * L), T.rt[:], 2600)
     dma("S", "th", a("thi"), T.th[:], 2600)
-    dma("Y", "vt", a("vw", 0, W), T.vt[:], 6000)
+    dma("Y", "vt", a("vw", 0, W), T.vt[:], 7500)
     iota(a("pi"), [[0, 1]], 0, 1)
     iota(a("iq"), [[1, 144]])
     iota(a("iti"), [[1, 16]])
+    iota(a("acc"), [[37 * 32, 16], [0, 16]])
     iota(a("ik"), [[1, 16], [0, 16]])
     iota(a("ig"), [[16, 8], [0, 16]])
     iota(a("im"), [[0, 16], [1, 16]])
     AND, SHR = ALU.bitwise_and, ALU.arith_shift_right
-    P_, M_, G_, Z_, X_, SW, TH, WH, WL, CN, PA, Y_, TB, TC = range(14)
+    P_, M_, G_, Z_, X_, SW, TH, WH, Y_, TB, TC, TD, R0 = range(13)
     cp(col("cf", P_), a("pi"))
     ts(col("ci", 0), a("pi"), 15, AND); cp(col("cf", M_), col("ci", 0))
     tt(col("cf", G_), col("cf", P_), col("cf", M_), ALU.subtract)
@@ -216,65 +226,97 @@ def build(g, core, T, topo, rank):
     ts(col("cf", TC), col("ci", 3), col("cf", X_), ALU.add, 16.0, ALU.mult)
     ts(a("pma"), a("iti"), col("cf", Y_), ALU.add, col("cf", TC), ALU.add)
     ts(a("bct"), a("iti"), 0.0, ALU.mult, col("cf", M_), ALU.add)
-    cp(a("nf"), a("nmi")); tr(a("nw", 0, L), a("nf"))
-    mm([(a("mi", 0, L), a("swf"), a("nw", 0, L))])
-    act(a("nw", L, 2 * L), a("mi", 0, L), AF.Identity)
-    cp(a("nb"), ind(a("nw"), a("pma")))
-    if W16:
-        ts(col("ci", 4), a("wti"), 2047, AND); cp(col("cf", WH), col("ci", 4))
-    else:
-        ts(col("ci", 4), a("wti"), 2040, AND); cp(col("cf", WH), col("ci", 4))
-        ts(col("ci", 5), a("wti"), 7, AND); cp(col("cf", WL), col("ci", 5))
-        ts(a("zlo"), a("iq"), col("cf", Z_), ALU.is_equal, col("cf", WL), ALU.mult)
+    ts(a("idf"), a("iq", 0, 128), col("cf", P_), ALU.is_equal)
+    for n, v in (("idn", 1.0), ("n64", -65536.0), ("nid", -1.0), ("n2k", -2048.0), ("hug", 2.0 ** 80), ("zer", 0.0)):
+        act(a(n), a("idf"), scale=v)
+    cp(a("p1"), a("nmi")); tr(a("nw", 0, L), a("p1"))
+    mm([(a("m1", 0, L), a("swf"), a("nw", 0, L))])
+    act(a("nw", L, 2 * L), a("m1", 0, L))
+    act(a("nb"), ind(a("nw"), a("pma")))
+    act(a("ff", 0, L), a("nb"), scale=32 + UO)
+    tt(a("qb", L, 2 * L), a("ff", 0, L), a("acc"), ALU.add)
+    ts(col("ci", 4), a("wti"), 2047, AND); cp(col("cf", WH), col("ci", 4))
     ts(a("zhi"), a("iq"), col("cf", Z_), ALU.is_equal, col("cf", WH), ALU.mult)
-    act(zsl(16), zsl(SL0), AF.Identity, bias=63.0, scale=-1.0)
-    mm(ured(a("ur0", 0, 32), "zs", 16 * L, 18 * L))
-    cp(a("h1", 0, 32), a("ur0", 0, 32)); ts(a("h2", 0, 32), a("h1", 0, 32), 2047, AND)
-    ts(a("u32", 0, 16), a("h2", 16, 32), 32.0, ALU.add)
-    ts(a("stk", 16, 32), a("h2", 0, 16), float((31 << 17) + 16 * 4096 + 32), ALU.add)
-    ts(a("cst", L, 2 * L), a("ik"), 1184.0, ALU.mult)
-    ts(a("idn"), a("iq", 0, 128), col("cf", P_), ALU.is_equal)
-    ts(a("nid"), a("idn"), -1.0, ALU.mult); ts(a("bid"), a("idn"), 2048.0 * BIG, ALU.mult)
-    ts(a("zon"), a("iq"), col("cf", Z_), ALU.is_equal); ts(a("znb"), a("zon"), -BIG, ALU.mult); ts(a("zpb"), a("zon"), BIG, ALU.mult)
-    ts(a("wb"), a("ig"), col("cf", G_), ALU.is_equal, 65536.0, ALU.mult)
-    ts(a("bb"), a("wb"), 256.0, ALU.mult)
-    ts(col("cf", CN), col("cf", M_), 0.0, ALU.is_equal, -2.0 ** -6, ALU.mult)
-    ts(col("cf", PA), col("cf", M_), 1.0, ALU.is_equal, 2.0 ** -17, ALU.mult)
-    ts(a("t16"), a("iq", 0, 64), 0.0, ALU.mult, col("cf", CN), ALU.add)
-    ts(a("cneg"), a("t16"), col("cf", PA), ALU.add)
+    act(zsl(16), zsl(SL0), bias=63.0, scale=-1.0)
+    mm(red(a("m2", 0, 32), "zhi", "zs", 16 * L, 18 * L))
+    cp(a("ki"), a("m2", 16, 32)); ts(a("u32"), a("ki"), 2047, AND); ts(a("uf", 0, 16), a("u32"), -UO, ALU.add)
+    cp(a("t16i"), a("m2", 0, 16)); ts(a("pl"), a("t16i"), 2047, AND)
+    ts(a("stk", 64, 80), a("pl"), (31 << 17) + 16 * 4096 - UO, ALU.add)
+    ts(a("zon"), a("iq"), col("cf", Z_), ALU.is_equal)
+    act(a("zne"), a("zon"), scale=-2.0 ** 25); act(a("zpo"), a("zon"), scale=2.0 ** 25)
+    if "A" in "".join(CFG["h1"]):
+        ts(a("zhn"), a("zhi"), -1.0, ALU.mult)
+    ts(a("uo"), a("idn"), 0.0, ALU.mult, -UO, ALU.add)
+    ts(a("wb"), a("ig"), col("cf", G_), ALU.is_equal)
+    act(a("wbb"), a("wb"), scale=2.0 ** 25)
     ts(col("cf", TH), a("thi"), 0.5, ALU.add)
     ts(a("thm"), a("ik"), col("cf", M_), ALU.is_equal, col("cf", TH), ALU.mult)
-    cp(a("swb"), a("swf"))
+    act(a("swb"), a("swf"))
     LN2 = math.log(2.0)
     for h in range(2):
         tr(a("crw", 2 * h * L, (2 * h + 1) * L), a("cr", h * L, (h + 1) * L))
-        mm([(a("mi", 0, L), a("swb"), a("crw", 2 * h * L, (2 * h + 1) * L))])
-        act(a("crw", (2 * h + 1) * L, (2 * h + 2) * L), a("mi", 0, L), AF.Identity)
-    act(a("cab"), ind(a("crw", 0, 2 * L), a("pma")), AF.Identity)
-    act(a("eca"), a("cab"), AF.Exp, bias=31 * LN2, scale=-LN2)
-    act(a("ert"), ind(a("crw", 2 * L, 4 * L), a("pma")), AF.Exp, bias=31 * LN2, scale=-LN2)
-    act(col("cb", 0), col("cf", M_), AF.Exp, bias=-1 * LN2, scale=-LN2)
-    act(a("thr"), a("im"), AF.Exp, bias=16 * LN2, scale=-LN2)
-    ts(a("ca32"), a("cab"), 32.0, ALU.add)
-    ts(a("acc"), a("ik"), 4096.0, ALU.mult, 1055.5, ALU.add)
-    act(a("key"), a("cab"), AF.Identity, scale=float(1 << 17))
-    tt(a("pkc"), a("key"), a("acc"), ALU.add)
-    ts(a("idf"), a("iq", 0, 128), col("cf", P_), ALU.is_equal)
-    ts(a("wd"), a("wb"), col("cb", 0), ALU.mult)
+        mm([(a("m2", 0, L), a("swb"), a("crw", 2 * h * L, (2 * h + 1) * L))])
+        act(a("crw", (2 * h + 1) * L, (2 * h + 2) * L), a("m2", 0, L))
+    act(a("cab"), ind(a("crw", 0, 2 * L), a("pma")))
+    act(a("eca"), a("cab"), AF.Exp, bias=75 * LN2, scale=-2 * LN2)
+    act(a("ert"), ind(a("crw", 2 * L, 4 * L), a("pma")), AF.Exp, bias=74 * LN2, scale=-2 * LN2)
+    act(a("c144"), a("cab"), bias=CB + 16.0)
+    act(a("c4"), a("ik"), scale=1.0 / 32)
+    mm([(a("m2", 0, L), a("idn"), a("cab")), (a("m2", 0, L), a("idn"), a("c4"))])
+    ts(a("sk"), a("m2", 0, L), -64.0, ALU.mult)
     ts(a("msk"), a("im"), col("cf", M_), ALU.is_equal)
     cp(a("bcc"), a("iti"))
-    ts(a("lc"), a("iti"), 16.0, ALU.mult, col("cf", M_), ALU.add); ts(a("dum"), a("lc"), float(W), ALU.add)
-    ms(a("hal"), 0.5); ms(a("vw", W, W + L), 0.0); ms(a("cs", 0, 16), 0.0); ms(a("tri", 0, 16), 0.25)
-    ms(a("dtm", 0, 16), 19616.0 - 592.0 ** 2)
-    ms(a("stk", 32, 128), 0.0); ms(a("stk", 144, 256), 0.0)
+    ts(a("w1"), a("iti"), 16.0, ALU.mult, col("cf", M_), ALU.add)
+    act(a("l16"), a("w1"), scale=16.0); act(a("dum"), a("w1"), bias=float(W - 4096))
+    for o, n, v in ((a("hal"), 128, None), (a("vw", W, W + L), L, 0), (a("lb", 48, 64), 16, 0), (a("lb", 64, 80), 16, 1),
+                    (a("stk", 0, 64), 64, 0), (a("stk", 192, 256), 64, 0), (a("stk", 80, 192), 112, 1 << 23), (a("stk", 272, 384), 112, 1 << 23)):
+        if v is None:
+            act(o, a("idf"), bias=0.5, scale=0.0)
+        else:
+            iota(o, [[0, n]], v)
+    iota(a("slc"), [[4096, RO], [0, 16]], SL0 * 4096)
+    iota(a("co"), [[0, 8]])
+    B2 = 2.0 ** 21
+    for j, cs in enumerate(([1, -16], [0, 0.5, 0, 1, 0.5], [0, 0, 0, 19616, (19616 - 592 ** 2) % 65536], [2 ** 17, -3 * B2, 2 * B2, 0, -(CB + 48) * 2 ** 17], [0, -4 * B2, 0, 0, -4 * B2], [0, 4 * B2, 0, 0, -4 * B2],
+                            [0, 0, 0, 19616, -592 ** 2 % 65536])):
+        for q in range(len(cs) - 1, -1, -1):
+            if q == len(cs) - 1 or cs[q] != cs[q + 1]:
+                pick(col("co", j), [[0, 1]], ALU.is_ge, float(cs[q]), -16 * (q + 1), 1)
+    act(a("sM"), a("msk"), scale=col("co", 0)); act(a("sW"), a("msk"), scale=col("co", 1)); ts(a("sD"), a("msk"), col("co", 2), ALU.mult)
+    act(a("sA", 48, 64), a("msk", 0, 16), scale=col("co", 3)); act(a("sA", 0, 48), a("msk", 0, 48), scale=col("co", 4))
+    act(a("sC"), a("msk", 0, 64), scale=col("co", 5)); ts(a("sO"), a("msk", 0, 16), col("co", 6), ALU.mult)
+    ts(a("uq"), a("iti"), col("cf", M_), ALU.is_equal, -1.0, ALU.mult)
+    for m in range(16):
+        act(a("sel", 128 * m, 128 * m + 128), a("wb"), scale=col("uq", m))
+    iota(a("g8r"), [[0, 16], [16, 8]])
+    ts(a("g8r"), a("g8r"), col("cf", G_), ALU.not_equal, 3 * POP, ALU.mult)
+    act(a("g8r"), a("g8r"), bias=POP)
+    iota(a("z8"), [[0, 144]])
+    pick(a("z8"), [[1, 144]], ALU.not_equal, 1.0, -15, -16)
+    iota(a("c2", 0, 128), [[1, 16], [0, 8]])
+    mm(red(a("k0", 0, 8), "zon", "c2", 0, 128))
+    ts(a("bc8"), a("k0", 0, 8), 1.0 / 16, ALU.mult)
+    iota(a("eq"), [[1, 16], [0, 40]])
+    pick(a("eq"), [[0, 64], [-1, 10]], ALU.is_ge, 99.0, 3, 0)
+    ts(a("tg"), a("eq"), col("cf", M_), ALU.is_le, 0.5, ALU.mult)
+    iota(a("los", 0, 112), [[0, 112]])
+    for h, side in ((0, 0), (48, 1)):
+        for p in range(10):
+            iota(a("los", h + p, h + 40, 10), [[4, 4]], PAIRS[p][side])
+    iota(a("los", 96, 112), [[1, 16]])
+    mm(red(a("k1", 0, 7), "zon", "los", 0, 112))
+    ts(a("rpl", 0, 7), a("k1", 0, 7), 1.0 / 16, ALU.mult)
     ts(a("t16i"), a("iti"), 1, AND)
     ts(a("w1"), a("t16i"), col("cf", X_), ALU.not_equal, 256.0, ALU.mult)
-    ts(a("a1"), a("iti"), 14, AND); tt(a("w2"), a("w1"), a("a1"), ALU.add)
-    ts(col("cf", TC + 1), col("cf", M_), 16.0, ALU.mult, col("cf", X_), ALU.add)
-    ts(a("pmb"), a("w2"), col("cf", TC + 1), ALU.add)
+    ts(a("t16i"), a("iti"), 14, AND); tt(a("w2"), a("w1"), a("t16i"), ALU.add)
+    ts(col("cf", TD), col("cf", M_), 16.0, ALU.mult, col("cf", X_), ALU.add)
+    ts(a("pmb"), a("w2"), col("cf", TD), ALU.add)
     ts(a("g8"), a("ig", 0, 128, 16), col("cf", G_), ALU.is_equal)
 
     blk = [0]
+    cb, sgn, dlt, dep = [a("lb", 16 * q, 16 * q + 16) for q in range(4)]
+    lt = a("lt", p=80)
+    QC = 3.0 - 592.0 ** 2
 
     def chunks(text):
         r, k = [], 0
@@ -285,54 +327,59 @@ def build(g, core, T, topo, rank):
         return r
 
     def columns(s):
-        c0, first = 0, None
+        c0 = 0
         for nk in CFG["oc"]:
             c1 = c0 + 16 * nk
-            tt(a("p1", c0, c1), ind(a("u32", 16 * (s % 2), 16 * (s % 2) + 16), a("bct", 0, nk)), a("nb", c0, c1), ALU.mult)
-            tt(a("p2", c0, c1), a("p1", c0, c1), a("cst", L + c0, L + c1), ALU.add)
-            ts(a("p3", c0, c1), a("p2", c0, c1), 5, SHR, 2047, AND)
+            at(s, 900 if c0 else 300)
+            tt(a("p1", c0, c1), ind(a("uf", 16 * (s % 2), 16 * (s % 2) + 16), a("bct", 0, nk)), a("nb", c0, c1), ALU.mult)
+            tt(a("h1", c0, c1), a("qb", L + c0, L + c1), a("p1", c0, c1), ALU.add)
+            ts(a("h2", c0, c1), a("h1", c0, c1), 5, SHR, 2047, AND)
             if s >= 2:
-                ts(a("o1", c0, c1), a("p3", c0, c1), a("av"), ALU.add)
+                ts(a("o1", c0, c1), a("h2", c0, c1), a("av"), ALU.add, 6144.0, ALU.add)
             else:
-                cp(a("o1", c0, c1), a("p3", c0, c1))
+                cp(a("o1", c0, c1), a("h2", c0, c1))
             c0 = c1
-            first = len(ops) - 1 if first is None else first
-        return first
 
     for s in range(RO):
+        step[0] = s
         pa, pb_ = s % 2, (s + 1) % 2
         z = zsl(SL0 + s)
-        u32, dtm, lv = a("u32", 16 * pa, 16 * pa + 16), a("dtm", 16 * pa, 16 * pa + 16), a("lv", 2 * pa * L, (2 * pa + 1) * L)
         last = s == RO - 1
         kind = 0 if s == 0 else 2 if last else 1
-        role[0] = 1000 * (kind + 1)
+        step[1] = 1000 * (kind + 1)
         h1, h2 = chunks(CFG["h1"][kind]), chunks(CFG["h2"][kind])
         if s == 0:
             columns(0)
         else:
             send(a("lz", (s - 1) * L, s * L), z, "az%d" % s, NEZ, 3000)
-        if s == 0:
-            mm([(a("f1", L, L + 16), a("idn"), a("ert", 16 * k, 16 * k + 16)) for k in range(16)])
-        else:
-            mm([(a("f1", 0, L), a("bid"), lv), (a("f1", 0, L), a("nid"), a("ert"))])
-            act(a("eru"), a("f1", 0, L), AF.Relu, scale=-1.0)
-            mm([(a("f1", L, L + 16), a("idn"), a("eru", 16 * k, 16 * k + 16)) for k in range(16)])
-        act(a("s1"), a("f1", L, L + 16), AF.Identity)
-        tt(a("c1"), ind(a("s1"), a("bct")), a("eca"), ALU.is_ge)
+        lv, eru = a("lv", 0, L), "ert"
+        at(s, CFG["tb"][2])
         if s >= 1:
-            tt(a("c2"), ind(a("cc"), a("bct")), a("ca32"), ALU.is_ge)
-            pl = a("pl", 16 * pa, 16 * pa + 16)
-            cp(a("uf"), u32); act(a("uq"), a("uf"), AF.Square, bias=560.0)
-            act(a("dt0"), dtm, AF.Identity, bias=-19616.0)
-            tt(a("ph"), a("uq"), a("dt0"), ALU.add); ts(pl, a("ph"), 5, SHR, 2047, AND)
-        def pens(c0, c1):
-            return [a("c1", c0, c1), a("c3", c0, c1)] + ([a("c2", c0, c1), a("lv", lv[1] + c0, lv[1] + c1)] if s else [])
+            mm([(a("m1", 0, L), a("hug"), lv), (a("m1", 0, L), a("nid"), a("ert"))])
+            act(a("eru"), a("m1", 0, L), AF.Relu, scale=-1.0)
+            eru = "eru"
+        mm([(a("m1", 0, 128), a(eru, 128 * h, 128 * h + 128), a("idn")) for h in range(2)])
+        act(a("kt"), a("m1", 0, 128))
+        mm([(a("m1", 0, L), a("kt"), a("msk")), (a("m1", 0, L), a("nid"), a("eca"))])
+        act(a("c1"), a("m1", 0, L), AF.Relu, scale=2.0 ** 25)
+        if s >= 1:
+            at(s, CFG["tb"][3])
+            act(a("uq"), a("uf", 16 * pa, 16 * pa + 16), AF.Square, bias=592 + UO)
+            mm([(a("qb", 0, 16), lt, a("sO", p=80))])
+            tt(a("ci"), a("qb", 0, 16), a("uq"), ALU.add)
+            mm([(a("qb", 0, L), lt, a("sD", p=80))])
+            at(s, CFG["tb"][5])
+            ts(a("pl"), a("ci"), 5, SHR, 2047, AND)
+            cp(a("rep"), ind(a("pl"), a("rpl", 0, 7)))
+        kept, least, turn = {}, [0], [0, 0]
 
-        pk0 = 0
-        for c, pieces in enumerate(h1):
+        def first(c):
+            pieces = h1[c]
             for md, k0, k1 in pieces:
+                zk, y = a("zs", k0 * L, k1 * L), a("yb", k0 * L, k1 * L)
+                at(s, CFG["tx"][turn[0]]); turn[0] += 1
                 if md == "S":
-                    act(a("yb", k0 * L, k1 * L), ind(a("xw"), a("o1", 16 * k0, 16 * k1)), AF.Identity)
+                    act(y, ind(a("xw"), a("o1", 16 * k0, 16 * k1)))
                     for k in range(k0, k1, 2):
                         d = "d%d" % (blk[0] % 2); blk[0] += 1
                         n = min(2, k1 - k)
@@ -340,161 +387,211 @@ def build(g, core, T, topo, rank):
                         act(a("zs", k * L, (k + n) * L), a(d, 0, n * L), AF.Abs)
                         act(a("sg", k * L, (k + n) * L), a(d, 0, n * L), AF.Sign, bias=0.5)
                 else:
+                    dd = "zs" if md == "A" else "yb"
                     for k in range(k0, k1):
-                        tt(a("yb", k * L, (k + 1) * L), ind(a("xw"), a("o1", 16 * k, 16 * k + 16)), z, ALU.subtract)
-                    act(a("zs", k0 * L, k1 * L), a("yb", k0 * L, k1 * L), AF.Abs)
-                    if md == "V":
-                        ts(a("sg", k0 * L, k1 * L), a("yb", k0 * L, k1 * L), 0.0, ALU.is_ge, -0.5, ALU.add)
+                        tt(a(dd, k * L, (k + 1) * L), ind(a("xw"), a("o1", 16 * k, 16 * k + 16)), z, ALU.subtract)
+                    d = a(dd, k0 * L, k1 * L)
+                    if md == "A":
+                        ts(y, d, 0.0, ALU.max, 2.0, ALU.mult)
                     else:
-                        act(a("sg", k0 * L, k1 * L), a("yb", k0 * L, k1 * L), AF.Sign, bias=0.5)
+                        act(zk, d, AF.Abs)
             k0, k1 = pieces[0][1], pieces[-1][2]
-            c0, c1, w = 16 * k0, 16 * k1, 16 * (k1 - k0)
-            ur = "ur%d" % (c % 2)
-            mm([(a(ur, 0, w), a("wb"), a("cneg", 0, w))] + ured(a(ur, 0, w), "zs", k0 * L, k1 * L))
-            act(a("r1", c0, c1), a(ur, 0, w), AF.Identity, bias=MAG, scale=2.0 ** -11)
-            act(a("r2", c0, c1), a("r1", c0, c1), AF.Identity, bias=2048.0 * MAG, scale=-2048.0)
-            tt(a("xx", c0, c1), a(ur, 0, w), a("r2", c0, c1), ALU.add)
-            act(a("qq", c0, c1), a("xx", c0, c1), AF.Square, bias=1615.5)
-            mm(red(a("f0", c0, c1), "zon", "sg", k0 * L, k1 * L))
-            if c in CFG["pg"]:
-                act(a("c3", pk0, c1), a("f0", pk0, c1), AF.Relu, scale=-1.0)
-                mm([(a("cst", pk0, c1), a("idf"), a("pkc", pk0, c1))] + [(a("cst", pk0, c1), a("bid"), x) for x in pens(pk0, c1)])
-                tt(a("pk", pk0, c1), a("xx", pk0, c1), a("cst", pk0, c1), ALU.add)
-                pk0 = c1
-            tt(a("h1", c0, c1), ind(dtm, a("bct", 0, w // 16)), a("qq", c0, c1), ALU.add)
-            ts(a("h2", c0, c1), a("h1", c0, c1), 5, SHR, 2047, AND)
-            cp(a("o2", c0, c1), a("h2", c0, c1))
-        if s >= 1:
-            tt(a("xd"), ind(pl, a("bcc")), a("msk"), ALU.mult)
-            mm([(a("mi", 0, L), a("wb"), a("xd"))])
-            ts(a("pb"), a("mi", 0, L), 2.0 ** -16, ALU.mult)
-        top = a("stk", 128 * pa + 16, 128 * pa + 32)
-        cur, off = None, 0
-        for c, pieces in enumerate(h2):
+            c0, c1 = 16 * k0, 16 * k1
+            kb = "k%d" % (c % 2)
+            for k in range(k0, k1):
+                kept[k] = md == "A"
+            u, r, xx = a(kb, c0, c1), a("r1", c0, c1), a("xx", c0, c1)
+            it = [(u, a("idn"), a("uo", 0, c1 - c0))]
+            if md == "A":
+                mm(it + red(u, "zhn", "zs", k0 * L, k1 * L))
+                mm(red(u, "zhi", "yb", k0 * L, k1 * L), start=False)
+            else:
+                mm(it + red(u, "zhi", "zs", k0 * L, k1 * L))
+            if CFG["uv"][c] == "V":
+                ts(r, u, MAG * 2048, ALU.add, -MAG * 2048, ALU.add)
+            else:
+                act(r, u, bias=MAG * 2048)
+                act(r, r, bias=-MAG * 2048)
+            tt(xx, u, r, ALU.subtract)
+            act(a("qq", c0, c1), xx, AF.Square, bias=592 + UO)
+            if s:
+                tt(a("h1", c0, c1), a("qb", c0, c1), a("qq", c0, c1), ALU.add)
+            else:
+                ts(a("h1", c0, c1), a("qq", c0, c1), 19616.0 - 592 ** 2, ALU.add)
+            ts(a("h2", c0, c1), a("h1", c0, c1), 5, SHR, 2047, AND); cp(a("o2", c0, c1), a("h2", c0, c1))
+
+        def third(c):
+            k0, k1 = h1[c][0][1], h1[c][-1][2]
+            at(s, CFG["tr"][c])
+            for md, j0, j1 in h1[c]:
+                if md in "AB":
+                    ts(a("sg", j0 * L, j1 * L), a("zs" if md == "A" else "yb", j0 * L, j1 * L), 0.0, ALU.is_ge, -0.5, ALU.add)
+                elif md == "T":
+                    act(a("sg", j0 * L, j1 * L), a("yb", j0 * L, j1 * L), AF.Sign, bias=0.5)
+            rows = a(CFG["rb"][c], L + 16 * k0, L + 16 * k1)
+            mm(red(rows, "zon", "sg", k0 * L, k1 * L))
+            act(a("c3", 16 * k0, 16 * k1), rows, AF.Relu, scale=-2.0 ** 38)
+
+        def second(c):
+            pieces, more = h2[c], []
             for md, k0, k1 in pieces:
                 e = a("eb", k0 * L, k1 * L)
+                at(s, CFG["tv"][turn[1]]); turn[1] += 1
                 v = ind(a("vw", 0, W), a("o2", 16 * k0, 16 * k1))
                 if md == "S":
-                    act(e, v, AF.Identity)
+                    act(e, v)
                     for k in range(k0, k1, 2):
                         d = "d%d" % (blk[0] % 2); blk[0] += 1
-                        n = min(2, k1 - k) * L
-                        mm([(a(d, 0, n), a("idn"), a("eb", k * L, k * L + n)), (a(d, 0, n), a("nid"), a("zs", k * L, k * L + n))])
-                        act(a("eb", k * L, k * L + n), a(d, 0, n), AF.Abs)
-                else:
+                        x0, x1 = k * L, min(k + 2, k1) * L
+                        o = a(d, 0, x1 - x0)
+                        if kept[k]:
+                            mm([(o, a("idn"), a("zs", x0, x1)), (o, a("nid"), a("yb", x0, x1)), (o, a("idn"), a("eb", x0, x1))])
+                        else:
+                            mm([(o, a("nid"), a("zs", x0, x1)), (o, a("idn"), a("eb", x0, x1))])
+                        act(a("eb", x0, x1), o, AF.Abs)
+                elif md == "V":
                     tt(e, v, a("zs", k0 * L, k1 * L), ALU.subtract)
-                    if md == "V":
-                        act(e, e, AF.Abs)
-                    else:
-                        ts(a("yb", k0 * L, k1 * L), e, 0.0, ALU.max, 2.0, ALU.mult)
+                    act(e, e, AF.Abs)
+                else:
+                    tt(a("rb", k0 * L, k1 * L), v, a("zs", k0 * L, k1 * L), ALU.subtract)
+                    ts(e, a("rb", k0 * L, k1 * L), 0.0, ALU.max, 2.0, ALU.mult)
+                    more += red(a(CFG["fk"][c], 16 * k0, 16 * k1), "zpo", "rb", k0 * L, k1 * L)
             k0, k1 = pieces[0][1], pieces[-1][2]
             c0, c1, w = 16 * k0, 16 * k1, 16 * (k1 - k0)
-            f = a("f%d" % ((c + 1) % 2), 0, w)
-            if md == "R":
-                mm([(f, a("bb"), a("thm", c0, c1))] + red(f, "zpb", "eb", k0 * L, k1 * L), stop=False)
-                mm(red(f, "znb", "yb", k0 * L, k1 * L), start=False)
+            f = a(CFG["fk"][c], c0, c1)
+            bars = [("idf", "xx"), ("n2k", "sk"), ("idn", "c1"), ("idn", "c3")] + ([("idn", "c2"), ("hug", "lv")] if s else [])
+            mm([(f, a("wbb"), a("thm", c0, c1))] + more)
+            mm(red(f, "zne", "eb", k0 * L, k1 * L), start=False)
+            key = a(CFG["kb"][c], c0, c1)
+            if CFG["kv"][c] == "D":
+                act(a("c4", c0, c1), f, AF.Relu)
+                mm([(key, a(x), a(y, c0, c1)) for x, y in bars])
+                mm([(key, a("idn"), a("c4", c0, c1))], start=False)
             else:
-                mm([(f, a("bb"), a("thm", c0, c1))] + red(f, "znb", "eb", k0 * L, k1 * L))
-            key = a("key", c0, c1)
-            tt(key, f, a("pk", c0, c1), ALU.max)
-            if cur is None:
-                tt(a("key", 0, 16), a("key", 0, 16), top, ALU.min)
-                cur = key
-            else:
-                nx = a("kf") if w == 16 and c + 1 == len(h2) else a("acc", off, off + w)
-                off += w
-                tt(nx, cur, key, ALU.min)
-                cur = nx
-            wn = 16 * (h2[c + 1][-1][2] - h2[c + 1][0][1]) if c + 1 < len(h2) else 16
-            while num(cur) > wn:
-                h = num(cur) // 2
-                nx = a("kf") if h == 16 and c + 1 == len(h2) else a("acc", off, off + h)
-                off += h
-                tt(nx, a(cur[0], cur[1], cur[1] + h), a(cur[0], cur[1] + h, cur[2]), ALU.min)
-                cur = nx
-        cp(a("ki"), a("kf"))
-        if s >= 1:
-            if not last:
-                act(a("sgn"), a("kf"), AF.Sign, bias=-POP, acc=a("cnt"))
-                mm([(a("mi", 300, 301), a("hal"), a("cnt"))])
-            act(a("kd"), a("kf"), AF.Identity, bias=-POP)
-            act(a("npb"), a("kf"), AF.Relu, bias=POP, scale=-1.0)
+                mm([(key, a(x), a(y, c0, c1)) for x, y in bars])
+                act(a("r1", c0, c1), key)
+                key = a("xx", c0, c1)
+                tt(key, f, a("r1", c0, c1), ALU.max)
+            end = c + 1 == len(h2)
+            tt(a("kf") if end and w == 16 else a("acc", 0, w), key, a("acc", 0, w) if c else a("stk", 192 * pa + 64, 192 * pa + 64 + w), ALU.min)
+            n = least[0] = max(w, least[0])
+            wn = 16 if end else 16 * (h2[-1][-1][2] - h2[-1][0][1]) if c + 2 == len(h2) else n
+            while n > wn:
+                h = min(n - wn, n // 32 * 16)
+                tt(a("kf") if end and n == 32 else a("acc", 0, h), a("acc", 0, h), a("acc", n - h, n), ALU.min)
+                n -= h
+            least[0] = n
+
+        def fourth(c):
+            if s == 0:
+                return
+            at(s, CFG["td"][1])
+            for h in range(2):
+                it = []
+                for m in range(8):
+                    o = a(CFG["eb"][h], 40 * m, 40 * m + 40)
+                    it += [(o, a("sel", 128 * (8 * h + m), 128 * (8 * h + m + 1)), a("rep", 48, 88)), (o, a("idn"), a("rep", 0, 40))]
+                mm(it, each=2)
+                at(s, CFG["td"][4 + h])
+                tt(a("eq", 320 * h, 320 * h + 320), a(CFG["eb"][h], 0, 320), a("tg", 320 * h, 320 * h + 320), ALU.is_equal)
+                at(s, CFG["td"][1])
+
+        done = {"X": 0, "R": 0, "V": 0, "E": 0}
+        for x in CFG["ord"][kind]:
+            {"X": first, "R": third, "V": second, "E": fourth}[x](done[x])
+            done[x] += 1
+        if s:
+            mm([(a("k0", 0, L, 1, 8), a("zer", 0, 8), a("msk"))])
+        at(s + 1, 0)
+        un = a("uf", 16 * pb_, 16 * pb_ + 16)
+        ts(a("w2"), a("kf"), MAG * 4096, ALU.add, -MAG * 4096, ALU.add)
+        tt(un, a("kf"), a("w2"), ALU.subtract)
+        count = s >= 1 and not last
+        act(sgn, a("kf"), AF.Sign, bias=0.5 - POP, acc=a("cnt") if count else None)
+        act(cb, a("kf"), bias=CB - 0.5 + 1.0 / 16, scale=2.0 ** -17)
+        if count:
+            mm([(a("ff", 300, 301), a("hal"), a("cnt"))])
+            act(a("ar"), a("ff", 300, 301), bias=191.5 + 1.0 / 64, scale=1.0 / 32)
+            ts(a("av"), a("ar"), -32.0, ALU.mult, a("ff", 300, 301), ALU.add)
         if not last:
-            ts(a("u32", 16 * pb_, 16 * pb_ + 16), a("ki"), 4095, AND)
-            if s >= 1:
-                ts(a("ar"), a("mi", 300, 301), 1.0 / 32, ALU.mult, -31.0 / 64, ALU.add)
-                ts(a("av"), a("ar"), -32.0, ALU.mult, a("mi", 300, 301), ALU.add)
-            lead = columns(s + 1)
-        ts(a("a1"), a("ki"), 4, SHR, 31 << 8, AND); tt(a("a2"), a("a1"), a("lc"), ALU.add); cp(a("a3"), a("a2"))
-        cp(zsl(SL0 + s + 1), ind(a("zs", 0, (SL0 + s + 1) * L), a("a3")))
-        ts(a("cc"), a("ki"), 17, SHR); ts(a("cx"), a("ki"), 17, SHR, 31, AND)
-        ts(a("cl"), a("cc"), 30.0, ALU.max, 32.0, ALU.min)
-        cs, tri = a("cs", 16 * pb_, 16 * pb_ + 16), a("tri", 16 * pb_, 16 * pb_ + 16)
-        tt(cs, a("cs", 16 * pa, 16 * pa + 16), a("cl"), ALU.add)
-        act(tri, cs, AF.Square, bias=31.0 * (s + 1) + 0.5, scale=-1.0)
-        tt(a("dl"), tri, a("tri", 16 * pa, 16 * pa + 16), ALU.subtract)
-        tt(a("ee"), ind(a("cx"), a("bct")), a("cab"), ALU.is_equal)
-        tt(a("gg"), ind(a("dl"), a("bct")), a("ee"), ALU.mult)
-        if s == 0:
-            cp(a("lv", 2 * pb_ * L, (2 * pb_ + 1) * L), a("gg"))
+            columns(s + 1)
+        at(s + 1, 0)
+        o = a("m1", 0, 16)
+        mm([(o, a("idn"), a("l16")), (o, a("idf"), a("w2")), (o, a("n64"), cb), (o, a("n64"), cb)])
+        ts(a("a3"), o, 1.0 / 16, ALU.mult, CB * 8192.0, ALU.add)
+        if CFG["zv"] == "S":
+            act(zsl(SL0 + s + 1), ind(a("zs", 0, (SL0 + s + 1) * L), a("a3")), AF.Abs)
         else:
-            mm([(a("f1", 0, L), a("idn"), lv), (a("f1", 0, L), a("idn"), a("gg"))])
-            act(a("lv", 2 * pb_ * L, (2 * pb_ + 1) * L), a("f1", 0, L), AF.Identity)
-        if not last:
-            act(a("dtm", 16 * pb_, 16 * pb_ + 16), cs, AF.Identity, bias=19616.0 * (31 * (s + 1) + 1) - 592.0 ** 2, scale=-19616.0)
-            nl = 16 * min(s + 2, RO - 1 - s)
-            b0, b1 = 128 * pa, 128 * pb_
-            act(a("n1"), a("cl"), AF.Identity, bias=float(31 * 2 ** 22 + (SL0 + s) * 4096), scale=-float(2 ** 22))
-            act(a("np1"), a("cl"), AF.Sign, bias=32.0, scale=-1.0)
-            ts(a("n3"), a("cc"), float(1 << 17), ALU.mult)
-            tt(a("n2"), a("n3"), u32, ALU.add); tt(a("stk", b0, b0 + 16), a("n2"), a("n1"), ALU.add)
-            tt(a("sd", 0, nl), a("stk", b0, b0 + nl), a("stk", b0 + 32, b0 + 32 + nl), ALU.subtract)
-            tt(a("se", 0, nl), ind(a("np1"), a("bct", 0, nl // 16)), a("sd", 0, nl), ALU.mult)
-            tt(a("stk", b1 + 16, b1 + 16 + nl), a("se", 0, nl), a("stk", b0 + 32, b0 + 32 + nl), ALU.add)
+            cp(zsl(SL0 + s + 1), ind(a("zs", 0, (SL0 + s + 1) * L), a("a3")))
         if s >= 1:
-            tt(a("pm"), pl, a("kd"), ALU.min)
-            if not last and CFG["lead"]:
-                ops[-1]["after"] = lead
-            mm([(a("mi", 0, L), a("nid"), a("thr"))], stop=False)
-            o = 0
-            for t in range(16):
-                n = L - 16 * t
-                ts(a("eq", o, o + n), a("pb", 16 * t, L), col("pm", t), ALU.is_equal)
-                it = [(a("mi", 16 * t, 16 * t + 16), a("wd"), a("eq", o, o + 16))]
-                if t < 15:
-                    it.append((a("mi", 16 * t + 16, L), a("wb"), a("eq", o + 16, o + n)))
-                mm(it, start=False, stop=t == 15)
-                o += n
-            act(a("los"), a("mi", 0, L), AF.Relu, bias=256.0, scale=256.0)
-            mm([(a("mi", L, L + 16), a("idn"), a("npb"))] + red(a("mi", L, L + 16), "zon", "los", 0, L))
-            tt(a("w1"), a("mi", L, L + 16), pl, ALU.max); tt(a("w2"), a("w1"), a("dum"), ALU.min)
+            at(s + 1, CFG["td"][0])
+            tt(a("rpa"), ind(a("kf"), a("bc8")), a("g8r"), ALU.is_ge)
+            mm([(a("k0", 4 * b + PAIRS[p][1], L, 16, 8), a("rpa", 8 * (4 * b + PAIRS[p][0]), 8 * (4 * b + PAIRS[p][0] + 1)), a("eq", 10 * b + p, 640, 40))
+                for b in range(4) for p in range(10)], start=False)
+            act(a("los", p=8), a("k0", 0, L, 1, 8), scale=4096.0)
+            o = a("k1", 0, 16)
+            mm([(o, a("idn"), a("rep", 96, 112)), (o, a("n2k"), sgn), (o, a("n2k"), sgn)])
+            mm([(o, a("z8", 15 - m, 143 - m, 1, 8), a("los", 16 * m, 16 * m + 16, 1, 8)) for m in range(16)], start=False)
+            tt(a("w1"), o, a("dum"), ALU.min)
             so = a("so", 16 * (s - 1), 16 * s)
-            cp(so, a("w2"))
+            ts(so, a("w1"), 4096.0, ALU.add)
             send(a("lo", 16 * (s - 1), 16 * s), so, "ao%d" % s, NEO, CFG["xl"])
-            cp(ind(a("vw"), so), z)
-            cp(ind(a("vw"), a("lo", 16 * (s - 1), 16 * s)), a("lz", (s - 1) * L, s * L))
+            for n, zz, z0 in (("so", "zs", (SL0 + s) * L), ("lo", "lz", (s - 1) * L)):
+                at(s + 1, CFG["td"][2 if n == "so" else 3])
+                for b in range(3, -1, -1):
+                    cp(ind(a("vw"), a(n, 16 * (s - 1) + 4 * b, 16 * (s - 1) + 4 * b + 4)), a(zz, z0 + 64 * b, z0 + 64 * b + 64))
+        at(s + 1, CFG["tb"][0])
+        act(dlt, cb, AF.Sign, bias=CB + 31.0, scale=-1.0)
+        tt(dep, dep, dlt, ALU.add)
+        mm([(a("m1", 0, 128, p=80), a("lb"), a("idn"))])
+        act(lt, a("m1", 0, 128, p=80))
+        at(s + 1, CFG["tb"][1])
+        mm([(a("m1", 0, L), lt, a("sM", p=80))])
+        tt(a("ee"), a("m1", 0, L), a("c144"), ALU.is_equal)
+        mm([(a("m1", 0, L), lt, a("sW", p=80))])
+        if s == 0:
+            tt(lv, a("m1", 0, L), a("ee"), ALU.mult)
+        else:
+            tt(a("gg"), a("m1", 0, L), a("ee"), ALU.mult)
+            mm([(a("m1", 0, L), a("idn"), lv), (a("m1", 0, L), a("nid"), a("gg"))])
+            act(lv, a("m1", 0, L), AF.Abs)
+        if not last:
+            at(s + 1, CFG["tb"][4])
+            mm([(a("m2", 0, L), a("lt", p=16), a("msk", p=16)), (a("m2", 0, L), a("nid"), a("cab"))])
+            act(a("c2"), a("m2", 0, L), AF.Relu, bias=-(CB + 31.5) * 2.0 ** 37, scale=2.0 ** 37)
+            nl = 16 * min(s + 2, RO - 1 - s)
+            b0, b1 = 192 * pa, 192 * pb_
+            o = a("m2", 0, nl)
+            mm([(o, lt, a("sC", 0, nl, p=80)), (o, a("idf"), a("stk", b0 + 64 - nl, b0 + 64))])
+            act(a("sc", 0, nl), o)
+            top = a("m2", nl - 16, nl)
+            mm([(o, lt, a("sA", 64 - nl, 64, p=80)), (top, a("idn"), a("slc", 16 * s, 16 * s + 16)), (top, a("idf"), a("uf", 16 * pa, 16 * pa + 16))]
+               + ([(a("m2", 0, nl - 16), a("idf"), a("stk", b0 + 96 - nl, b0 + 80))] if nl > 16 else []))
+            tt(a("stk", b1 + 80 - nl, b1 + 80), o, a("sc", 0, nl), ALU.max)
+    step[0] = RO
     dma("Y", "yz", T.yz[:], zsl(SL0 + RO), 2400)
-    mm([(a("ur0", 0, L), a("swb"), a("lv", 0, L))])
-    act(a("lv", L, 2 * L), a("ur0", 0, L), AF.Identity)
-    act(a("ylt"), ind(a("lv", 0, 2 * L), a("pmb")), AF.Identity, scale=0.5)
+    mm([(a("d0", 0, L), a("swb"), a("lv", 0, L))])
+    act(a("lv", L, 2 * L), a("d0", 0, L))
+    act(a("ylt"), ind(a("lv"), a("pmb")))
     tr(a("ylo"), a("ylt"))
     dma("Y", "yl", T.yl[:], a("ylo"), 2400)
-    tt(a("xp"), ind(a("cc"), a("bcc")), a("msk"), ALU.mult)
-    mm([(a("ur1", 0, L, 1, 8), a("g8"), a("xp"))])
-    ts(a("ypo", 0, L, 1, 8), a("ur1", 0, L, 1, 8), -32.0, ALU.add, -1.0, ALU.max)
+    tt(a("xp"), ind(cb, a("bcc")), a("msk"), ALU.mult)
+    mm([(a("d1", 0, L, 1, 8), a("g8"), a("xp"))])
+    ts(a("ypo", 0, L, 1, 8), a("d1", 0, L, 1, 8), -32.0 - CB, ALU.add, -1.0, ALU.max)
     dma("Y", "yp", T.yp[:], a("ypo", 0, L, 1, 8), 2400)
     dma("Y", "yv", T.yv[:, 0:W // 2], a("vw", 0, W // 2), 3500)
     dma("S", "yv2", T.yv[:, W // 2:W], a("vw", W // 2, W), 3500)
     return ops, sent[0]
 
 
-def plan(ops, hook=None):
+def plan(ops):
     n = len(ops)
     dep = [dict() for _ in range(n)]
     hist, turn = {}, {}
     for j, o in enumerate(ops):
         if o["after"] is not None:
             dep[j][o["after"]] = False
+        soft = CFG["soft"] and o["e"] in "VS" and o["sem"] is None
         for x, wr in [(x, False) for x in o["r"]] + [(x, True) for x in o["w"]]:
             h = hist.setdefault(x[0], [])
             ps = x[0] in PS
@@ -507,13 +604,15 @@ def plan(ops, hook=None):
                     dep[j][i] = True
                 elif ps and o["e"] == "P":
                     dep[j].setdefault(i, False)
+                elif hit and wr and same and soft and ops[i]["sem"] is None:
+                    dep[j].setdefault(i, False)
                 elif hit:
                     dep[j][i] = True
             if ps:
                 if h and ops[h[-1][0]]["e"] != o["e"]:
                     h[:] = [e for e in h if ops[e[0]]["e"] == ops[h[-1][0]]["e"] and e[0] > turn.get(x[0], -1)]
                     turn[x[0]] = j - 1
-            elif wr:
+            elif wr and x[3] == 1 and x[4] == 128:
                 h[:] = [e for e in h if not (x[1] <= e[1] and e[2] <= x[2])]
             h.append((j, x[1], x[2], wr))
     pri = [0.0] * n
@@ -521,7 +620,10 @@ def plan(ops, hook=None):
     for j in range(n):
         for i in dep[j]:
             succ[i].append(j)
-    cost = [max(o["c"], 1.0) for o in ops]
+    LAT = CFG["lat"]
+    cost = [max(o["c"] + (CFG["pm"] * len(o["w"]) + CFG["px"] * o["c"] if o["e"] == "P" else CFG["ov"] if o["e"] in "VS" and not o["g"] else 0.0), 1.0) for o in ops]
+    raw = cost
+    cost = [raw[j] * (CFG["gm"] if ops[j]["g"] else CFG["f"] if ops[j]["e"] in "VSPG" else 1.0) for j in range(n)]
     back = [[(i, ops[i]["lat"] + LAT if dep[j][i] else 0.0) for i in dep[j]] for j in range(n)]
     fwd = [[(k, ops[j]["lat"] + LAT if dep[k][j] else 0.0) for k in succ[j]] for j in range(n)]
     x = CFG["seed"] * 7919 + 1
@@ -556,19 +658,85 @@ def plan(ops, hook=None):
         rv = place(sorted(range(n), key=lambda j: -(st[j] + cost[j])), fwd, tail)
         st = place(sorted(range(n), key=lambda j: -(rv[j] + cost[j])), back, zero)
     end, st = best
+    key = [0.0] * n
+    for j in range(n):
+        key[j] = max([ops[j]["h"] if ops[j]["step"] >= 0 else st[j]] + [key[i] + cost[i] + d for i, d in back[j]])
+    s2 = place(sorted(range(n), key=lambda j: key[j]), back, zero)
+    if CFG["hint"]:
+        end, st = max(s2[j] + cost[j] + tail[j] for j in range(n)), s2
+    roles = {}
+    for j in range(n):
+        roles.setdefault(ops[j]["role"], []).append(j)
+    names = [r for r in sorted(roles) for _ in range(3 if len(roles[r]) > 1 else 1)]
+    pre = [list(d) for d in dep]
+    def held(st):
+        before, lastof, r = {}, {}, []
+        for j in sorted(range(n), key=lambda j: st[j]):
+            before[j] = lastof.get(ops[j]["e"]); lastof[ops[j]["e"]] = j
+        j = max(range(n - 40, n), key=lambda j: st[j] + cost[j] + tail[j])
+        while j is not None:
+            t, i = max([(st[i] + cost[i] + d, i) for i, d in back[j]] + [(0.0, None)], key=lambda q: q[0])
+            if t < st[j] - 0.5:
+                i = before[j]
+                r.append((i, j))
+            j = i
+        return r
 
-    def move(st, role, by):
-        key = [st[j] + (by if ops[j]["role"] == role else 0.0) for j in range(n)]
+    views = []
+    for w, f, gm, lat, xl in CFG["views"]:
+        c2 = [raw[j] * (gm if ops[j]["g"] else f if ops[j]["e"] in "VSPG" else 1.0) for j in range(n)]
+        views.append((w, c2, [[(i, c2[i] + (ops[i]["lat"] * (xl if ops[i]["e"] == "X" else 1.0) + lat if dep[j][i] else 0.0)) for i in dep[j]] for j in range(n)]))
+    eng = [o["e"] for o in ops]
+
+    def others(st, each=False):
+        turns, r = sorted(range(n), key=lambda j: st[j]), []
+        for w, c2, b2 in views:
+            t, free = [0.0] * n, {}
+            for j in turns:
+                t[j] = max([t[i] + d for i, d in b2[j]] + [free.get(eng[j], 0.0)])
+                free[eng[j]] = t[j] + c2[j]
+            r.append(max(t[j] + c2[j] + tail[j] for j in range(n - 40, n)))
+        return r if each else sum(v[0] * e for v, e in zip(views, r))
+
+    own = [end]
+    end += others(st)
+    pairs, top = held(st), (end, st)
+    for it in range(CFG["tries"]):
+        x = (x * 1103515245 + 12345) % 2147483648
+        by = (-4000.0, -1500.0, -500.0, -150.0, 150.0, 500.0, 1500.0, 4000.0)[(x >> 8) % 8]
+        role = names[(x >> 12) % len(names)]
+        if pairs and (x >> 5) % 4:
+            i, j = pairs[(x >> 12) % len(pairs)]
+            more = (0.0, 0.0, 300.0, 1000.0)[(x >> 9) % 4]
+            role, by = (ops[j]["role"], st[i] - st[j] - 1 - more) if (x >> 8) % 2 else (ops[i]["role"], st[j] - st[i] + 1 + more)
+        key = list(st)
+        for j in roles[role]:
+            key[j] += by
+            todo = [j] if by < 0 else []
+            while todo:
+                k = todo.pop()
+                for i in pre[k]:
+                    if key[i] >= key[k]:
+                        key[i] = key[k] - 0.01
+                        todo.append(i)
         for j in range(n):
-            for i in dep[j]:
+            for i in pre[j]:
                 if key[j] <= key[i]:
                     key[j] = key[i] + 0.01
-        return place(sorted(range(n), key=lambda j: key[j]), back, zero)
-
-    for role, by in MOVES:
-        st = move(st, role, by)
-    if hook is not None:
-        st = hook(st, move, back)
+        s2 = place(sorted(range(n), key=lambda j: key[j]), back, zero)
+        if it % CFG["fb"] == 0:
+            rv = place(sorted(range(n), key=lambda j: -(s2[j] + cost[j])), fwd, tail)
+            s2 = place(sorted(range(n), key=lambda j: -(rv[j] + cost[j])), back, zero)
+        e2 = max(s2[j] + cost[j] + tail[j] for j in range(n - 40, n))
+        if e2 > own[0] + 4 * CFG["heat"]:
+            continue
+        e1 = e2
+        e2 += others(s2) if any(v[0] for v in views) else 0.0
+        if e2 <= end + CFG["heat"] * (1.0 - it / CFG["tries"]) * ((x >> 3) % 64) / 64:
+            end, st, pairs, own[0] = e2, s2, held(s2), e1
+            if end < top[0]:
+                top = (end, st)
+    st = top[1]
     end = max(st[j] + cost[j] + tail[j] for j in range(n))
     order = sorted((st[j], j) for j in range(n))
     seq = [j for t, j in order]
@@ -597,7 +765,7 @@ def plan(ops, hook=None):
                         kn[k2] = p2
         waits[j] = ws
         clock[j] = dict(kn); clock[j][pos[j][0]] = pos[j][1]
-    return {"seq": seq, "waits": waits, "need": need, "end": end, "order": order}
+    return {"seq": seq, "waits": waits, "need": need, "end": end, "order": order, "dep": dep, "cost": cost, "views": others(st, True)}
 
 
 def rank_program(g, core, T, topo):

@@ -4,14 +4,15 @@ from concourse.mybir import AluOpType as ALU, AxisListType, ActivationFunctionTy
 W, L, RO, SH = 2048, 256, 8, 3
 CFG = {
     "h1": ["S4 B4 B4 B4"] * 3,
-    "h2": ["S2V2 S2V2 S2V2 V4"] * 3,
-    "oc": [8, 8], "seed": 0, "amp": 0.0, "xl": 4000, "it": 3, "po": 10, "zv": "S", "tries": 9000,
-    "lat": 250, "pm": 0, "px": 0.05, "ov": 5, "soft": False, "fb": 1000, "views": [], "f": 1.3, "gm": 0.85, "k0": 0.75, "k1": 1.1, "heat": 300, "cv": True, "a3": "P",
-    "uv": "VVVV", "kv": "DDDC", "kb": ["m2", "k0", "k1", "m2"], "ord": ["XXXXERRRRVVVV"] * 3,
+    "h2": ["S2V3 V4 R4 V3", "S2V3 S2V2 S2V2 V3", "S2V3 S2V2 S2V2 V3"],
+    "oc": [8, 8], "seed": 2, "amp": 0.0, "xl": 3200, "it": 3, "po": 10, "zv": "S", "tries": [7, 2500, 300, 5000],
+    "lat": 250, "pm": 0, "px": 0.05, "ov": 5, "soft": False, "fb": 1000, "views": [(0.6, 1.0, 1.2, 250, 0.75)], "f": 1.3, "gm": 0.85, "b0": 0, "s1": "S2V3 V4 S2V2 V3", "ts": [-42000, -38000, 9000, 16000], "k0": 0.75, "k1": 1.1, "heat": 300, "cv": True, "a3": "P",
+    "uv": "VVVV", "kv": "EEEE", "ki": False, "kb": ["m2", "k0", "k1", "m2"], "ord": ["XXXXERRRRVVVV"] * 3,
     "hint": True, "tx": [1900, 2600, 5000, 7400], "tv": [12000, 12000, 13500, 13000, 15000, 14000, 15000], "tr": [7000, 9000, 11000, 13000],
-    "rb": ["m1"] * 4, "tb": [1500, 3500, 5000, 3000, 8000, 5000], "td": [0, 7000, 4000, 10500, 9000, 10000], "eb": ["d0", "d1"], "fk": ["ff", "m1", "ff", "m1"],
+    "rb": ["k0", "k1", "k0", "k1"], "tb": [1500, 3500, 5000, 3000, 8000, 5000], "td": [0, 7000, 4000, 10500, 9000, 10000], "eb": ["d0", "d1"], "fk": ["ff", "m1", "ff", "m1"],
 }
 MAG, UO = 1.5 * 2 ** 23, 1023.5
+KO = 0.0
 NEZ, NEO = 8, 8
 POP = float(32 << 17)
 CB = 129
@@ -37,12 +38,12 @@ SCRATCH = {
     "zhi": _sb(144, H), "zhn": _sb(144, H), "zon": _sb(144, B), "zne": _sb(144, B), "wb": _sb(128, B), "hal": _sb(128, F), "g8": _sb(8, B),
     "msk": _sb(L, B), "thm": _sb(L, H), "sk": _sb(L, H), "c16": _sb(L, H), "c129": _sb(L, B), "slc": _sb(16 * RO, B), "l16": _sb(16, B),
     "sM": _sb(L, B), "sW": _sb(L, B), "sD": _sb(L, H), "sA": _sb(64, B), "sC": _sb(64, B), "sel": _sb(2048, B), "tg": _sb(640, B),
-    "bct": _sb(16, U), "bcc": _sb(16, U), "pma": _sb(16, U), "pmb": _sb(16, U), "rpl": _sb(8, U), "dum": _sb(16, F),
+    "bct": _sb(16, U), "bcc": _sb(16, U), "pma": _sb(16, U), "pmb": _sb(16, U), "rpl": _sb(16, U), "dum": _sb(16, F),
     "p1": _sb(L, F), "rr": _sb(L, B), "o1": _sb(L, U), "r1": _sb(L, F), "xx": _sb(L, F), "qq": _sb(L, F), "rq": _sb(L, B), "h1": _sb(L, I), "h2": _sb(L, I), "o2": _sb(L, U),
     "acc": _sb(L, F), "c1": _sb(L, B), "c2": _sb(L, B), "c3": _sb(L, B), "c4": _sb(L, B), "ee": _sb(L, B), "gg": _sb(L, B), "lv": _sb(2 * L, B),
     "eru": _sb(L, B), "kt": _sb(128, B), "lb": _sb(80, B), "lt": _sb(128, B),
-    "kf": _sb(16, F), "ki": _sb(16, I), "u32": _sb(16, I), "uf": _sb(32, F), "a3": _sb(16, U), "stk": _sb(2 * 192, F), "sc": _sb(64, F),
-    "uq": _sb(16, F), "pl": _sb(16, I), "rep": _sb(112, H), "rpa": _sb(128, B), "g8r": _sb(128, B), "z8": _sb(144, B), "bc8": _sb(8, U),
+    "kf": _sb(16, F), "ki": _sb(16, I), "kj": _sb(16, I), "u32": _sb(16, I), "uf": _sb(32, F), "a3": _sb(16, U), "stk": _sb(2 * 192, F), "sc": _sb(64, F),
+    "uq": _sb(16, F), "pl": _sb(16, I), "rep": _sb(112, H), "rpa": _sb(128, B), "g8r": _sb(128, B), "z8": _sb(144, B),
     "cnt": _sb(1, F), "ar": _sb(1, B), "av": _sb(1, F), "eq": _sb(640, B), "los": _sb(L, B), "w1": _sb(16, F), "w2": _sb(16, F),
 }
 ALIAS = {"xp": "c1", "ylt": "c2", "ylo": "c3", "ypo": "qq", "nf": "acc"}
@@ -208,9 +209,6 @@ def build(g, core, T, topo, rank):
     iota(a("iq"), [[1, 144]])
     iota(a("iti"), [[1, 16]])
     iota(a("acc"), [[37 * 32, 16], [0, 16]])
-    iota(a("ik"), [[1, 16], [0, 16]])
-    iota(a("ig"), [[16, 8], [0, 16]])
-    iota(a("im"), [[0, 16], [1, 16]])
     AND, SHR = ALU.bitwise_and, ALU.arith_shift_right
     P_, M_, G_, Z_, X_, SW, TH, WH, Y_, TB, TC, TD, R0 = range(13)
     cp(col("cf", P_), a("pi"))
@@ -227,21 +225,30 @@ def build(g, core, T, topo, rank):
     ts(a("pma"), a("iti"), col("cf", Y_), ALU.add, col("cf", TC), ALU.add)
     ts(a("bct"), a("iti"), 0.0, ALU.mult, col("cf", M_), ALU.add)
     ts(a("idf"), a("iq", 0, 128), col("cf", P_), ALU.is_equal)
-    for n, v in (("idn", 1.0), ("n64", -65536.0), ("nid", -1.0), ("n2k", -2048.0), ("hug", 2.0 ** 80), ("zer", 0.0)):
+    act(a("lb", 64, 80), a("iq", 0, 16), AF.Exp, scale=0.0)
+    ops[-1]["c"] += 1560
+    table = len(ops) - 1
+    for n, v in (("idn", 1.0), ("nid", -1.0), ("n2k", -2048.0)):
         act(a(n), a("idf"), scale=v)
-    cp(a("p1"), a("nmi")); tr(a("nw", 0, L), a("p1"))
-    mm([(a("m1", 0, L), a("swf"), a("nw", 0, L))])
-    act(a("nw", L, 2 * L), a("m1", 0, L))
+    iota(a("kj"), [[32, 8], [-16, 2]], 16)
+    ts(a("a3"), a("kj"), col("cf", M_), ALU.add)
+    cp(a("p1"), a("nmi")); cp(a("qq"), ind(a("nmi"), a("a3")))
+    tr(a("nw", 0, L), a("p1")); tr(a("nw", L, 2 * L), a("qq"))
     act(a("nb"), ind(a("nw"), a("pma")))
-    act(a("ff", 0, L), a("nb"), scale=32 + UO)
+    act(a("ff", 0, L), a("nb"), scale=32 + KO)
     tt(a("qb", L, 2 * L), a("ff", 0, L), a("acc"), ALU.add)
     ts(col("ci", 4), a("wti"), 2047, AND); cp(col("cf", WH), col("ci", 4))
     ts(a("zhi"), a("iq"), col("cf", Z_), ALU.is_equal, col("cf", WH), ALU.mult)
     act(zsl(16), zsl(SL0), bias=63.0, scale=-1.0)
     mm(red(a("m2", 0, 32), "zhi", "zs", 16 * L, 18 * L))
-    cp(a("ki"), a("m2", 16, 32)); ts(a("u32"), a("ki"), 2047, AND); ts(a("uf", 0, 16), a("u32"), -UO, ALU.add)
-    cp(a("t16i"), a("m2", 0, 16)); ts(a("pl"), a("t16i"), 2047, AND)
-    ts(a("stk", 64, 80), a("pl"), (31 << 17) + 16 * 4096 - UO, ALU.add)
+    cp(a("ki"), a("m2", 16, 32)); ts(a("u32"), a("ki"), 2047, AND); ts(a("uf", 0, 16), a("u32"), -KO, ALU.add)
+    cp(a("t16i"), a("m2", 0, 16))
+    at(0, CFG["ts"][0])
+    iota(a("ik"), [[1, 16], [0, 16]])
+    iota(a("ig"), [[16, 8], [0, 16]])
+    iota(a("im"), [[0, 16], [1, 16]])
+    ts(a("pl"), a("t16i"), 2047, AND)
+    ts(a("stk", 64, 80), a("pl"), (31 << 17) + 16 * 4096 - KO, ALU.add)
     ts(a("zon"), a("iq"), col("cf", Z_), ALU.is_equal)
     act(a("zne"), a("zon"), scale=-2.0 ** 25); act(a("zpo"), a("zon"), scale=2.0 ** 25)
     if "A" in "".join(CFG["h1"]):
@@ -251,6 +258,7 @@ def build(g, core, T, topo, rank):
     act(a("wbb"), a("wb"), scale=2.0 ** 25)
     ts(col("cf", TH), a("thi"), 0.5, ALU.add)
     ts(a("thm"), a("ik"), col("cf", M_), ALU.is_equal, col("cf", TH), ALU.mult)
+    at(0, CFG["ts"][1])
     act(a("swb"), a("swf"))
     LN2 = math.log(2.0)
     for h in range(2):
@@ -260,20 +268,24 @@ def build(g, core, T, topo, rank):
     act(a("cab"), ind(a("crw", 0, 2 * L), a("pma")))
     act(a("eca"), a("cab"), AF.Exp, bias=75 * LN2, scale=-2 * LN2)
     act(a("ert"), ind(a("crw", 2 * L, 4 * L), a("pma")), AF.Exp, bias=74 * LN2, scale=-2 * LN2)
-    act(a("c144"), a("cab"), bias=CB + 16.0)
+    ops[-1]["after"] = ops[-2]["after"] = table
     act(a("c4"), a("ik"), scale=1.0 / 32)
     mm([(a("m2", 0, L), a("idn"), a("cab")), (a("m2", 0, L), a("idn"), a("c4"))])
-    ts(a("sk"), a("m2", 0, L), -64.0, ALU.mult)
+    if CFG["kv"].strip("E"):
+        ts(a("sk"), a("m2", 0, L), -64.0, ALU.mult)
+    if "E" in CFG["kv"]:
+        ts(a("m2", L, 2 * L), a("m2", 0, L), 2.0 ** 17, ALU.mult, UO - KO, ALU.add)
     ts(a("msk"), a("im"), col("cf", M_), ALU.is_equal)
-    cp(a("bcc"), a("iti"))
+    iota(a("stk", 80, 192), [[0, 112]], 1 << 23)
+    at(0, CFG["ts"][2])
+    act(a("c144"), a("cab"), bias=CB + 16.0)
+    for n, v in (("n64", -65536.0), ("hug", 2.0 ** 80), ("zer", 0.0)):
+        act(a(n), a("idf"), scale=v)
     ts(a("w1"), a("iti"), 16.0, ALU.mult, col("cf", M_), ALU.add)
     act(a("l16"), a("w1"), scale=16.0); act(a("dum"), a("w1"), bias=float(W - 4096))
-    for o, n, v in ((a("hal"), 128, None), (a("vw", W, W + L), L, 0), (a("lb", 48, 64), 16, 0), (a("lb", 64, 80), 16, 1),
-                    (a("stk", 0, 64), 64, 0), (a("stk", 192, 256), 64, 0), (a("stk", 80, 192), 112, 1 << 23), (a("stk", 272, 384), 112, 1 << 23)):
-        if v is None:
-            act(o, a("idf"), bias=0.5, scale=0.0)
-        else:
-            iota(o, [[0, n]], v)
+    act(a("hal"), a("idf"), bias=0.5, scale=0.0)
+    for o, n, v in ((a("lb", 48, 64), 16, 0), (a("stk", 0, 64), 64, 0), (a("stk", 192, 256), 64, 0), (a("stk", 272, 384), 112, 1 << 23), (a("vw", W, W + L), L, 0)):
+        iota(o, [[0, n]], v)
     iota(a("slc"), [[4096, RO], [0, 16]], SL0 * 4096)
     iota(a("co"), [[0, 8]])
     B2 = 2.0 ** 21
@@ -285,33 +297,35 @@ def build(g, core, T, topo, rank):
     act(a("sM"), a("msk"), scale=col("co", 0)); act(a("sW"), a("msk"), scale=col("co", 1)); ts(a("sD"), a("msk"), col("co", 2), ALU.mult)
     act(a("sA", 48, 64), a("msk", 0, 16), scale=col("co", 3)); act(a("sA", 0, 48), a("msk", 0, 48), scale=col("co", 4))
     act(a("sC"), a("msk", 0, 64), scale=col("co", 5)); ts(a("sO"), a("msk", 0, 16), col("co", 6), ALU.mult)
-    ts(a("uq"), a("iti"), col("cf", M_), ALU.is_equal, -1.0, ALU.mult)
-    for m in range(16):
-        act(a("sel", 128 * m, 128 * m + 128), a("wb"), scale=col("uq", m))
-    iota(a("g8r"), [[0, 16], [16, 8]])
-    ts(a("g8r"), a("g8r"), col("cf", G_), ALU.not_equal, 3 * POP, ALU.mult)
-    act(a("g8r"), a("g8r"), bias=POP)
-    iota(a("z8"), [[0, 144]])
-    pick(a("z8"), [[1, 144]], ALU.not_equal, 1.0, -15, -16)
-    iota(a("c2", 0, 128), [[1, 16], [0, 8]])
-    mm(red(a("k0", 0, 8), "zon", "c2", 0, 128))
-    ts(a("bc8"), a("k0", 0, 8), 1.0 / 16, ALU.mult)
-    iota(a("eq"), [[1, 16], [0, 40]])
-    pick(a("eq"), [[0, 64], [-1, 10]], ALU.is_ge, 99.0, 3, 0)
-    ts(a("tg"), a("eq"), col("cf", M_), ALU.is_le, 0.5, ALU.mult)
-    iota(a("los", 0, 112), [[0, 112]])
-    for h, side in ((0, 0), (48, 1)):
-        for p in range(10):
-            iota(a("los", h + p, h + 40, 10), [[4, 4]], PAIRS[p][side])
-    iota(a("los", 96, 112), [[1, 16]])
-    mm(red(a("k1", 0, 7), "zon", "los", 0, 112))
-    ts(a("rpl", 0, 7), a("k1", 0, 7), 1.0 / 16, ALU.mult)
-    ts(a("t16i"), a("iti"), 1, AND)
-    ts(a("w1"), a("t16i"), col("cf", X_), ALU.not_equal, 256.0, ALU.mult)
-    ts(a("t16i"), a("iti"), 14, AND); tt(a("w2"), a("w1"), a("t16i"), ALU.add)
-    ts(col("cf", TD), col("cf", M_), 16.0, ALU.mult, col("cf", X_), ALU.add)
-    ts(a("pmb"), a("w2"), col("cf", TD), ALU.add)
-    ts(a("g8"), a("ig", 0, 128, 16), col("cf", G_), ALU.is_equal)
+
+    def later():
+        at(0, CFG["ts"][3])
+        ts(a("uq"), a("iti"), col("cf", M_), ALU.is_equal, -1.0, ALU.mult)
+        for m in range(16):
+            act(a("sel", 128 * m, 128 * m + 128), a("wb"), scale=col("uq", m))
+        iota(a("g8r"), [[0, 16], [16, 8]])
+        ts(a("g8r"), a("g8r"), col("cf", G_), ALU.not_equal, 3 * POP, ALU.mult)
+        act(a("g8r"), a("g8r"), bias=POP)
+        iota(a("z8"), [[0, 144]])
+        pick(a("z8"), [[1, 144]], ALU.not_equal, 1.0, -15, -16)
+        iota(a("los", 128, 256), [[1, 16], [0, 8]])
+        iota(a("los", 0, 128), [[0, 128]])
+        for h, side in ((0, 0), (48, 1)):
+            for p in range(10):
+                iota(a("los", h + p, h + 40, 10), [[4, 4]], PAIRS[p][side])
+        iota(a("los", 96, 112), [[1, 16]])
+        mm(red(a("d0", 0, 16), "zon", "los", 0, L))
+        ts(a("rpl"), a("d0", 0, 16), 1.0 / 16, ALU.mult)
+        iota(a("eq"), [[1, 16], [0, 40]])
+        pick(a("eq"), [[0, 64], [-1, 10]], ALU.is_ge, 99.0, 3, 0)
+        ts(a("tg"), a("eq"), col("cf", M_), ALU.is_le, 0.5, ALU.mult)
+        ts(a("t16i"), a("iti"), 1, AND); ts(a("ki"), a("iti"), 14, AND)
+        ts(a("cf", 16, 32), a("t16i"), col("cf", X_), ALU.not_equal, 256.0, ALU.mult)
+        tt(a("cf", 16, 32), a("cf", 16, 32), a("ki"), ALU.add)
+        ts(col("cf", TD), col("cf", M_), 16.0, ALU.mult, col("cf", X_), ALU.add)
+        ts(a("pmb"), a("cf", 16, 32), col("cf", TD), ALU.add)
+        ts(a("g8"), a("ig", 0, 128, 16), col("cf", G_), ALU.is_equal)
+        cp(a("bcc"), a("iti"))
 
     blk = [0]
     cb, sgn, dlt, dep = [a("lb", 16 * q, 16 * q + 16) for q in range(4)]
@@ -331,11 +345,11 @@ def build(g, core, T, topo, rank):
         for nk in CFG["oc"]:
             c1 = c0 + 16 * nk
             at(s, 900 if c0 else 300)
-            tt(a("p1", c0, c1), ind(a("uf", 16 * (s % 2), 16 * (s % 2) + 16), a("bct", 0, nk)), a("nb", c0, c1), ALU.mult)
+            tt(a("p1", c0, c1), ind(a("u32") if CFG["ki"] else a("uf", 16 * (s % 2), 16 * (s % 2) + 16), a("bct", 0, nk)), a("nb", c0, c1), ALU.mult)
             tt(a("h1", c0, c1), a("qb", L + c0, L + c1), a("p1", c0, c1), ALU.add)
             ts(a("h2", c0, c1), a("h1", c0, c1), 5, SHR, 2047, AND)
             if s >= 2:
-                ts(a("o1", c0, c1), a("h2", c0, c1), a("av"), ALU.add, 6144.0, ALU.add)
+                ts(a("o1", c0, c1), a("h2", c0, c1), a("av"), ALU.add, a("ff", 300, 301), ALU.add)
             else:
                 cp(a("o1", c0, c1), a("h2", c0, c1))
             c0 = c1
@@ -346,8 +360,10 @@ def build(g, core, T, topo, rank):
         z = zsl(SL0 + s)
         last = s == RO - 1
         kind = 0 if s == 0 else 2 if last else 1
-        step[1] = 1000 * (kind + 1)
+        step[1], blk[0] = 1000 * (kind + 1), CFG["b0"]
         h1, h2 = chunks(CFG["h1"][kind]), chunks(CFG["h2"][kind])
+        if s == 1 and CFG["s1"]:
+            h2, step[1] = chunks(CFG["s1"]), 4000
         if s == 0:
             columns(0)
         else:
@@ -364,7 +380,7 @@ def build(g, core, T, topo, rank):
         act(a("c1"), a("m1", 0, L), AF.Relu, scale=2.0 ** 25)
         if s >= 1:
             at(s, CFG["tb"][3])
-            act(a("uq"), a("uf", 16 * pa, 16 * pa + 16), AF.Square, bias=592 + UO)
+            act(a("uq"), a("uf", 16 * pa, 16 * pa + 16), AF.Square, bias=592 + KO)
             mm([(a("qb", 0, 16), lt, a("sO", p=80))])
             tt(a("ci"), a("qb", 0, 16), a("uq"), ALU.add)
             mm([(a("qb", 0, L), lt, a("sD", p=80))])
@@ -460,25 +476,38 @@ def build(g, core, T, topo, rank):
             c0, c1, w = 16 * k0, 16 * k1, 16 * (k1 - k0)
             f = a(CFG["fk"][c], c0, c1)
             bars = [("idf", "xx"), ("n2k", "sk"), ("idn", "c1"), ("idn", "c3")] + ([("idn", "c2"), ("hug", "lv")] if s else [])
-            mm([(f, a("wbb"), a("thm", c0, c1))] + more)
+            lean = CFG["kv"][c] == "E"
+            mm([(f, a("wbb"), a("thm", c0, c1))] + ([(f, a(x), a(y, c0, c1)) for x, y in bars[2:]] if lean else []) + more)
             mm(red(f, "zne", "eb", k0 * L, k1 * L), start=False)
             key = a(CFG["kb"][c], c0, c1)
-            if CFG["kv"][c] == "D":
+            if lean:
+                tt(a("r1", c0, c1), a("m2", L + c0, L + c1), a("xx", c0, c1), ALU.add)
+                key = a("acc", 144, 144 + w) if c + 1 == len(h2) else a("xx", c0, c1)
+                tt(key, f, a("r1", c0, c1), ALU.max)
+            elif CFG["kv"][c] == "D":
                 act(a("c4", c0, c1), f, AF.Relu)
                 mm([(key, a(x), a(y, c0, c1)) for x, y in bars])
                 mm([(key, a("idn"), a("c4", c0, c1))], start=False)
             else:
                 mm([(key, a(x), a(y, c0, c1)) for x, y in bars])
                 act(a("r1", c0, c1), key)
-                key = a("xx", c0, c1)
+                key = a("acc", 144, 144 + w) if c + 1 == len(h2) else a("xx", c0, c1)
                 tt(key, f, a("r1", c0, c1), ALU.max)
             end = c + 1 == len(h2)
-            tt(a("kf") if end and w == 16 else a("acc", 0, w), key, a("acc", 0, w) if c else a("stk", 192 * pa + 64, 192 * pa + 64 + w), ALU.min)
-            n = least[0] = max(w, least[0])
-            wn = 16 if end else 16 * (h2[-1][-1][2] - h2[-1][0][1]) if c + 2 == len(h2) else n
+            if not end:
+                tt(a("acc", 0, w), key, a("acc", 0, w) if c else a("stk", 192 * pa + 64, 192 * pa + 64 + w), ALU.min)
+            b, n = (128, 16 + w) if end else (0, max(w, least[0]))
+            wn = 16 if c + 2 >= len(h2) else 16 * (h2[c + 1][-1][2] - h2[c + 1][0][1])
             while n > wn:
                 h = min(n - wn, n // 32 * 16)
-                tt(a("kf") if end and n == 32 else a("acc", 0, h), a("acc", 0, h), a("acc", n - h, n), ALU.min)
+                o = a("acc", b, b + h) if n - h > 16 else a("kf") if end else a("acc", 128, 144)
+                if end and n % 32 == 16 and n > 32:
+                    tt(a("acc", b + 16, b + 16 + h), a("acc", b + 16, b + 16 + h), a("acc", b + n - h, b + n), ALU.min)
+                else:
+                    if o[0] == "kf" and CFG["ki"] and not last:
+                        tt(a("kj"), a("acc", b, b + h), a("acc", b + n - h, b + n), ALU.min)
+                        ts(a("u32"), a("kj"), 2047, AND)
+                    tt(o, a("acc", b, b + h), a("acc", b + n - h, b + n), ALU.min)
                 n -= h
             least[0] = n
 
@@ -502,7 +531,10 @@ def build(g, core, T, topo, rank):
             done[x] += 1
         if s:
             mm([(a("k0", 0, L, 1, 8), a("zer", 0, 8), a("msk"))])
+        else:
+            later()
         at(s + 1, 0)
+        step[1] = 1000 * (kind + 1) + 500
         un = a("uf", 16 * pb_, 16 * pb_ + 16)
         ts(a("w2"), a("kf"), MAG * 4096, ALU.add, -MAG * 4096, ALU.add)
         tt(un, a("kf"), a("w2"), ALU.subtract)
@@ -512,7 +544,7 @@ def build(g, core, T, topo, rank):
         if count:
             mm([(a("ff", 300, 301), a("hal"), a("cnt"))])
             act(a("ar"), a("ff", 300, 301), bias=191.5 + 1.0 / 64, scale=1.0 / 32)
-            ts(a("av"), a("ar"), -32.0, ALU.mult, a("ff", 300, 301), ALU.add)
+            act(a("av"), a("ar"), bias=6144.0, scale=-32.0)
         if not last:
             columns(s + 1)
         at(s + 1, 0)
@@ -525,7 +557,7 @@ def build(g, core, T, topo, rank):
             cp(zsl(SL0 + s + 1), ind(a("zs", 0, (SL0 + s + 1) * L), a("a3")))
         if s >= 1:
             at(s + 1, CFG["td"][0])
-            tt(a("rpa"), ind(a("kf"), a("bc8")), a("g8r"), ALU.is_ge)
+            tt(a("rpa"), ind(a("kf"), a("rpl", 8, 16)), a("g8r"), ALU.is_ge)
             mm([(a("k0", 4 * b + PAIRS[p][1], L, 16, 8), a("rpa", 8 * (4 * b + PAIRS[p][0]), 8 * (4 * b + PAIRS[p][0] + 1)), a("eq", 10 * b + p, 640, 40))
                 for b in range(4) for p in range(10)], start=False)
             act(a("los", p=8), a("k0", 0, L, 1, 8), scale=4096.0)
@@ -634,7 +666,10 @@ def plan(ops):
     def place(turns, pre, head):
         st, line = [0.0] * n, {}
         for j in turns:
-            t = max([st[i] + cost[i] + d for i, d in pre[j]] + [head[j]])
+            t = head[j]
+            for i, d in pre[j]:
+                if st[i] + cost[i] + d > t:
+                    t = st[i] + cost[i] + d
             s0, s1 = line.setdefault(ops[j]["e"], ([], []))
             lo, hi = 0, len(s1)
             while lo < hi:
@@ -660,20 +695,15 @@ def plan(ops):
     end, st = best
     key = [0.0] * n
     for j in range(n):
-        key[j] = max([ops[j]["h"] if ops[j]["step"] >= 0 else st[j]] + [key[i] + cost[i] + d for i, d in back[j]])
-    s2 = place(sorted(range(n), key=lambda j: key[j]), back, zero)
-    if CFG["hint"]:
-        end, st = max(s2[j] + cost[j] + tail[j] for j in range(n)), s2
-    roles = {}
-    for j in range(n):
-        roles.setdefault(ops[j]["role"], []).append(j)
-    names = [r for r in sorted(roles) for _ in range(3 if len(roles[r]) > 1 else 1)]
+        key[j] = max([ops[j]["h"]] + [key[i] + cost[i] + d for i, d in back[j]])
+    st = place(sorted(range(n), key=lambda j: key[j]), back, zero)
     pre = [list(d) for d in dep]
-    def held(st):
+
+    def held(st, m, goal):
         before, lastof, r = {}, {}, []
-        for j in sorted(range(n), key=lambda j: st[j]):
+        for j in sorted(range(m), key=lambda j: st[j]):
             before[j] = lastof.get(ops[j]["e"]); lastof[ops[j]["e"]] = j
-        j = max(range(n - 40, n), key=lambda j: st[j] + cost[j] + tail[j])
+        j = max(goal, key=lambda j: st[j] + cost[j] + tail[j])
         while j is not None:
             t, i = max([(st[i] + cost[i] + d, i) for i, d in back[j]] + [(0.0, None)], key=lambda q: q[0])
             if t < st[j] - 0.5:
@@ -688,55 +718,96 @@ def plan(ops):
         views.append((w, c2, [[(i, c2[i] + (ops[i]["lat"] * (xl if ops[i]["e"] == "X" else 1.0) + lat if dep[j][i] else 0.0)) for i in dep[j]] for j in range(n)]))
     eng = [o["e"] for o in ops]
 
-    def others(st, each=False):
-        turns, r = sorted(range(n), key=lambda j: st[j]), []
+    def others(st, m, goal, each=False):
+        turns, r = sorted(range(m), key=lambda j: st[j]), []
         for w, c2, b2 in views:
-            t, free = [0.0] * n, {}
+            if not (w or each):
+                r.append(0.0)
+                continue
+            t, free = [0.0] * m, {}
             for j in turns:
-                t[j] = max([t[i] + d for i, d in b2[j]] + [free.get(eng[j], 0.0)])
-                free[eng[j]] = t[j] + c2[j]
-            r.append(max(t[j] + c2[j] + tail[j] for j in range(n - 40, n)))
+                u = free.get(eng[j], 0.0)
+                for i, d in b2[j]:
+                    if t[i] + d > u:
+                        u = t[i] + d
+                t[j] = u
+                free[eng[j]] = u + c2[j]
+            r.append(max(t[j] + c2[j] + tail[j] for j in goal))
         return r if each else sum(v[0] * e for v, e in zip(views, r))
 
-    own = [end]
-    end += others(st)
-    pairs, top = held(st), (end, st)
-    for it in range(CFG["tries"]):
-        x = (x * 1103515245 + 12345) % 2147483648
-        by = (-4000.0, -1500.0, -500.0, -150.0, 150.0, 500.0, 1500.0, 4000.0)[(x >> 8) % 8]
-        role = names[(x >> 12) % len(names)]
-        if pairs and (x >> 5) % 4:
-            i, j = pairs[(x >> 12) % len(pairs)]
-            more = (0.0, 0.0, 300.0, 1000.0)[(x >> 9) % 4]
-            role, by = (ops[j]["role"], st[i] - st[j] - 1 - more) if (x >> 8) % 2 else (ops[i]["role"], st[j] - st[i] + 1 + more)
-        key = list(st)
-        for j in roles[role]:
-            key[j] += by
-            todo = [j] if by < 0 else []
-            while todo:
-                k = todo.pop()
-                for i in pre[k]:
-                    if key[i] >= key[k]:
-                        key[i] = key[k] - 0.01
-                        todo.append(i)
-        for j in range(n):
+    def settle(key, m):
+        for j in range(m):
             for i in pre[j]:
                 if key[j] <= key[i]:
                     key[j] = key[i] + 0.01
-        s2 = place(sorted(range(n), key=lambda j: key[j]), back, zero)
-        if it % CFG["fb"] == 0:
-            rv = place(sorted(range(n), key=lambda j: -(s2[j] + cost[j])), fwd, tail)
-            s2 = place(sorted(range(n), key=lambda j: -(rv[j] + cost[j])), back, zero)
-        e2 = max(s2[j] + cost[j] + tail[j] for j in range(n - 40, n))
-        if e2 > own[0] + 4 * CFG["heat"]:
-            continue
-        e1 = e2
-        e2 += others(s2) if any(v[0] for v in views) else 0.0
-        if e2 <= end + CFG["heat"] * (1.0 - it / CFG["tries"]) * ((x >> 3) % 64) / 64:
-            end, st, pairs, own[0] = e2, s2, held(s2), e1
-            if end < top[0]:
-                top = (end, st)
-    st = top[1]
+        return place(sorted(range(m), key=lambda j: key[j]), back, zero)
+
+    def search(st, m, goal, lo, hi, tries, x):
+        roles = {}
+        for j in range(m):
+            if lo <= ops[j]["step"] <= hi:
+                roles.setdefault(ops[j]["role"], []).append(j)
+        names = [r for r in sorted(roles) for _ in range(3 if len(roles[r]) > 1 else 1)]
+        st = settle(list(st), m)
+        own = max(st[j] + cost[j] + tail[j] for j in goal)
+        end = own + others(st, m, goal)
+        pairs, top = [q for q in held(st, m, goal) if ops[q[0]]["role"] in roles and ops[q[1]]["role"] in roles], (end, st)
+        for it in range(tries):
+            x = (x * 1103515245 + 12345) % 2147483648
+            by = (-4000.0, -1500.0, -500.0, -150.0, 150.0, 500.0, 1500.0, 4000.0)[(x >> 8) % 8]
+            role = names[(x >> 12) % len(names)]
+            if pairs and (x >> 5) % 4:
+                i, j = pairs[(x >> 12) % len(pairs)]
+                more = (0.0, 0.0, 300.0, 1000.0)[(x >> 9) % 4]
+                role, by = (ops[j]["role"], st[i] - st[j] - 1 - more) if (x >> 8) % 2 else (ops[i]["role"], st[j] - st[i] + 1 + more)
+            key = st[:m]
+            for j in roles[role]:
+                key[j] += by
+                todo = [j] if by < 0 else []
+                while todo:
+                    k = todo.pop()
+                    for i in pre[k]:
+                        if key[i] >= key[k]:
+                            key[i] = key[k] - 0.01
+                            todo.append(i)
+            s2 = settle(key, m)
+            if it % CFG["fb"] == 0 and lo < 1 < hi:
+                rv = place(sorted(range(m), key=lambda j: -(s2[j] + cost[j])), [[q for q in f if q[0] < m] for f in fwd], tail)
+                s2 = place(sorted(range(m), key=lambda j: -(rv[j] + cost[j])), back, zero)
+            e1 = max(s2[j] + cost[j] + tail[j] for j in goal)
+            if e1 > own + 2 * CFG["heat"]:
+                continue
+            e2 = e1 + others(s2, m, goal)
+            if e2 <= end + CFG["heat"] * (1.0 - it / tries) * ((x >> 3) % 64) / 64:
+                end, st, own = e2, s2, e1
+                pairs = [q for q in held(st, m, goal) if ops[q[0]]["role"] in roles and ops[q[1]]["role"] in roles]
+                if end < top[0]:
+                    top = (end, st)
+        return top[1]
+
+    of = {}
+    for j in range(n):
+        of.setdefault(ops[j]["step"], []).append(j)
+    move = {s: [j for j in of[s] if ops[j]["w"] and ops[j]["w"][0][0] == "kf"] for s in range(RO)}
+    t0, t1, t2, t3 = CFG["tries"]
+    m = of[3][-1] + 1
+    s1 = min((search(st, m, move[3], -1, 3, t1, x + k) for k in range(t0)), key=lambda q: q[move[3][0]] + others(q, m, move[3]), default=st)
+    st, per = s1[:m] + st[m:], s1[move[3][0]] - s1[move[2][0]]
+    for s in range(4, RO) if t0 else []:
+        k = 0
+        for j in of[s]:
+            while (eng[of[2][k]], ops[of[2][k]]["w"][:1] and ops[of[2][k]]["w"][0][0]) != (eng[j], ops[j]["w"][:1] and ops[j]["w"][0][0]):
+                k += 1
+            st[j] = st[of[2][k]] + per * (s - 2)
+            k += 1
+    for j in of[3] if t0 else []:
+        if j > move[3][0]:
+            st[j] = st[of[2][of[3].index(j)]] + per
+    for j in of[RO] if t0 else []:
+        st[j] = per * RO + 40000
+    goal = list(range(n - 40, n))
+    st = search(st, n, goal, RO - 1, RO, t2, x)
+    st = search(st, n, goal, -1, RO, t3, x + 1) if t3 else st
     end = max(st[j] + cost[j] + tail[j] for j in range(n))
     order = sorted((st[j], j) for j in range(n))
     seq = [j for t, j in order]
@@ -765,7 +836,7 @@ def plan(ops):
                         kn[k2] = p2
         waits[j] = ws
         clock[j] = dict(kn); clock[j][pos[j][0]] = pos[j][1]
-    return {"seq": seq, "waits": waits, "need": need, "end": end, "order": order, "dep": dep, "cost": cost, "views": others(st, True)}
+    return {"seq": seq, "waits": waits, "need": need, "end": end, "order": order, "dep": dep, "cost": cost, "views": others(st, n, goal, True)}
 
 
 def rank_program(g, core, T, topo):

import math
from concourse.mybir import AluOpType as ALU, AxisListType, ActivationFunctionType as AF

W, L, RO, SH = 2048, 256, 8, 3
CFG = {
    "h1": ["S4 B4 B4 B4"] * 3,
    "h2": ["S2V3 V4 R4 V3", "S2V3 S2V2 S2V2 V3", "S2V3 S2V2 S2V2 V3"],
    "oc": [8, 8], "seed": 2, "amp": 0.0, "xl": 3200, "it": 3, "po": 10, "zv": "S", "tries": [7, 2500, 300, 5000],
    "lat": 250, "pm": 0, "px": 0.05, "ov": 5, "soft": False, "fb": 1000, "views": [(0.6, 1.0, 1.2, 250, 0.75)], "f": 1.3, "gm": 0.85, "b0": 0, "s1": "S2V3 V4 S2V2 V3", "ts": [-42000, -38000, 9000, 16000], "k0": 0.75, "k1": 1.1, "heat": 300, "cv": True, "a3": "P",
    "uv": "VVVV", "kv": "EEEE", "ki": False, "kb": ["m2", "k0", "k1", "m2"], "ord": ["XXXXERRRRVVVV"] * 3,
    "hint": True, "tx": [1900, 2600, 5000, 7400], "tv": [12000, 12000, 13500, 13000, 15000, 14000, 15000], "tr": [7000, 9000, 11000, 13000],
    "rb": ["k0", "k1", "k0", "k1"], "tb": [1500, 3500, 5000, 3000, 8000, 5000], "td": [0, 7000, 4000, 10500, 9000, 10000], "eb": ["d0", "d1"], "fk": ["ff", "m1", "ff", "m1"],
}
MAG, UO = 1.5 * 2 ** 23, 1023.5
KO = 0.0
NEZ, NEO = 8, 8
POP = float(32 << 17)
CB = 129
SL0 = 17
XW = W + 64
PAIRS = [(i, i) for i in range(4)] + [(i, j) for j in range(4) for i in range(j)]
F, B, I, U, H = "float32", "bfloat16", "int32", "uint16", "float16"


def _sb(n, d):
    return ("sbuf", [128, n], d)


SCRATCH = {
    "xw": _sb(XW, B), "vw": _sb(W + L, B), "zs": _sb(26 * L, B), "yb": _sb(4096, B), "sg": _sb(4096, B), "eb": _sb(4096, B), "rb": _sb(4096, B),
    "lz": _sb(7 * L, B), "lo": _sb(7 * 16, U), "so": _sb(7 * 16, U),
    "nmi": _sb(L, I), "cr": _sb(2 * L, B), "wti": _sb(1, I), "thi": _sb(1, I),
    "nw": _sb(2 * L, F), "crw": _sb(4 * L, B), "nb": _sb(L, F), "cab": _sb(L, B), "c144": _sb(L, B), "eca": _sb(L, B), "ert": _sb(L, B),
    "pi": _sb(1, I), "ci": _sb(16, I), "cf": _sb(32, F), "co": _sb(8, F),
    "iq": _sb(144, F), "ig": _sb(128, F), "ik": _sb(L, F), "im": _sb(L, F), "iti": _sb(16, I), "t16i": _sb(16, I),
    "idn": _sb(128, B), "nid": _sb(128, B), "hug": _sb(128, B), "n2k": _sb(128, B), "n64": _sb(128, B), "uo": _sb(128, H), "wbb": _sb(128, B), "zpo": _sb(144, B), "sO": _sb(16, H), "zer": _sb(128, B),
    "idf": _sb(128, F), "nif": _sb(128, F), "swb": _sb(128, B), "swf": _sb(128, F),
    "zhi": _sb(144, H), "zhn": _sb(144, H), "zon": _sb(144, B), "zne": _sb(144, B), "wb": _sb(128, B), "hal": _sb(128, F), "g8": _sb(8, B),
    "msk": _sb(L, B), "thm": _sb(L, H), "sk": _sb(L, H), "c16": _sb(L, H), "c129": _sb(L, B), "slc": _sb(16 * RO, B), "l16": _sb(16, B),
    "sM": _sb(L, B), "sW": _sb(L, B), "sD": _sb(L, H), "sA": _sb(64, B), "sC": _sb(64, B), "sel": _sb(2048, B), "tg": _sb(640, B),
    "bct": _sb(16, U), "bcc": _sb(16, U), "pma": _sb(16, U), "pmb": _sb(16, U), "rpl": _sb(16, U), "dum": _sb(16, F),
    "p1": _sb(L, F), "rr": _sb(L, B), "o1": _sb(L, U), "r1": _sb(L, F), "xx": _sb(L, F), "qq": _sb(L, F), "rq": _sb(L, B), "h1": _sb(L, I), "h2": _sb(L, I), "o2": _sb(L, U),
    "acc": _sb(L, F), "c1": _sb(L, B), "c2": _sb(L, B), "c3": _sb(L, B), "c4": _sb(L, B), "ee": _sb(L, B), "gg": _sb(L, B), "lv": _sb(2 * L, B),
    "eru": _sb(L, B), "kt": _sb(128, B), "lb": _sb(80, B), "lt": _sb(128, B),
    "kf": _sb(16, F), "ki": _sb(16, I), "kj": _sb(16, I), "u32": _sb(16, I), "uf": _sb(32, F), "a3": _sb(16, U), "stk": _sb(2 * 192, F), "sc": _sb(64, F),
    "uq": _sb(16, F), "pl": _sb(16, I), "rep": _sb(112, H), "rpa": _sb(128, B), "g8r": _sb(128, B), "z8": _sb(144, B),
    "cnt": _sb(1, F), "ar": _sb(1, B), "av": _sb(1, F), "eq": _sb(640, B), "los": _sb(L, B), "w1": _sb(16, F), "w2": _sb(16, F),
}
ALIAS = {"xp": "c1", "ylt": "c2", "ylo": "c3", "ypo": "qq", "nf": "acc"}
PS = ["d0", "d1", "k0", "k1", "ff", "qb", "m1", "m2"]
for _n in PS:
    SCRATCH[_n] = ("psum", [128, 512], F)
DMAS = ["nm", "ca", "rt", "z0", "wt", "th", "xt", "x2", "xe", "vt", "yv", "yv2", "yz", "yl", "yp"]
SEMAPHORES = ["eV", "eS", "eP", "eG", "sent"] + ["m_" + n for n in DMAS] + ["az%d" % s for s in range(RO)] + ["ao%d" % s for s in range(RO)]
CACHE = {}
LAT = 70
GC, SC, TT = 1.56, 3.8, 2.0


def build(g, core, T, topo, rank):
    ops, step, group, since = [], [-1, 0, 0], {}, {}

    def at(s, t):
        step[2] = 40000 * (s + 1) + t * CFG["k1"] * (1.0 if s else CFG["k0"])
        since.clear()

    two = {n: SCRATCH[n][2] in (B, U, H) for n in SCRATCH}

    def a(n, c0=0, c1=None, st=1, p=128):
        n = ALIAS.get(n, n)
        return (n, c0, SCRATCH[n][1][1] if c1 is None else c1, st, p)

    def ind(w, o):
        return ("*", w, o)

    def ap(x):
        if not isinstance(x, tuple):
            return x
        if x[0] == "*":
            return ap(x[1]).indirect(ap(x[2]))
        if x[3] == 1:
            return T[x[0]][0:x[4], x[1]:x[2]]
        return T[x[0]][0:x[4], x[1]:x[2]:x[3]]

    def regs(xs):
        r = []
        for x in xs:
            if isinstance(x, tuple):
                r += [x[1], x[2]] if x[0] == "*" else [x]
        return r

    def num(x):
        return 16 * num(x[2]) if x[0] == "*" else len(range(x[1], x[2], x[3]))

    def add(e, cost, rd, wr, fn, sem=None, lat=0, after=None):
        r, w = regs(rd), []
        for x in wr:
            if x[0] == "*":
                w.append(x[1]); r.append(x[2])
            else:
                w.append(x)
        ops.append({"e": e, "c": cost, "r": r, "w": w, "f": fn, "sem": sem, "lat": lat, "after": after, "step": step[0], "role": step[1], "h": step[2] + since.get(e, 0),
                    "g": any(isinstance(x, tuple) and x[0] == "*" for x in rd + wr)})
        step[1] += 1
        since[e] = since.get(e, 0) + cost
        return len(ops) - 1

    def vcost(o, i, rate=None):
        n = num(o)
        if o[0] == "*":
            return 60 + SC * n
        if i[0] == "*":
            return 60 + GC * n
        if rate is None:
            rate = 0.5 if two[o[0]] and two[i[0]] else 1.0
        return 20 + max(64, rate * n)

    def cp(o, i):
        add("V", vcost(o, i), [i], [o], lambda: g.vector.tensor_copy(ap(o), ap(i)))

    def ms(o, v):
        add("V", 20 + max(64, num(o) * (0.5 if two[o[0]] else 1)), [], [o], lambda: g.vector.memset(ap(o), v))

    def tt(o, x, y, op):
        rate = 1.0 if (x[0] in PS or y[0] in PS) else TT
        add("V", vcost(o, x, rate), [x, y], [o], lambda: g.vector.tensor_tensor(ap(o), ap(x), ap(y), op))

    def ts(o, x, s1, op0, s2=None, op1=None):
        if op1 is None:
            fn = lambda: g.vector.tensor_scalar(ap(o), ap(x), ap(s1), None, op0)
        else:
            fn = lambda: g.vector.tensor_scalar(ap(o), ap(x), ap(s1), ap(s2), op0, op1)
        add("V", vcost(o, x), [x, s1, s2], [o], fn)

    def tr(o, i):
        add("V", vcost(o, i), [i], [o], lambda: g.vector.transpose(ap(o), ap(i)))

    def act(o, i, f=AF.Identity, bias=0.0, scale=1.0, acc=None):
        c = (80 + GC * num(o)) if i[0] == "*" else 40 + max(64, num(o))
        if acc is None:
            fn = lambda: g.scalar.activation(ap(o), ap(i), f, bias=ap(bias), scale=ap(scale))
        else:
            fn = lambda: g.scalar.activation(ap(o), ap(i), f, bias=ap(bias), scale=ap(scale), accum_out=ap(acc))
        add("S", c, [i, bias, scale], [o] + ([acc] if acc else []), fn)

    def mm(items, start=True, each=0):
        stop = [True]
        if not start:
            group[items[0][0][0]][0] = False
        group[items[0][0][0]] = stop

        def fn():
            r = None
            for j, (o, l, x) in enumerate(items):
                if each:
                    r = g.tensor.matmul(ap(o), ap(l), ap(x), j % each == 0, j % each == each - 1)
                else:
                    r = g.tensor.matmul(ap(o), ap(l), ap(x), start and j == 0, stop[0] and j == len(items) - 1)
            return r
        c = sum(max(min(64, num(l)), num(x)) * (0.5 if two[x[0]] else 2.0) for o, l, x in items) + CFG["po"]
        add("P", c, [z for o, l, x in items for z in (l, x)], [o for o, l, x in items], fn, lat=40 - CFG["po"])

    def red(o, z, src, c0, c1):
        return [(o, a(z, 15 - m, 143 - m), a(src, c0 + m, c1, 16)) for m in range(16)]

    def iota(o, pat, base=0, cm=0):
        if SCRATCH[o[0]][2] == I:
            fn = lambda: g.iota(ap(o), pat, base, cm)
        else:
            fn = lambda: g.iota(ap(o), pat, base, cm, allow_small_or_imprecise_dtypes=True)
        add("G", 160 + 2 * num(o), [], [o], fn)

    def pick(o, pat, op, fill, base, cm):
        add("G", 205 + 2 * num(o), [o], [o], lambda: g.affine_select(ap(o), ap(o), pat, op, fill, base, cm))

    def dma(q, name, o, i, lat):
        eng = g.sync if q == "Y" else g.scalar
        add(q, 70, [i], [o] if isinstance(o, tuple) else [], lambda: eng.dma_start(ap(o), ap(i)), sem=("m_" + name, 16), lat=lat)

    dst = T.cores[(rank + SH) % len(T.cores)]
    src = T.cores[(rank - SH) % len(T.cores)]
    rid, pid = topo.addr(dst, core)
    sent = [0, None]

    def send(o, i, sem, ne, lat):
        en = topo.engines(core, dst)[:ne]
        m = sum(1 << e for e in en)
        sent[0] += len(en)
        j = add("G", 600, [i], [], lambda: g.remote_dma(ap(o), ap(i), T.sem[sem], T.sem.sent, pid, rid, m), sem=("", 0), after=sent[1])
        sent[1] = j
        add("X", 0, [], [o], None, sem=(sem, len(topo.engines(src, core)[:ne])), lat=lat, after=j)

    def zsl(s):
        return a("zs", s * L, (s + 1) * L)

    def col(n, j):
        return a(n, j, j + 1)

    dma("Y", "nm", a("nmi"), T.nm[:], 2400)
    dma("S", "z0", zsl(SL0), T.z0[:], 2400)
    dma("Y", "wt", a("wti"), T.wt[:], 2400)
    dma("S", "xe", a("xw", XW - 64, XW), T.xt[:, 0:64], 2400)
    dma("Y", "xt", a("xw", 0, W), T.xt[:], 4500)
    dma("S", "ca", a("cr", 0, L), T.ca[:], 2600)
    dma("S", "rt", a("cr", L, 2 * L), T.rt[:], 2600)
    dma("S", "th", a("thi"), T.th[:], 2600)
    dma("Y", "vt", a("vw", 0, W), T.vt[:], 7500)
    iota(a("pi"), [[0, 1]], 0, 1)
    iota(a("iq"), [[1, 144]])
    iota(a("iti"), [[1, 16]])
    iota(a("acc"), [[37 * 32, 16], [0, 16]])
    AND, SHR = ALU.bitwise_and, ALU.arith_shift_right
    P_, M_, G_, Z_, X_, SW, TH, WH, Y_, TB, TC, TD, R0 = range(13)
    cp(col("cf", P_), a("pi"))
    ts(col("ci", 0), a("pi"), 15, AND); cp(col("cf", M_), col("ci", 0))
    tt(col("cf", G_), col("cf", P_), col("cf", M_), ALU.subtract)
    ts(col("cf", Z_), col("cf", G_), 15.0, ALU.add)
    ts(col("ci", 1), a("pi"), 4, SHR, 1, AND); cp(col("cf", X_), col("ci", 1))
    ts(col("cf", TB), col("cf", X_), -32.0, ALU.mult, col("cf", P_), ALU.add)
    ts(col("cf", SW), col("cf", TB), 16.0, ALU.add)
    ts(a("swf"), a("iq", 0, 128), col("cf", SW), ALU.is_equal)
    ts(col("ci", 2), a("pi"), 1, AND); ts(col("ci", 3), a("pi"), 14, AND)
    ts(col("cf", Y_), col("ci", 2), col("cf", X_), ALU.not_equal, 256.0, ALU.mult)
    ts(col("cf", TC), col("ci", 3), col("cf", X_), ALU.add, 16.0, ALU.mult)
    ts(a("pma"), a("iti"), col("cf", Y_), ALU.add, col("cf", TC), ALU.add)
    ts(a("bct"), a("iti"), 0.0, ALU.mult, col("cf", M_), ALU.add)
    ts(a("idf"), a("iq", 0, 128), col("cf", P_), ALU.is_equal)
    act(a("lb", 64, 80), a("iq", 0, 16), AF.Exp, scale=0.0)
    ops[-1]["c"] += 1560
    table = len(ops) - 1
    for n, v in (("idn", 1.0), ("nid", -1.0), ("n2k", -2048.0)):
        act(a(n), a("idf"), scale=v)
    iota(a("kj"), [[32, 8], [-16, 2]], 16)
    ts(a("a3"), a("kj"), col("cf", M_), ALU.add)
    cp(a("p1"), a("nmi")); cp(a("qq"), ind(a("nmi"), a("a3")))
    tr(a("nw", 0, L), a("p1")); tr(a("nw", L, 2 * L), a("qq"))
    act(a("nb"), ind(a("nw"), a("pma")))
    act(a("ff", 0, L), a("nb"), scale=32 + KO)
    tt(a("qb", L, 2 * L), a("ff", 0, L), a("acc"), ALU.add)
    ts(col("ci", 4), a("wti"), 2047, AND); cp(col("cf", WH), col("ci", 4))
    ts(a("zhi"), a("iq"), col("cf", Z_), ALU.is_equal, col("cf", WH), ALU.mult)
    act(zsl(16), zsl(SL0), bias=63.0, scale=-1.0)
    mm(red(a("m2", 0, 32), "zhi", "zs", 16 * L, 18 * L))
    cp(a("ki"), a("m2", 16, 32)); ts(a("u32"), a("ki"), 2047, AND); ts(a("uf", 0, 16), a("u32"), -KO, ALU.add)
    cp(a("t16i"), a("m2", 0, 16))
    at(0, CFG["ts"][0])
    iota(a("ik"), [[1, 16], [0, 16]])
    iota(a("ig"), [[16, 8], [0, 16]])
    iota(a("im"), [[0, 16], [1, 16]])
    ts(a("pl"), a("t16i"), 2047, AND)
    ts(a("stk", 64, 80), a("pl"), (31 << 17) + 16 * 4096 - KO, ALU.add)
    ts(a("zon"), a("iq"), col("cf", Z_), ALU.is_equal)
    act(a("zne"), a("zon"), scale=-2.0 ** 25); act(a("zpo"), a("zon"), scale=2.0 ** 25)
    if "A" in "".join(CFG["h1"]):
        ts(a("zhn"), a("zhi"), -1.0, ALU.mult)
    ts(a("uo"), a("idn"), 0.0, ALU.mult, -UO, ALU.add)
    ts(a("wb"), a("ig"), col("cf", G_), ALU.is_equal)
    act(a("wbb"), a("wb"), scale=2.0 ** 25)
    ts(col("cf", TH), a("thi"), 0.5, ALU.add)
    ts(a("thm"), a("ik"), col("cf", M_), ALU.is_equal, col("cf", TH), ALU.mult)
    at(0, CFG["ts"][1])
    act(a("swb"), a("swf"))
    LN2 = math.log(2.0)
    for h in range(2):
        tr(a("crw", 2 * h * L, (2 * h + 1) * L), a("cr", h * L, (h + 1) * L))
        mm([(a("m2", 0, L), a("swb"), a("crw", 2 * h * L, (2 * h + 1) * L))])
        act(a("crw", (2 * h + 1) * L, (2 * h + 2) * L), a("m2", 0, L))
    act(a("cab"), ind(a("crw", 0, 2 * L), a("pma")))
    act(a("eca"), a("cab"), AF.Exp, bias=75 * LN2, scale=-2 * LN2)
    act(a("ert"), ind(a("crw", 2 * L, 4 * L), a("pma")), AF.Exp, bias=74 * LN2, scale=-2 * LN2)
    ops[-1]["after"] = ops[-2]["after"] = table
    act(a("c4"), a("ik"), scale=1.0 / 32)
    mm([(a("m2", 0, L), a("idn"), a("cab")), (a("m2", 0, L), a("idn"), a("c4"))])
    if CFG["kv"].strip("E"):
        ts(a("sk"), a("m2", 0, L), -64.0, ALU.mult)
    if "E" in CFG["kv"]:
        ts(a("m2", L, 2 * L), a("m2", 0, L), 2.0 ** 17, ALU.mult, UO - KO, ALU.add)
    ts(a("msk"), a("im"), col("cf", M_), ALU.is_equal)
    iota(a("stk", 80, 192), [[0, 112]], 1 << 23)
    at(0, CFG["ts"][2])
    act(a("c144"), a("cab"), bias=CB + 16.0)
    for n, v in (("n64", -65536.0), ("hug", 2.0 ** 80), ("zer", 0.0)):
        act(a(n), a("idf"), scale=v)
    ts(a("w1"), a("iti"), 16.0, ALU.mult, col("cf", M_), ALU.add)
    act(a("l16"), a("w1"), scale=16.0); act(a("dum"), a("w1"), bias=float(W - 4096))
    act(a("hal"), a("idf"), bias=0.5, scale=0.0)
    for o, n, v in ((a("lb", 48, 64), 16, 0), (a("stk", 0, 64), 64, 0), (a("stk", 192, 256), 64, 0), (a("stk", 272, 384), 112, 1 << 23), (a("vw", W, W + L), L, 0)):
        iota(o, [[0, n]], v)
    iota(a("slc"), [[4096, RO], [0, 16]], SL0 * 4096)
    iota(a("co"), [[0, 8]])
    B2 = 2.0 ** 21
    for j, cs in enumerate(([1, -16], [0, 0.5, 0, 1, 0.5], [0, 0, 0, 19616, (19616 - 592 ** 2) % 65536], [2 ** 17, -3 * B2, 2 * B2, 0, -(CB + 48) * 2 ** 17], [0, -4 * B2, 0, 0, -4 * B2], [0, 4 * B2, 0, 0, -4 * B2],
                            [0, 0, 0, 19616, -592 ** 2 % 65536])):
        for q in range(len(cs) - 1, -1, -1):
            if q == len(cs) - 1 or cs[q] != cs[q + 1]:
                pick(col("co", j), [[0, 1]], ALU.is_ge, float(cs[q]), -16 * (q + 1), 1)
    act(a("sM"), a("msk"), scale=col("co", 0)); act(a("sW"), a("msk"), scale=col("co", 1)); ts(a("sD"), a("msk"), col("co", 2), ALU.mult)
    act(a("sA", 48, 64), a("msk", 0, 16), scale=col("co", 3)); act(a("sA", 0, 48), a("msk", 0, 48), scale=col("co", 4))
    act(a("sC"), a("msk", 0, 64), scale=col("co", 5)); ts(a("sO"), a("msk", 0, 16), col("co", 6), ALU.mult)

    def later():
        at(0, CFG["ts"][3])
        ts(a("uq"), a("iti"), col("cf", M_), ALU.is_equal, -1.0, ALU.mult)
        for m in range(16):
            act(a("sel", 128 * m, 128 * m + 128), a("wb"), scale=col("uq", m))
        iota(a("g8r"), [[0, 16], [16, 8]])
        ts(a("g8r"), a("g8r"), col("cf", G_), ALU.not_equal, 3 * POP, ALU.mult)
        act(a("g8r"), a("g8r"), bias=POP)
        iota(a("z8"), [[0, 144]])
        pick(a("z8"), [[1, 144]], ALU.not_equal, 1.0, -15, -16)
        iota(a("los", 128, 256), [[1, 16], [0, 8]])
        iota(a("los", 0, 128), [[0, 128]])
        for h, side in ((0, 0), (48, 1)):
            for p in range(10):
                iota(a("los", h + p, h + 40, 10), [[4, 4]], PAIRS[p][side])
        iota(a("los", 96, 112), [[1, 16]])
        mm(red(a("d0", 0, 16), "zon", "los", 0, L))
        ts(a("rpl"), a("d0", 0, 16), 1.0 / 16, ALU.mult)
        iota(a("eq"), [[1, 16], [0, 40]])
        pick(a("eq"), [[0, 64], [-1, 10]], ALU.is_ge, 99.0, 3, 0)
        ts(a("tg"), a("eq"), col("cf", M_), ALU.is_le, 0.5, ALU.mult)
        ts(a("t16i"), a("iti"), 1, AND); ts(a("ki"), a("iti"), 14, AND)
        ts(a("cf", 16, 32), a("t16i"), col("cf", X_), ALU.not_equal, 256.0, ALU.mult)
        tt(a("cf", 16, 32), a("cf", 16, 32), a("ki"), ALU.add)
        ts(col("cf", TD), col("cf", M_), 16.0, ALU.mult, col("cf", X_), ALU.add)
        ts(a("pmb"), a("cf", 16, 32), col("cf", TD), ALU.add)
        ts(a("g8"), a("ig", 0, 128, 16), col("cf", G_), ALU.is_equal)
        cp(a("bcc"), a("iti"))

    blk = [0]
    cb, sgn, dlt, dep = [a("lb", 16 * q, 16 * q + 16) for q in range(4)]
    lt = a("lt", p=80)
    QC = 3.0 - 592.0 ** 2

    def chunks(text):
        r, k = [], 0
        for x in text.split():
            r.append([])
            for i in range(0, len(x), 2):
                r[-1].append((x[i], k, k + int(x[i + 1]))); k += int(x[i + 1])
        return r

    def columns(s):
        c0 = 0
        for nk in CFG["oc"]:
            c1 = c0 + 16 * nk
            at(s, 900 if c0 else 300)
            tt(a("p1", c0, c1), ind(a("u32") if CFG["ki"] else a("uf", 16 * (s % 2), 16 * (s % 2) + 16), a("bct", 0, nk)), a("nb", c0, c1), ALU.mult)
            tt(a("h1", c0, c1), a("qb", L + c0, L + c1), a("p1", c0, c1), ALU.add)
            ts(a("h2", c0, c1), a("h1", c0, c1), 5, SHR, 2047, AND)
            if s >= 2:
                ts(a("o1", c0, c1), a("h2", c0, c1), a("av"), ALU.add, a("ff", 300, 301), ALU.add)
            else:
                cp(a("o1", c0, c1), a("h2", c0, c1))
            c0 = c1

    for s in range(RO):
        step[0] = s
        pa, pb_ = s % 2, (s + 1) % 2
        z = zsl(SL0 + s)
        last = s == RO - 1
        kind = 0 if s == 0 else 2 if last else 1
        step[1], blk[0] = 1000 * (kind + 1), CFG["b0"]
        h1, h2 = chunks(CFG["h1"][kind]), chunks(CFG["h2"][kind])
        if s == 1 and CFG["s1"]:
            h2, step[1] = chunks(CFG["s1"]), 4000
        if s == 0:
            columns(0)
        else:
            send(a("lz", (s - 1) * L, s * L), z, "az%d" % s, NEZ, 3000)
        lv, eru = a("lv", 0, L), "ert"
        at(s, CFG["tb"][2])
        if s >= 1:
            mm([(a("m1", 0, L), a("hug"), lv), (a("m1", 0, L), a("nid"), a("ert"))])
            act(a("eru"), a("m1", 0, L), AF.Relu, scale=-1.0)
            eru = "eru"
        mm([(a("m1", 0, 128), a(eru, 128 * h, 128 * h + 128), a("idn")) for h in range(2)])
        act(a("kt"), a("m1", 0, 128))
        mm([(a("m1", 0, L), a("kt"), a("msk")), (a("m1", 0, L), a("nid"), a("eca"))])
        act(a("c1"), a("m1", 0, L), AF.Relu, scale=2.0 ** 25)
        if s >= 1:
            at(s, CFG["tb"][3])
            act(a("uq"), a("uf", 16 * pa, 16 * pa + 16), AF.Square, bias=592 + KO)
            mm([(a("qb", 0, 16), lt, a("sO", p=80))])
            tt(a("ci"), a("qb", 0, 16), a("uq"), ALU.add)
            mm([(a("qb", 0, L), lt, a("sD", p=80))])
            at(s, CFG["tb"][5])
            ts(a("pl"), a("ci"), 5, SHR, 2047, AND)
            cp(a("rep"), ind(a("pl"), a("rpl", 0, 7)))
        kept, least, turn = {}, [0], [0, 0]

        def first(c):
            pieces = h1[c]
            for md, k0, k1 in pieces:
                zk, y = a("zs", k0 * L, k1 * L), a("yb", k0 * L, k1 * L)
                at(s, CFG["tx"][turn[0]]); turn[0] += 1
                if md == "S":
                    act(y, ind(a("xw"), a("o1", 16 * k0, 16 * k1)))
                    for k in range(k0, k1, 2):
                        d = "d%d" % (blk[0] % 2); blk[0] += 1
                        n = min(2, k1 - k)
                        mm([(a(d, 0, n * L), a("idn"), a("yb", k * L, (k + n) * L))] + [(a(d, i * L, (i + 1) * L), a("nid"), z) for i in range(n)])
                        act(a("zs", k * L, (k + n) * L), a(d, 0, n * L), AF.Abs)
                        act(a("sg", k * L, (k + n) * L), a(d, 0, n * L), AF.Sign, bias=0.5)
                else:
                    dd = "zs" if md == "A" else "yb"
                    for k in range(k0, k1):
                        tt(a(dd, k * L, (k + 1) * L), ind(a("xw"), a("o1", 16 * k, 16 * k + 16)), z, ALU.subtract)
                    d = a(dd, k0 * L, k1 * L)
                    if md == "A":
                        ts(y, d, 0.0, ALU.max, 2.0, ALU.mult)
                    else:
                        act(zk, d, AF.Abs)
            k0, k1 = pieces[0][1], pieces[-1][2]
            c0, c1 = 16 * k0, 16 * k1
            kb = "k%d" % (c % 2)
            for k in range(k0, k1):
                kept[k] = md == "A"
            u, r, xx = a(kb, c0, c1), a("r1", c0, c1), a("xx", c0, c1)
            it = [(u, a("idn"), a("uo", 0, c1 - c0))]
            if md == "A":
                mm(it + red(u, "zhn", "zs", k0 * L, k1 * L))
                mm(red(u, "zhi", "yb", k0 * L, k1 * L), start=False)
            else:
                mm(it + red(u, "zhi", "zs", k0 * L, k1 * L))
            if CFG["uv"][c] == "V":
                ts(r, u, MAG * 2048, ALU.add, -MAG * 2048, ALU.add)
            else:
                act(r, u, bias=MAG * 2048)
                act(r, r, bias=-MAG * 2048)
            tt(xx, u, r, ALU.subtract)
            act(a("qq", c0, c1), xx, AF.Square, bias=592 + UO)
            if s:
                tt(a("h1", c0, c1), a("qb", c0, c1), a("qq", c0, c1), ALU.add)
            else:
                ts(a("h1", c0, c1), a("qq", c0, c1), 19616.0 - 592 ** 2, ALU.add)
            ts(a("h2", c0, c1), a("h1", c0, c1), 5, SHR, 2047, AND); cp(a("o2", c0, c1), a("h2", c0, c1))

        def third(c):
            k0, k1 = h1[c][0][1], h1[c][-1][2]
            at(s, CFG["tr"][c])
            for md, j0, j1 in h1[c]:
                if md in "AB":
                    ts(a("sg", j0 * L, j1 * L), a("zs" if md == "A" else "yb", j0 * L, j1 * L), 0.0, ALU.is_ge, -0.5, ALU.add)
                elif md == "T":
                    act(a("sg", j0 * L, j1 * L), a("yb", j0 * L, j1 * L), AF.Sign, bias=0.5)
            rows = a(CFG["rb"][c], L + 16 * k0, L + 16 * k1)
            mm(red(rows, "zon", "sg", k0 * L, k1 * L))
            act(a("c3", 16 * k0, 16 * k1), rows, AF.Relu, scale=-2.0 ** 38)

        def second(c):
            pieces, more = h2[c], []
            for md, k0, k1 in pieces:
                e = a("eb", k0 * L, k1 * L)
                at(s, CFG["tv"][turn[1]]); turn[1] += 1
                v = ind(a("vw", 0, W), a("o2", 16 * k0, 16 * k1))
                if md == "S":
                    act(e, v)
                    for k in range(k0, k1, 2):
                        d = "d%d" % (blk[0] % 2); blk[0] += 1
                        x0, x1 = k * L, min(k + 2, k1) * L
                        o = a(d, 0, x1 - x0)
                        if kept[k]:
                            mm([(o, a("idn"), a("zs", x0, x1)), (o, a("nid"), a("yb", x0, x1)), (o, a("idn"), a("eb", x0, x1))])
                        else:
                            mm([(o, a("nid"), a("zs", x0, x1)), (o, a("idn"), a("eb", x0, x1))])
                        act(a("eb", x0, x1), o, AF.Abs)
                elif md == "V":
                    tt(e, v, a("zs", k0 * L, k1 * L), ALU.subtract)
                    act(e, e, AF.Abs)
                else:
                    tt(a("rb", k0 * L, k1 * L), v, a("zs", k0 * L, k1 * L), ALU.subtract)
                    ts(e, a("rb", k0 * L, k1 * L), 0.0, ALU.max, 2.0, ALU.mult)
                    more += red(a(CFG["fk"][c], 16 * k0, 16 * k1), "zpo", "rb", k0 * L, k1 * L)
            k0, k1 = pieces[0][1], pieces[-1][2]
            c0, c1, w = 16 * k0, 16 * k1, 16 * (k1 - k0)
            f = a(CFG["fk"][c], c0, c1)
            bars = [("idf", "xx"), ("n2k", "sk"), ("idn", "c1"), ("idn", "c3")] + ([("idn", "c2"), ("hug", "lv")] if s else [])
            lean = CFG["kv"][c] == "E"
            mm([(f, a("wbb"), a("thm", c0, c1))] + ([(f, a(x), a(y, c0, c1)) for x, y in bars[2:]] if lean else []) + more)
            mm(red(f, "zne", "eb", k0 * L, k1 * L), start=False)
            key = a(CFG["kb"][c], c0, c1)
            if lean:
                tt(a("r1", c0, c1), a("m2", L + c0, L + c1), a("xx", c0, c1), ALU.add)
                key = a("acc", 144, 144 + w) if c + 1 == len(h2) else a("xx", c0, c1)
                tt(key, f, a("r1", c0, c1), ALU.max)
            elif CFG["kv"][c] == "D":
                act(a("c4", c0, c1), f, AF.Relu)
                mm([(key, a(x), a(y, c0, c1)) for x, y in bars])
                mm([(key, a("idn"), a("c4", c0, c1))], start=False)
            else:
                mm([(key, a(x), a(y, c0, c1)) for x, y in bars])
                act(a("r1", c0, c1), key)
                key = a("acc", 144, 144 + w) if c + 1 == len(h2) else a("xx", c0, c1)
                tt(key, f, a("r1", c0, c1), ALU.max)
            end = c + 1 == len(h2)
            if not end:
                tt(a("acc", 0, w), key, a("acc", 0, w) if c else a("stk", 192 * pa + 64, 192 * pa + 64 + w), ALU.min)
            b, n = (128, 16 + w) if end else (0, max(w, least[0]))
            wn = 16 if c + 2 >= len(h2) else 16 * (h2[c + 1][-1][2] - h2[c + 1][0][1])
            while n > wn:
                h = min(n - wn, n // 32 * 16)
                o = a("acc", b, b + h) if n - h > 16 else a("kf") if end else a("acc", 128, 144)
                if end and n % 32 == 16 and n > 32:
                    tt(a("acc", b + 16, b + 16 + h), a("acc", b + 16, b + 16 + h), a("acc", b + n - h, b + n), ALU.min)
                else:
                    if o[0] == "kf" and CFG["ki"] and not last:
                        tt(a("kj"), a("acc", b, b + h), a("acc", b + n - h, b + n), ALU.min)
                        ts(a("u32"), a("kj"), 2047, AND)
                    tt(o, a("acc", b, b + h), a("acc", b + n - h, b + n), ALU.min)
                n -= h
            least[0] = n

        def fourth(c):
            if s == 0:
                return
            at(s, CFG["td"][1])
            for h in range(2):
                it = []
                for m in range(8):
                    o = a(CFG["eb"][h], 40 * m, 40 * m + 40)
                    it += [(o, a("sel", 128 * (8 * h + m), 128 * (8 * h + m + 1)), a("rep", 48, 88)), (o, a("idn"), a("rep", 0, 40))]
                mm(it, each=2)
                at(s, CFG["td"][4 + h])
                tt(a("eq", 320 * h, 320 * h + 320), a(CFG["eb"][h], 0, 320), a("tg", 320 * h, 320 * h + 320), ALU.is_equal)
                at(s, CFG["td"][1])

        done = {"X": 0, "R": 0, "V": 0, "E": 0}
        for x in CFG["ord"][kind]:
            {"X": first, "R": third, "V": second, "E": fourth}[x](done[x])
            done[x] += 1
        if s:
            mm([(a("k0", 0, L, 1, 8), a("zer", 0, 8), a("msk"))])
        else:
            later()
        at(s + 1, 0)
        step[1] = 1000 * (kind + 1) + 500
        un = a("uf", 16 * pb_, 16 * pb_ + 16)
        ts(a("w2"), a("kf"), MAG * 4096, ALU.add, -MAG * 4096, ALU.add)
        tt(un, a("kf"), a("w2"), ALU.subtract)
        count = s >= 1 and not last
        act(sgn, a("kf"), AF.Sign, bias=0.5 - POP, acc=a("cnt") if count else None)
        act(cb, a("kf"), bias=CB - 0.5 + 1.0 / 16, scale=2.0 ** -17)
        if count:
            mm([(a("ff", 300, 301), a("hal"), a("cnt"))])
            act(a("ar"), a("ff", 300, 301), bias=191.5 + 1.0 / 64, scale=1.0 / 32)
            act(a("av"), a("ar"), bias=6144.0, scale=-32.0)
        if not last:
            columns(s + 1)
        at(s + 1, 0)
        o = a("m1", 0, 16)
        mm([(o, a("idn"), a("l16")), (o, a("idf"), a("w2")), (o, a("n64"), cb), (o, a("n64"), cb)])
        ts(a("a3"), o, 1.0 / 16, ALU.mult, CB * 8192.0, ALU.add)
        if CFG["zv"] == "S":
            act(zsl(SL0 + s + 1), ind(a("zs", 0, (SL0 + s + 1) * L), a("a3")), AF.Abs)
        else:
            cp(zsl(SL0 + s + 1), ind(a("zs", 0, (SL0 + s + 1) * L), a("a3")))
        if s >= 1:
            at(s + 1, CFG["td"][0])
            tt(a("rpa"), ind(a("kf"), a("rpl", 8, 16)), a("g8r"), ALU.is_ge)
            mm([(a("k0", 4 * b + PAIRS[p][1], L, 16, 8), a("rpa", 8 * (4 * b + PAIRS[p][0]), 8 * (4 * b + PAIRS[p][0] + 1)), a("eq", 10 * b + p, 640, 40))
                for b in range(4) for p in range(10)], start=False)
            act(a("los", p=8), a("k0", 0, L, 1, 8), scale=4096.0)
            o = a("k1", 0, 16)
            mm([(o, a("idn"), a("rep", 96, 112)), (o, a("n2k"), sgn), (o, a("n2k"), sgn)])
            mm([(o, a("z8", 15 - m, 143 - m, 1, 8), a("los", 16 * m, 16 * m + 16, 1, 8)) for m in range(16)], start=False)
            tt(a("w1"), o, a("dum"), ALU.min)
            so = a("so", 16 * (s - 1), 16 * s)
            ts(so, a("w1"), 4096.0, ALU.add)
            send(a("lo", 16 * (s - 1), 16 * s), so, "ao%d" % s, NEO, CFG["xl"])
            for n, zz, z0 in (("so", "zs", (SL0 + s) * L), ("lo", "lz", (s - 1) * L)):
                at(s + 1, CFG["td"][2 if n == "so" else 3])
                for b in range(3, -1, -1):
                    cp(ind(a("vw"), a(n, 16 * (s - 1) + 4 * b, 16 * (s - 1) + 4 * b + 4)), a(zz, z0 + 64 * b, z0 + 64 * b + 64))
        at(s + 1, CFG["tb"][0])
        act(dlt, cb, AF.Sign, bias=CB + 31.0, scale=-1.0)
        tt(dep, dep, dlt, ALU.add)
        mm([(a("m1", 0, 128, p=80), a("lb"), a("idn"))])
        act(lt, a("m1", 0, 128, p=80))
        at(s + 1, CFG["tb"][1])
        mm([(a("m1", 0, L), lt, a("sM", p=80))])
        tt(a("ee"), a("m1", 0, L), a("c144"), ALU.is_equal)
        mm([(a("m1", 0, L), lt, a("sW", p=80))])
        if s == 0:
            tt(lv, a("m1", 0, L), a("ee"), ALU.mult)
        else:
            tt(a("gg"), a("m1", 0, L), a("ee"), ALU.mult)
            mm([(a("m1", 0, L), a("idn"), lv), (a("m1", 0, L), a("nid"), a("gg"))])
            act(lv, a("m1", 0, L), AF.Abs)
        if not last:
            at(s + 1, CFG["tb"][4])
            mm([(a("m2", 0, L), a("lt", p=16), a("msk", p=16)), (a("m2", 0, L), a("nid"), a("cab"))])
            act(a("c2"), a("m2", 0, L), AF.Relu, bias=-(CB + 31.5) * 2.0 ** 37, scale=2.0 ** 37)
            nl = 16 * min(s + 2, RO - 1 - s)
            b0, b1 = 192 * pa, 192 * pb_
            o = a("m2", 0, nl)
            mm([(o, lt, a("sC", 0, nl, p=80)), (o, a("idf"), a("stk", b0 + 64 - nl, b0 + 64))])
            act(a("sc", 0, nl), o)
            top = a("m2", nl - 16, nl)
            mm([(o, lt, a("sA", 64 - nl, 64, p=80)), (top, a("idn"), a("slc", 16 * s, 16 * s + 16)), (top, a("idf"), a("uf", 16 * pa, 16 * pa + 16))]
               + ([(a("m2", 0, nl - 16), a("idf"), a("stk", b0 + 96 - nl, b0 + 80))] if nl > 16 else []))
            tt(a("stk", b1 + 80 - nl, b1 + 80), o, a("sc", 0, nl), ALU.max)
    step[0] = RO
    dma("Y", "yz", T.yz[:], zsl(SL0 + RO), 2400)
    mm([(a("d0", 0, L), a("swb"), a("lv", 0, L))])
    act(a("lv", L, 2 * L), a("d0", 0, L))
    act(a("ylt"), ind(a("lv"), a("pmb")))
    tr(a("ylo"), a("ylt"))
    dma("Y", "yl", T.yl[:], a("ylo"), 2400)
    tt(a("xp"), ind(cb, a("bcc")), a("msk"), ALU.mult)
    mm([(a("d1", 0, L, 1, 8), a("g8"), a("xp"))])
    ts(a("ypo", 0, L, 1, 8), a("d1", 0, L, 1, 8), -32.0 - CB, ALU.add, -1.0, ALU.max)
    dma("Y", "yp", T.yp[:], a("ypo", 0, L, 1, 8), 2400)
    dma("Y", "yv", T.yv[:, 0:W // 2], a("vw", 0, W // 2), 3500)
    dma("S", "yv2", T.yv[:, W // 2:W], a("vw", W // 2, W), 3500)
    return ops, sent[0]


def plan(ops):
    n = len(ops)
    dep = [dict() for _ in range(n)]
    hist, turn = {}, {}
    for j, o in enumerate(ops):
        if o["after"] is not None:
            dep[j][o["after"]] = False
        soft = CFG["soft"] and o["e"] in "VS" and o["sem"] is None
        for x, wr in [(x, False) for x in o["r"]] + [(x, True) for x in o["w"]]:
            h = hist.setdefault(x[0], [])
            ps = x[0] in PS
            for (i, c0, c1, w) in h:
                if i == j:
                    continue
                hit = c0 < x[2] and x[1] < c1 and (w or wr)
                same = ops[i]["e"] == o["e"]
                if ps and not same:
                    dep[j][i] = True
                elif ps and o["e"] == "P":
                    dep[j].setdefault(i, False)
                elif hit and wr and same and soft and ops[i]["sem"] is None:
                    dep[j].setdefault(i, False)
                elif hit:
                    dep[j][i] = True
            if ps:
                if h and ops[h[-1][0]]["e"] != o["e"]:
                    h[:] = [e for e in h if ops[e[0]]["e"] == ops[h[-1][0]]["e"] and e[0] > turn.get(x[0], -1)]
                    turn[x[0]] = j - 1
            elif wr and x[3] == 1 and x[4] == 128:
                h[:] = [e for e in h if not (x[1] <= e[1] and e[2] <= x[2])]
            h.append((j, x[1], x[2], wr))
    pri = [0.0] * n
    succ = [[] for _ in range(n)]
    for j in range(n):
        for i in dep[j]:
            succ[i].append(j)
    LAT = CFG["lat"]
    cost = [max(o["c"] + (CFG["pm"] * len(o["w"]) + CFG["px"] * o["c"] if o["e"] == "P" else CFG["ov"] if o["e"] in "VS" and not o["g"] else 0.0), 1.0) for o in ops]
    raw = cost
    cost = [raw[j] * (CFG["gm"] if ops[j]["g"] else CFG["f"] if ops[j]["e"] in "VSPG" else 1.0) for j in range(n)]
    back = [[(i, ops[i]["lat"] + LAT if dep[j][i] else 0.0) for i in dep[j]] for j in range(n)]
    fwd = [[(k, ops[j]["lat"] + LAT if dep[k][j] else 0.0) for k in succ[j]] for j in range(n)]
    x = CFG["seed"] * 7919 + 1
    for j in range(n - 1, -1, -1):
        x = (x * 1103515245 + 12345) % 2147483648
        pri[j] = cost[j] * (1.0 + CFG["amp"] * x / 2147483648.0) + max([pri[k] + d for k, d in fwd[j]] + [ops[j]["lat"]])

    def place(turns, pre, head):
        st, line = [0.0] * n, {}
        for j in turns:
            t = head[j]
            for i, d in pre[j]:
                if st[i] + cost[i] + d > t:
                    t = st[i] + cost[i] + d
            s0, s1 = line.setdefault(ops[j]["e"], ([], []))
            lo, hi = 0, len(s1)
            while lo < hi:
                mid = (lo + hi) // 2
                if s1[mid] <= t:
                    lo = mid + 1
                else:
                    hi = mid
            while lo < len(s0) and s0[lo] < t + cost[j]:
                t = max(t, s1[lo]); lo += 1
            s0.insert(lo, t); s1.insert(lo, t + cost[j]); st[j] = t
        return st

    zero, tail = [0.0] * n, [o["lat"] for o in ops]
    st = place(sorted(range(n), key=lambda j: -pri[j]), back, zero)
    best = None
    for _ in range(CFG["it"]):
        end = max(st[j] + cost[j] + tail[j] for j in range(n))
        if best is None or end < best[0]:
            best = (end, st)
        rv = place(sorted(range(n), key=lambda j: -(st[j] + cost[j])), fwd, tail)
        st = place(sorted(range(n), key=lambda j: -(rv[j] + cost[j])), back, zero)
    end, st = best
    key = [0.0] * n
    for j in range(n):
        key[j] = max([ops[j]["h"]] + [key[i] + cost[i] + d for i, d in back[j]])
    st = place(sorted(range(n), key=lambda j: key[j]), back, zero)
    pre = [list(d) for d in dep]

    def held(st, m, goal):
        before, lastof, r = {}, {}, []
        for j in sorted(range(m), key=lambda j: st[j]):
            before[j] = lastof.get(ops[j]["e"]); lastof[ops[j]["e"]] = j
        j = max(goal, key=lambda j: st[j] + cost[j] + tail[j])
        while j is not None:
            t, i = max([(st[i] + cost[i] + d, i) for i, d in back[j]] + [(0.0, None)], key=lambda q: q[0])
            if t < st[j] - 0.5:
                i = before[j]
                r.append((i, j))
            j = i
        return r

    views = []
    for w, f, gm, lat, xl in CFG["views"]:
        c2 = [raw[j] * (gm if ops[j]["g"] else f if ops[j]["e"] in "VSPG" else 1.0) for j in range(n)]
        views.append((w, c2, [[(i, c2[i] + (ops[i]["lat"] * (xl if ops[i]["e"] == "X" else 1.0) + lat if dep[j][i] else 0.0)) for i in dep[j]] for j in range(n)]))
    eng = [o["e"] for o in ops]

    def others(st, m, goal, each=False):
        turns, r = sorted(range(m), key=lambda j: st[j]), []
        for w, c2, b2 in views:
            if not (w or each):
                r.append(0.0)
                continue
            t, free = [0.0] * m, {}
            for j in turns:
                u = free.get(eng[j], 0.0)
                for i, d in b2[j]:
                    if t[i] + d > u:
                        u = t[i] + d
                t[j] = u
                free[eng[j]] = u + c2[j]
            r.append(max(t[j] + c2[j] + tail[j] for j in goal))
        return r if each else sum(v[0] * e for v, e in zip(views, r))

    def settle(key, m):
        for j in range(m):
            for i in pre[j]:
                if key[j] <= key[i]:
                    key[j] = key[i] + 0.01
        return place(sorted(range(m), key=lambda j: key[j]), back, zero)

    def search(st, m, goal, lo, hi, tries, x):
        roles = {}
        for j in range(m):
            if lo <= ops[j]["step"] <= hi:
                roles.setdefault(ops[j]["role"], []).append(j)
        names = [r for r in sorted(roles) for _ in range(3 if len(roles[r]) > 1 else 1)]
        st = settle(list(st), m)
        own = max(st[j] + cost[j] + tail[j] for j in goal)
        end = own + others(st, m, goal)
        pairs, top = [q for q in held(st, m, goal) if ops[q[0]]["role"] in roles and ops[q[1]]["role"] in roles], (end, st)
        for it in range(tries):
            x = (x * 1103515245 + 12345) % 2147483648
            by = (-4000.0, -1500.0, -500.0, -150.0, 150.0, 500.0, 1500.0, 4000.0)[(x >> 8) % 8]
            role = names[(x >> 12) % len(names)]
            if pairs and (x >> 5) % 4:
                i, j = pairs[(x >> 12) % len(pairs)]
                more = (0.0, 0.0, 300.0, 1000.0)[(x >> 9) % 4]
                role, by = (ops[j]["role"], st[i] - st[j] - 1 - more) if (x >> 8) % 2 else (ops[i]["role"], st[j] - st[i] + 1 + more)
            key = st[:m]
            for j in roles[role]:
                key[j] += by
                todo = [j] if by < 0 else []
                while todo:
                    k = todo.pop()
                    for i in pre[k]:
                        if key[i] >= key[k]:
                            key[i] = key[k] - 0.01
                            todo.append(i)
            s2 = settle(key, m)
            if it % CFG["fb"] == 0 and lo < 1 < hi:
                rv = place(sorted(range(m), key=lambda j: -(s2[j] + cost[j])), [[q for q in f if q[0] < m] for f in fwd], tail)
                s2 = place(sorted(range(m), key=lambda j: -(rv[j] + cost[j])), back, zero)
            e1 = max(s2[j] + cost[j] + tail[j] for j in goal)
            if e1 > own + 2 * CFG["heat"]:
                continue
            e2 = e1 + others(s2, m, goal)
            if e2 <= end + CFG["heat"] * (1.0 - it / tries) * ((x >> 3) % 64) / 64:
                end, st, own = e2, s2, e1
                pairs = [q for q in held(st, m, goal) if ops[q[0]]["role"] in roles and ops[q[1]]["role"] in roles]
                if end < top[0]:
                    top = (end, st)
        return top[1]

    of = {}
    for j in range(n):
        of.setdefault(ops[j]["step"], []).append(j)
    move = {s: [j for j in of[s] if ops[j]["w"] and ops[j]["w"][0][0] == "kf"] for s in range(RO)}
    t0, t1, t2, t3 = CFG["tries"]
    m = of[3][-1] + 1
    s1 = min((search(st, m, move[3], -1, 3, t1, x + k) for k in range(t0)), key=lambda q: q[move[3][0]] + others(q, m, move[3]), default=st)
    st, per = s1[:m] + st[m:], s1[move[3][0]] - s1[move[2][0]]
    for s in range(4, RO) if t0 else []:
        k = 0
        for j in of[s]:
            while (eng[of[2][k]], ops[of[2][k]]["w"][:1] and ops[of[2][k]]["w"][0][0]) != (eng[j], ops[j]["w"][:1] and ops[j]["w"][0][0]):
                k += 1
            st[j] = st[of[2][k]] + per * (s - 2)
            k += 1
    for j in of[3] if t0 else []:
        if j > move[3][0]:
            st[j] = st[of[2][of[3].index(j)]] + per
    for j in of[RO] if t0 else []:
        st[j] = per * RO + 40000
    goal = list(range(n - 40, n))
    st = search(st, n, goal, RO - 1, RO, t2, x)
    st = search(st, n, goal, -1, RO, t3, x + 1) if t3 else st
    end = max(st[j] + cost[j] + tail[j] for j in range(n))
    order = sorted((st[j], j) for j in range(n))
    seq = [j for t, j in order]
    pos, cnt = {}, {}
    for j in seq:
        e = ops[j]["e"]
        if ops[j]["sem"] is None:
            cnt[e] = cnt.get(e, 0) + 1
            pos[j] = (e, cnt[e])
        else:
            pos[j] = (j, 1)
    known, clock, waits, need = {}, {}, {}, set()
    for j in seq:
        e = ops[j]["e"]
        if e == "X":
            clock[j] = {j: 1}
            continue
        kn = known.setdefault(e, {})
        ws = []
        for i in sorted((i for i in dep[j] if dep[j][i]), key=lambda i: -pos[i][1]):
            key, p = pos[i]
            if kn.get(key, 0) < p:
                ws.append(i); need.add(i)
                for k2, p2 in clock[i].items():
                    if kn.get(k2, 0) < p2:
                        kn[k2] = p2
        waits[j] = ws
        clock[j] = dict(kn); clock[j][pos[j][0]] = pos[j][1]
    return {"seq": seq, "waits": waits, "need": need, "end": end, "order": order, "dep": dep, "cost": cost, "views": others(st, n, goal, True)}


def rank_program(g, core, T, topo):
    rank = T.rank_of(core)
    if rank is None:
        return
    ops, sent = build(g, core, T, topo, rank)
    if "p" not in CACHE:
        CACHE["p"] = plan(ops)
    p = CACHE["p"]
    q = {"V": g.vector, "S": g.scalar, "P": g.tensor, "G": g, "Y": g.sync}
    val, cnt = {}, {"V": 0, "S": 0, "P": 0, "G": 0}
    for j in p["seq"]:
        o = ops[j]
        if o["sem"] is not None:
            val[j] = o["sem"]
        elif j in p["need"]:
            cnt[o["e"]] += 1
            val[j] = ("e" + o["e"], cnt[o["e"]])
    for j in p["seq"]:
        o = ops[j]
        if o["e"] == "X":
            continue
        for i in p["waits"][j]:
            q[o["e"]].wait_ge(T.sem[val[i][0]], val[i][1])
        r = o["f"]()
        if o["sem"] is not None:
            if o["sem"][0]:
                r.then_inc(T.sem[o["sem"][0]], 16)
        elif j in p["need"]:
            r.then_inc(T.sem["e" + o["e"]], 1)
    for e in cnt:
        if cnt[e]:
            g.wait_ge(T.sem["e" + e], cnt[e])
    g.wait_ge(T.sem.sent, sent)
    for o in ops:
        if o["sem"] is not None and o["sem"][0]:
            g.wait_ge(T.sem[o["sem"][0]], o["sem"][1])
